import numpy as np
import ml_dtypes


def mxq(x, axis, fmt="e4m3"):
    dtype, down = {"e4m3": (ml_dtypes.float8_e4m3fn, 7), "e5m2": (ml_dtypes.float8_e5m2, 14)}[fmt]
    v = np.moveaxis(np.asarray(x, np.float32).astype(ml_dtypes.bfloat16).astype(np.float64), axis, -1)
    blocks = v.reshape(v.shape[:-1] + (-1, 32))
    amax = np.abs(blocks).max(-1, keepdims=True)
    byte = np.maximum(np.where(amax > 0, np.frexp(amax)[1] - 1 + 127, 0) - down, 1)
    scale = np.exp2(byte - 127.0)
    codes = (blocks / scale).astype(np.float32).astype(dtype).astype(np.float64)
    return np.moveaxis((codes * scale).reshape(v.shape), -1, axis)


WIDE = False


def mx_kscale(k):
    if not WIDE:
        return np.ones(k)
    levels = np.array([24, -24, 12, -12, 0])
    if k % 512:
        return np.exp2(np.random.permutation(np.resize(levels, k // 32))).repeat(32)
    a = np.empty((k // 512, 16))
    for p in range(k // 512):
        a[p, :8] = np.random.permutation(np.resize(levels, 8))
        for g in range(8):
            far = levels[np.abs(levels - a[p, g]) >= 10]
            a[p, g + 8] = far[np.random.randint(len(far))]
    return np.exp2(a.ravel()).repeat(32)


def f64(x):
    return np.asarray(x).astype(np.float64)


def striped(idx):
    return np.tile(idx.reshape(-1, 16).T, (8, 1)).astype(np.uint16)


def unstriped(offs):
    return offs[:16].T.reshape(-1).astype(np.int64)


def striped8(idx):
    return np.concatenate([v.reshape(-1, 16).T for v in idx]).astype(np.uint16)


def unstriped8(offs):
    return np.stack([offs[16 * g:16 * g + 16].T.reshape(-1) for g in range(8)]).astype(np.int64)


E2M1 = np.array([0.0, 0.5, 1.0, 1.5, 2.0, 3.0, 4.0, 6.0, -0.0, -0.5, -1.0, -1.5, -2.0, -3.0, -4.0, -6.0])


def pack_weight(w, fmt):
    k, n = w.shape
    w = f64(np.asarray(w, np.float32).astype(ml_dtypes.bfloat16)).reshape(k // 32, 32, n)
    amax = np.abs(w).max(1)
    if fmt == "e4m3":
        byte = np.frexp(amax)[1] - 1 + 127 - 7
    else:
        mant, ex = np.frexp(amax / 6.0)
        byte = np.where(mant > 0.5, ex, ex - 1) + 127
    byte = np.clip(np.where(amax > 0, byte, 1), 1, 254)
    scaled = (w * np.exp2(127.0 - byte)[:, None, :]).reshape(k, n).astype(np.float32)
    by_word = np.ascontiguousarray(scaled.reshape(k // 512, 128, 4, n).transpose(0, 1, 3, 2))
    if fmt == "e4m3":
        words = by_word.astype(ml_dtypes.float8_e4m3fn).view(np.uint8)
    else:
        c = by_word.astype(ml_dtypes.float4_e2m1fn).view(np.uint8) & 0xF
        words = (c[..., 0::2] | (c[..., 1::2] << 4)).reshape(k // 512, 128, 2 * n)
    return np.ascontiguousarray(words), np.ascontiguousarray(byte.astype(np.uint8).reshape(k // 512, 16, n))


def unpack_weight(words, scales, fmt):
    g, _, n = scales.shape
    words = np.ascontiguousarray(words).reshape(g, 128, n, -1)
    if fmt == "e4m3":
        vals = words.view(ml_dtypes.float8_e4m3fn).astype(np.float64)
    else:
        nib = np.empty((g, 128, n, 4), np.uint8)
        nib[..., 0::2] = words & 0xF
        nib[..., 1::2] = words >> 4
        vals = E2M1[nib]
    vals = vals * np.repeat(np.exp2(scales.astype(np.float64) - 127.0), 8, axis=1)[..., None]
    return vals.transpose(0, 1, 3, 2).reshape(g * 512, n)


def planes(y):
    n, m = y.shape
    v = y.astype(np.float32).astype(ml_dtypes.bfloat16).astype(np.float64).reshape(n // 32, 32, m)
    top = np.abs(v).max(1)
    byte = np.clip(np.where(top > 0, np.frexp(top)[1] - 1 + 127 - 7, 1), 1, 254)
    codes = (v * np.exp2(127.0 - byte)[:, None, :]).reshape(n, m).astype(np.float32).astype(ml_dtypes.float8_e4m3fn).view(np.uint8)
    words = codes.reshape(n // 512, 128, 4, m).transpose(0, 1, 3, 2)
    return np.ascontiguousarray(words), np.ascontiguousarray(byte.astype(np.uint8).reshape(n // 512, 16, m))


def silu(f):
    return f / (1.0 + np.exp(-np.maximum(f, -700.0)))


K, L, R, N, T, J = 512, 512, 512, 512, 2048, 1024


def setup_inputs():
    n = np.random.standard_normal
    s = mx_kscale(K)[:, None]
    s2 = mx_kscale(L)[:, None]
    u = mx_kscale(R)[:, None]
    p_tab = pack_weight(n((L, T)) * s2, "e4m3")
    p_wd = pack_weight(n((R, N)) / np.sqrt(R) / u, "e2m1")
    return {
        "tab_words": p_tab[0],
        "tab_scales": p_tab[1],
        "xT": (n((K, T)) * s).astype(np.float32),
        "wgt2": np.repeat(np.random.uniform(0.5, 2.0, (8, J)), 16, axis=0).astype(np.float32),
        "wa": (n((K, R)) / np.sqrt(K) / s).astype(np.float32),
        "wb": (n((L, R)) / np.sqrt(L) / s2 * u.T).astype(np.float32),
        "wd_words": p_wd[0],
        "wd_scales": p_wd[1],
        "res": (n((N, J))).astype(np.float32),
        "offs": striped(np.random.permutation(T)[:J]),
        "offs2": striped8(np.stack([np.random.permutation(T)[:J] for _ in range(8)])),
    }


def reference(tab_words, tab_scales, xT, wgt2, wa, wb, wd_words, wd_scales, res, offs, offs2):
    idx = unstriped(offs)
    idx2 = unstriped8(offs2)
    tab_ = unpack_weight(tab_words, tab_scales, "e4m3")[:, idx]
    rows = np.arange(K)
    xg = f64(wgt2)[rows // 4 % 128] * f64(xT)[rows[:, None], idx2[rows % 512 // 64]]
    xT_ = mxq(xg, 0, "e4m3")
    wa_ = mxq(f64(wa), 0, "e4m3")
    wb_ = mxq(f64(wb), 0, "e4m3")
    ya = wa_.T @ xT_
    yb = wb_.T @ tab_
    h = silu(ya) * yb
    h_ = mxq(h, 0, "e4m3")
    wd_ = unpack_weight(wd_words, wd_scales, "e2m1")
    y = wd_.T @ h_
    out_0 = f64(res) + y
    return (out_0,) + planes(out_0)

@@ -1,0 +1,221 @@
+from contextlib import ExitStack
+
+import concourse.mybir as mybir
+
+K, L, R, N, T, J = 512, 512, 512, 512, 2048, 1024
+FLOPS = 2 * J * (K * R + L * R + R * N)
+
+F32 = mybir.dt.float32
+BF16 = mybir.dt.bfloat16
+I32 = mybir.dt.int32
+U32 = mybir.dt.uint32
+U16 = mybir.dt.uint16
+U8 = mybir.dt.uint8
+FP8X4 = mybir.dt.float8_e4m3fn_x4
+FP4X4 = mybir.dt.float4_e2m1fn_x4
+MULT = mybir.AluOpType.mult
+ADD = mybir.AluOpType.add
+SILU = mybir.ActivationFunctionType.Silu
+
+P = 128
+PACK = 4
+HALF = 512
+CHUNKS = [256, 256, 256, 128, 128]
+BLOCK = 128
+
+
+def tile_list_htabg_glu_resP_kernel(
+    tc, tab_words, tab_scales, xT, wgt2, wa, wb, wd_words, wd_scales, res, offs, offs2, out_0, out_1, out_2
+):
+    nc = tc.nc
+    with ExitStack() as ctx:
+        sb = ctx.enter_context(tc.tile_pool(name="sb", bufs=1))
+        ps = ctx.enter_context(tc.psum_pool(name="ps", bufs=1))
+
+        def tile(name, shape, dtype):
+            return sb.tile(shape, dtype, name=name, align_bytes=64)
+
+        tab_list = tile("tab_list", [P, J // 16], U16)
+        head_lists = tile("head_lists", [P, J // 16], U16)
+        tab_plane = tile("tab_plane", [P, T], U8)
+        wd_plane = tile("wd_plane", [P, N], U8)
+        wd_raw = tile("wd_raw", [P, 2 * N], U8)
+        x_plane = [tile("x_plane%d" % i, [P, T], F32) for i in range(PACK)]
+        wgt = tile("wgt", [P, J], F32)
+        tab_codes = tile("tab_codes", [P, T], U32)
+        wa_raw = [tile("wa_raw%d" % s, [P, PACK, R // 2], F32) for s in range(2)]
+        wb_raw = [tile("wb_raw%d" % s, [P, PACK, R // 2], F32) for s in range(2)]
+        res_half = [tile("res%d" % h, [P, PACK, HALF], F32) for h in range(J // HALF)]
+
+        nc.vector.memset(tab_plane[:].bitcast(I32), 0)
+        nc.vector.memset(wd_plane[:].bitcast(I32), 0)
+
+        x_rows = xT.rearrange("(p i) t -> p i t", i=PACK)
+        res_rows = res.rearrange("(p t) j -> p t j", t=PACK)
+
+        def load_weight(raw, w):
+            rows = w.rearrange("(p i) r -> p i r", i=PACK)
+            for s in range(2):
+                nc.sync.dma_start(raw[s][:], rows[:, :, s * (R // 2) : (s + 1) * (R // 2)])
+
+        nc.sync.dma_start(tab_list[:], offs)
+        for q in range(4):
+            nc.sync.dma_start(tab_plane[32 * q : 32 * q + 4, :].bitcast(I32), tab_scales[0, 4 * q : 4 * q + 4, :].bitcast(I32))
+        nc.sync.dma_start(wd_raw[:].bitcast(I32), wd_words[0].bitcast(I32))
+        nc.sync.dma_start(x_plane[0][:], x_rows[:, 0, :])
+        nc.sync.dma_start(head_lists[:], offs2)
+        nc.sync.dma_start(wgt[:], wgt2)
+        for q in range(4):
+            nc.sync.dma_start(wd_plane[32 * q : 32 * q + 4, :].bitcast(I32), wd_scales[0, 4 * q : 4 * q + 4, :].bitcast(I32))
+        nc.sync.dma_start(x_plane[1][:], x_rows[:, 1, :])
+        nc.sync.dma_start(x_plane[2][:], x_rows[:, 2, :])
+        load_weight(wa_raw, wa)
+        nc.sync.dma_start(x_plane[3][:], x_rows[:, 3, :])
+        load_weight(wb_raw, wb)
+        nc.sync.dma_start(tab_codes[:].bitcast(I32), tab_words[0].rearrange("p t i -> p (t i)").bitcast(I32))
+        for h in range(J // HALF):
+            nc.sync.dma_start(res_half[h][:], res_rows[:, :, h * HALF : (h + 1) * HALF])
+
+        v_scales = tile("v_scales", [P, J], U8)
+        nc.vector.tensor_copy(v_scales[:], tab_plane[:].indirect(tab_list[:]))
+
+        wd_codes = tile("wd_codes", [P, 2 * N], U8)
+        wd_sc = tile("wd_sc", [P, N], U8)
+        nc.vector.tensor_copy(
+            wd_codes[:].rearrange("p (t m b) -> p t m b", t=PACK, b=2),
+            wd_raw[:].rearrange("p (m t b) -> p t m b", t=PACK, b=2),
+        )
+        nc.vector.tensor_copy(
+            wd_sc[:].rearrange("p (t m) -> p t m", t=PACK),
+            wd_plane[:].rearrange("p (m t) -> p t m", t=PACK),
+        )
+
+        picked = [tile("picked%d" % h, [P, PACK, HALF], F32) for h in range(J // HALF)]
+        v_codes = [tile("v_codes%d" % h, [P, HALF], U32) for h in range(J // HALF)]
+        out_rows = out_0.rearrange("(p t) j -> p t j", t=PACK)
+        out_words = out_1[0].rearrange("p j i -> p (j i)").bitcast(I32)
+        out_plane = tile("out_plane", [P, J], U8)
+        starts = [sum(CHUNKS[:c]) for c in range(len(CHUNKS))]
+        gates = {}
+        h_ops = {}
+
+        def gather_x(i, j0, width):
+            h, c0 = divmod(j0, HALF)
+            nc.vector.tensor_tensor(
+                picked[h][:, i, c0 : c0 + width],
+                x_plane[i][:].indirect(head_lists[:, j0 // 16 : (j0 + width) // 16]),
+                wgt[:, j0 : j0 + width],
+                MULT,
+            )
+
+        def gather_v(h):
+            nc.vector.tensor_copy(v_codes[h][:], tab_codes[:].indirect(tab_list[:, 32 * h : 32 * (h + 1)]))
+
+        def quantise_weight(name, raw):
+            dealt = tile(name + "_bf", [P, PACK * R], BF16)
+            codes = tile(name + "_codes", [P, R], U32)
+            scales = tile(name + "_scales", [P, R], U8)
+            dst = dealt[:].rearrange("p (u e s m i) -> p s u m i e", u=2, e=2, s=2, i=PACK)
+            for s in range(2):
+                nc.scalar.copy(dst[:, s], raw[s][:].rearrange("p i (m u e) -> p u m i e", u=2, e=2))
+            nc.vector.quantize_mx(codes[:].bitcast(FP8X4), scales[:], dealt[:])
+            return codes, scales
+
+        def interleave(dst, src):
+            nc.scalar.copy(
+                dst.rearrange("p (c e i) -> p c i e", e=4, i=PACK),
+                src.rearrange("p i (c e) -> p c i e", e=4),
+            )
+
+        def front(c):
+            j0, width = starts[c], CHUNKS[c]
+            h, c0 = divmod(j0, HALF)
+            x_bf = tile("x_bf%d" % c, [P, PACK * width], BF16)
+            x_codes = tile("x_codes%d" % c, [P, width], U32)
+            x_scales = tile("x_scales%d" % c, [P, width], U8)
+            interleave(x_bf[:], picked[h][:, :, c0 : c0 + width])
+            nc.vector.quantize_mx(x_codes[:].bitcast(FP8X4), x_scales[:], x_bf[:])
+            for b in range(width // BLOCK):
+                ya = ps.tile([P, PACK, BLOCK], F32, name="ya", bufs=2)
+                xc = slice(b * BLOCK, (b + 1) * BLOCK)
+                for t in range(PACK):
+                    m = slice(t * P, (t + 1) * P)
+                    nc.tensor.matmul_mx(
+                        ya[:, t, :], lhsT=wa_codes[:, m].bitcast(FP8X4), lhsT_scale=wa_scales[:, m],
+                        rhs=x_codes[:, xc].bitcast(FP8X4), rhs_scale=x_scales[:, xc], start=True, stop=True,
+                    )
+                gate = tile("gate%d_%d" % (c, b), [P, BLOCK, PACK], F32)
+                nc.scalar.activation(gate[:], ya[:].rearrange("p t n -> p n t"), SILU)
+                gates[c, b] = gate
+
+        def middle(c):
+            j0, width = starts[c], CHUNKS[c]
+            h, c0 = divmod(j0, HALF)
+            h_bf = tile("h_bf%d" % c, [P, PACK * width], BF16)
+            for b in range(width // BLOCK):
+                yb = ps.tile([P, PACK, BLOCK], F32, name="yb", bufs=3)
+                vc = slice(c0 + b * BLOCK, c0 + (b + 1) * BLOCK)
+                jc = slice(j0 + b * BLOCK, j0 + (b + 1) * BLOCK)
+                for t in range(PACK):
+                    m = slice(t * P, (t + 1) * P)
+                    nc.tensor.matmul_mx(
+                        yb[:, t, :], lhsT=wb_codes[:, m].bitcast(FP8X4), lhsT_scale=wb_scales[:, m],
+                        rhs=v_codes[h][:, vc].bitcast(FP8X4), rhs_scale=v_scales[:, jc], start=True, stop=True,
+                    )
+                nc.vector.tensor_tensor(
+                    h_bf[:, b * PACK * BLOCK : (b + 1) * PACK * BLOCK].rearrange("p (n t) -> p n t", t=PACK),
+                    gates[c, b][:],
+                    yb[:].rearrange("p t n -> p n t"),
+                    MULT,
+                )
+            h_codes = tile("h_codes%d" % c, [P, width], U32)
+            h_scales = tile("h_scales%d" % c, [P, width], U8)
+            nc.vector.quantize_mx(h_codes[:].bitcast(FP8X4), h_scales[:], h_bf[:])
+            h_ops[c] = (h_codes, h_scales)
+
+        def back(c):
+            j0, width = starts[c], CHUNKS[c]
+            h, c0 = divmod(j0, HALF)
+            h_codes, h_scales = h_ops[c]
+            y_out = tile("y_out%d" % c, [P, PACK, width], F32)
+            per_bank = HALF // width
+            for t0 in range(0, PACK, per_bank):
+                y = ps.tile([P, per_bank, width], F32, name="y", bufs=3)
+                for e in range(per_bank):
+                    t = t0 + e
+                    nc.tensor.matmul_mx(
+                        y[:, e, :], lhsT=wd_codes[:, 2 * t * P : 2 * (t + 1) * P].bitcast(FP4X4),
+                        lhsT_scale=wd_sc[:, t * P : (t + 1) * P],
+                        rhs=h_codes[:].bitcast(FP8X4), rhs_scale=h_scales[:], start=True, stop=True,
+                    )
+                nc.vector.tensor_tensor(
+                    y_out[:, t0 : t0 + per_bank, :], y[:], res_half[h][:, t0 : t0 + per_bank, c0 : c0 + width], ADD
+                )
+            jc = slice(j0, j0 + width)
+            nc.sync.dma_start(out_rows[:, :, jc], y_out[:])
+            o_bf = tile("o_bf%d" % c, [P, PACK * width], BF16)
+            o_codes = tile("o_codes%d" % c, [P, width], U32)
+            interleave(o_bf[:], y_out[:])
+            nc.vector.quantize_mx(o_codes[:].bitcast(FP8X4), out_plane[:, jc], o_bf[:])
+            nc.sync.dma_start(out_words[:, jc], o_codes[:].bitcast(I32))
+
+        for i in range(PACK - 1):
+            for h in range(J // HALF):
+                gather_x(i, h * HALF, HALF)
+        wa_codes, wa_scales = quantise_weight("wa", wa_raw)
+        for j0 in range(0, J, 256):
+            gather_x(PACK - 1, j0, 256)
+        front(0)
+        wb_codes, wb_scales = quantise_weight("wb", wb_raw)
+        for h in range(J // HALF):
+            gather_v(h)
+        for step in range(1, len(CHUNKS) + 2):
+            if step < len(CHUNKS):
+                front(step)
+            if step - 1 < len(CHUNKS):
+                middle(step - 1)
+            if step >= 2:
+                back(step - 2)
+        for q in range(4):
+            queue = nc.sync if q < 2 else nc.scalar
+            queue.dma_start(out_2[0, 4 * q : 4 * q + 4, :].bitcast(I32), out_plane[32 * q : 32 * q + 4, :].bitcast(I32))

@@ -1,6 +1,7 @@
 from contextlib import ExitStack
 
 import concourse.mybir as mybir
+from concourse.masks import make_identity
 
 K, L, R, N, T, J = 512, 512, 512, 512, 2048, 1024
 FLOPS = 2 * J * (K * R + L * R + R * N)
@@ -20,7 +21,7 @@ SILU = mybir.ActivationFunctionType.Silu
 P = 128
 PACK = 4
 HALF = 512
-CHUNKS = [256, 256, 256, 128, 128]
+CHUNKS = [256, 256, 256, 256]
 BLOCK = 128
 
 
@@ -41,40 +42,55 @@ def tile_list_htabg_glu_resP_kernel(
         wd_plane = tile("wd_plane", [P, N], U8)
         wd_raw = tile("wd_raw", [P, 2 * N], U8)
         x_plane = [tile("x_plane%d" % i, [P, T], F32) for i in range(PACK)]
-        wgt = tile("wgt", [P, J], F32)
+        wgt = [tile("wgt%d" % h, [P, HALF], F32) for h in range(J // HALF)]
         tab_codes = tile("tab_codes", [P, T], U32)
-        wa_raw = [tile("wa_raw%d" % s, [P, PACK, R // 2], F32) for s in range(2)]
-        wb_raw = [tile("wb_raw%d" % s, [P, PACK, R // 2], F32) for s in range(2)]
+        wa_raw = tile("wa_raw", [P, PACK, R], F32)
+        wb_raw = tile("wb_raw", [P, PACK, R], F32)
         res_half = [tile("res%d" % h, [P, PACK, HALF], F32) for h in range(J // HALF)]
 
-        nc.vector.memset(tab_plane[:].bitcast(I32), 0)
-        nc.vector.memset(wd_plane[:].bitcast(I32), 0)
+        nc.gpsimd.memset(tab_plane[:].bitcast(I32), 0)
+        nc.gpsimd.memset(wd_plane[:].bitcast(I32), 0)
+
+        warm = tile("warm", [P, 2], F32)
+        nc.vector.memset(warm[:, 0:1], 0.0)
+        nc.scalar.activation(warm[:, 1:2], warm[:, 0:1], SILU)
+
+        wgt_rows = tile("wgt_rows", [P, P], F32)
+        ident = tile("ident", [P, P], F32)
+        nc.vector.memset(wgt_rows[64:, :], 0.0)
+        make_identity(nc, ident[:])
 
         x_rows = xT.rearrange("(p i) t -> p i t", i=PACK)
         res_rows = res.rearrange("(p t) j -> p t j", t=PACK)
 
-        def load_weight(raw, w):
-            rows = w.rearrange("(p i) r -> p i r", i=PACK)
-            for s in range(2):
-                nc.sync.dma_start(raw[s][:], rows[:, :, s * (R // 2) : (s + 1) * (R // 2)])
-
         nc.sync.dma_start(tab_list[:], offs)
         for q in range(4):
             nc.sync.dma_start(tab_plane[32 * q : 32 * q + 4, :].bitcast(I32), tab_scales[0, 4 * q : 4 * q + 4, :].bitcast(I32))
-        nc.sync.dma_start(wd_raw[:].bitcast(I32), wd_words[0].bitcast(I32))
-        nc.sync.dma_start(x_plane[0][:], x_rows[:, 0, :])
         nc.sync.dma_start(head_lists[:], offs2)
-        nc.sync.dma_start(wgt[:], wgt2)
+        nc.sync.dma_start(wgt_rows[:64, :], wgt2.rearrange("(g q) (b j) -> q g b j", q=16, j=P)[0])
+        nc.sync.dma_start(x_plane[0][:], x_rows[:, 0, :])
+        nc.sync.dma_start(x_plane[1][:], x_rows[:, 1, :])
+        nc.sync.dma_start(wd_raw[:].bitcast(I32), wd_words[0].bitcast(I32))
         for q in range(4):
             nc.sync.dma_start(wd_plane[32 * q : 32 * q + 4, :].bitcast(I32), wd_scales[0, 4 * q : 4 * q + 4, :].bitcast(I32))
-        nc.sync.dma_start(x_plane[1][:], x_rows[:, 1, :])
         nc.sync.dma_start(x_plane[2][:], x_rows[:, 2, :])
-        load_weight(wa_raw, wa)
+        nc.sync.dma_start(wa_raw[:], wa.rearrange("(p i) r -> p i r", i=PACK))
         nc.sync.dma_start(x_plane[3][:], x_rows[:, 3, :])
-        load_weight(wb_raw, wb)
+        nc.sync.dma_start(wb_raw[:], wb.rearrange("(p i) r -> p i r", i=PACK))
         nc.sync.dma_start(tab_codes[:].bitcast(I32), tab_words[0].rearrange("p t i -> p (t i)").bitcast(I32))
         for h in range(J // HALF):
             nc.sync.dma_start(res_half[h][:], res_rows[:, :, h * HALF : (h + 1) * HALF])
+
+        turned = ps.tile([P, P], F32, name="y", bufs=3)
+        nc.tensor.transpose(turned[:], wgt_rows[:], ident[:])
+        by_block = turned[:, :64].rearrange("p (g b) -> p b g", b=8)
+        for h in range(J // HALF):
+            spread = tile("spread%d" % h, [P, PACK, 8, 16], F32)
+            nc.scalar.copy(spread[:], by_block[:, PACK * h : PACK * (h + 1), :].unsqueeze(3).to_broadcast([P, PACK, 8, 16]))
+            back_turned = ps.tile([P, PACK, P], F32, name="yb", bufs=3)
+            for b in range(PACK):
+                nc.tensor.transpose(back_turned[:, b, :], spread[:, b].rearrange("p g q -> p (g q)"), ident[:])
+            nc.scalar.copy(wgt[h][:], back_turned[:].rearrange("p b j -> p (b j)"))
 
         v_scales = tile("v_scales", [P, J], U8)
         nc.vector.tensor_copy(v_scales[:], tab_plane[:].indirect(tab_list[:]))
@@ -97,6 +113,7 @@ def tile_list_htabg_glu_resP_kernel(
         out_plane = tile("out_plane", [P, J], U8)
         starts = [sum(CHUNKS[:c]) for c in range(len(CHUNKS))]
         gates = {}
+        x_ops = {}
         h_ops = {}
 
         def gather_x(i, j0, width):
@@ -104,25 +121,26 @@ def tile_list_htabg_glu_resP_kernel(
             nc.vector.tensor_tensor(
                 picked[h][:, i, c0 : c0 + width],
                 x_plane[i][:].indirect(head_lists[:, j0 // 16 : (j0 + width) // 16]),
-                wgt[:, j0 : j0 + width],
+                wgt[h][:, c0 : c0 + width],
                 MULT,
             )
 
         def gather_v(h):
             nc.vector.tensor_copy(v_codes[h][:], tab_codes[:].indirect(tab_list[:, 32 * h : 32 * (h + 1)]))
 
-        def quantise_weight(name, raw):
+        def quantise_weight(name, raw, copies):
             dealt = tile(name + "_bf", [P, PACK * R], BF16)
             codes = tile(name + "_codes", [P, R], U32)
             scales = tile(name + "_scales", [P, R], U8)
-            dst = dealt[:].rearrange("p (u e s m i) -> p s u m i e", u=2, e=2, s=2, i=PACK)
-            for s in range(2):
-                nc.scalar.copy(dst[:, s], raw[s][:].rearrange("p i (m u e) -> p u m i e", u=2, e=2))
+            src = raw[:].rearrange("p i (m u e) -> p u m i e", u=2, e=2)
+            dst = dealt[:].rearrange("p (u e m i) -> p u m i e", u=2, e=2, i=PACK)
+            for u in range(2):
+                copies[u](dst[:, u], src[:, u])
             nc.vector.quantize_mx(codes[:].bitcast(FP8X4), scales[:], dealt[:])
             return codes, scales
 
-        def interleave(dst, src):
-            nc.scalar.copy(
+        def interleave(copy, dst, src):
+            copy(
                 dst.rearrange("p (c e i) -> p c i e", e=4, i=PACK),
                 src.rearrange("p i (c e) -> p c i e", e=4),
             )
@@ -133,8 +151,13 @@ def tile_list_htabg_glu_resP_kernel(
             x_bf = tile("x_bf%d" % c, [P, PACK * width], BF16)
             x_codes = tile("x_codes%d" % c, [P, width], U32)
             x_scales = tile("x_scales%d" % c, [P, width], U8)
-            interleave(x_bf[:], picked[h][:, :, c0 : c0 + width])
+            interleave(nc.scalar.copy, x_bf[:], picked[h][:, :, c0 : c0 + width])
             nc.vector.quantize_mx(x_codes[:].bitcast(FP8X4), x_scales[:], x_bf[:])
+            x_ops[c] = (x_codes, x_scales)
+
+        def gate_of(c):
+            width = CHUNKS[c]
+            x_codes, x_scales = x_ops[c]
             for b in range(width // BLOCK):
                 ya = ps.tile([P, PACK, BLOCK], F32, name="ya", bufs=2)
                 xc = slice(b * BLOCK, (b + 1) * BLOCK)
@@ -195,23 +218,25 @@ def tile_list_htabg_glu_resP_kernel(
             nc.sync.dma_start(out_rows[:, :, jc], y_out[:])
             o_bf = tile("o_bf%d" % c, [P, PACK * width], BF16)
             o_codes = tile("o_codes%d" % c, [P, width], U32)
-            interleave(o_bf[:], y_out[:])
+            interleave(nc.vector.tensor_copy if c >= len(CHUNKS) - 1 else nc.scalar.copy, o_bf[:], y_out[:])
             nc.vector.quantize_mx(o_codes[:].bitcast(FP8X4), out_plane[:, jc], o_bf[:])
             nc.sync.dma_start(out_words[:, jc], o_codes[:].bitcast(I32))
 
         for i in range(PACK - 1):
             for h in range(J // HALF):
                 gather_x(i, h * HALF, HALF)
-        wa_codes, wa_scales = quantise_weight("wa", wa_raw)
+        wa_codes, wa_scales = quantise_weight("wa", wa_raw, [nc.scalar.copy, nc.scalar.copy])
         for j0 in range(0, J, 256):
             gather_x(PACK - 1, j0, 256)
         front(0)
-        wb_codes, wb_scales = quantise_weight("wb", wb_raw)
+        gate_of(0)
+        wb_codes, wb_scales = quantise_weight("wb", wb_raw, [nc.scalar.copy, nc.vector.tensor_copy])
         for h in range(J // HALF):
             gather_v(h)
         for step in range(1, len(CHUNKS) + 2):
             if step < len(CHUNKS):
                 front(step)
+                gate_of(step)
             if step - 1 < len(CHUNKS):
                 middle(step - 1)
             if step >= 2:

@@ -33,8 +33,8 @@ def tile_list_htabg_glu_resP_kernel(
         sb = ctx.enter_context(tc.tile_pool(name="sb", bufs=1))
         ps = ctx.enter_context(tc.psum_pool(name="ps", bufs=1))
 
-        def tile(name, shape, dtype):
-            return sb.tile(shape, dtype, name=name, align_bytes=64)
+        def tile(name, shape, dtype, tag=""):
+            return sb.tile(shape, dtype, name=name, tag=tag or name, align_bytes=64)
 
         tab_list = tile("tab_list", [P, J // 16], U16)
         head_lists = tile("head_lists", [P, J // 16], U16)
@@ -42,7 +42,7 @@ def tile_list_htabg_glu_resP_kernel(
         wd_plane = tile("wd_plane", [P, N], U8)
         wd_raw = tile("wd_raw", [P, 2 * N], U8)
         x_plane = [tile("x_plane%d" % i, [P, T], F32) for i in range(PACK)]
-        wgt = [tile("wgt%d" % h, [P, HALF], F32) for h in range(J // HALF)]
+        wgt = tile("wgt", [P, J], F32)
         tab_codes = tile("tab_codes", [P, T], U32)
         wa_raw = tile("wa_raw", [P, PACK, R], F32)
         wb_raw = tile("wb_raw", [P, PACK, R], F32)
@@ -51,26 +51,25 @@ def tile_list_htabg_glu_resP_kernel(
         nc.gpsimd.memset(tab_plane[:].bitcast(I32), 0)
         nc.gpsimd.memset(wd_plane[:].bitcast(I32), 0)
 
-        warm = tile("warm", [P, 2], F32)
-        nc.vector.memset(warm[:, 0:1], 0.0)
-        nc.scalar.activation(warm[:, 1:2], warm[:, 0:1], SILU)
 
         wgt_rows = tile("wgt_rows", [P, P], F32)
         ident = tile("ident", [P, P], F32)
         nc.vector.memset(wgt_rows[64:, :], 0.0)
         make_identity(nc, ident[:])
+        warm = tile("warm", [P, 1], F32)
+        nc.scalar.activation(warm[:], ident[:, 0:1], SILU)
 
         x_rows = xT.rearrange("(p i) t -> p i t", i=PACK)
         res_rows = res.rearrange("(p t) j -> p t j", t=PACK)
 
+        nc.scalar.dma_start(wgt_rows[:64, :], wgt2.rearrange("(g q) (b j) -> q g b j", q=16, j=P)[0])
         nc.sync.dma_start(tab_list[:], offs)
+        nc.sync.dma_start(wd_raw[:].bitcast(I32), wd_words[0].bitcast(I32))
         for q in range(4):
             nc.sync.dma_start(tab_plane[32 * q : 32 * q + 4, :].bitcast(I32), tab_scales[0, 4 * q : 4 * q + 4, :].bitcast(I32))
-        nc.sync.dma_start(head_lists[:], offs2)
-        nc.sync.dma_start(wgt_rows[:64, :], wgt2.rearrange("(g q) (b j) -> q g b j", q=16, j=P)[0])
         nc.sync.dma_start(x_plane[0][:], x_rows[:, 0, :])
+        nc.sync.dma_start(head_lists[:], offs2)
         nc.sync.dma_start(x_plane[1][:], x_rows[:, 1, :])
-        nc.sync.dma_start(wd_raw[:].bitcast(I32), wd_words[0].bitcast(I32))
         for q in range(4):
             nc.sync.dma_start(wd_plane[32 * q : 32 * q + 4, :].bitcast(I32), wd_scales[0, 4 * q : 4 * q + 4, :].bitcast(I32))
         nc.sync.dma_start(x_plane[2][:], x_rows[:, 2, :])
@@ -90,7 +89,7 @@ def tile_list_htabg_glu_resP_kernel(
             back_turned = ps.tile([P, PACK, P], F32, name="yb", bufs=3)
             for b in range(PACK):
                 nc.tensor.transpose(back_turned[:, b, :], spread[:, b].rearrange("p g q -> p (g q)"), ident[:])
-            nc.scalar.copy(wgt[h][:], back_turned[:].rearrange("p b j -> p (b j)"))
+            nc.scalar.copy(wgt[:, h * HALF : (h + 1) * HALF], back_turned[:].rearrange("p b j -> p (b j)"))
 
         v_scales = tile("v_scales", [P, J], U8)
         nc.vector.tensor_copy(v_scales[:], tab_plane[:].indirect(tab_list[:]))
@@ -98,15 +97,15 @@ def tile_list_htabg_glu_resP_kernel(
         wd_codes = tile("wd_codes", [P, 2 * N], U8)
         wd_sc = tile("wd_sc", [P, N], U8)
         nc.vector.tensor_copy(
-            wd_codes[:].rearrange("p (t m b) -> p t m b", t=PACK, b=2),
-            wd_raw[:].rearrange("p (m t b) -> p t m b", t=PACK, b=2),
+            wd_codes[:].bitcast(U16).rearrange("p (t m) -> p t m", t=PACK),
+            wd_raw[:].bitcast(U16).rearrange("p (m t) -> p t m", t=PACK),
         )
         nc.vector.tensor_copy(
             wd_sc[:].rearrange("p (t m) -> p t m", t=PACK),
             wd_plane[:].rearrange("p (m t) -> p t m", t=PACK),
         )
 
-        picked = [tile("picked%d" % h, [P, PACK, HALF], F32) for h in range(J // HALF)]
+        picked = tile("picked", [P, PACK, J], F32)
         v_codes = [tile("v_codes%d" % h, [P, HALF], U32) for h in range(J // HALF)]
         out_rows = out_0.rearrange("(p t) j -> p t j", t=PACK)
         out_words = out_1[0].rearrange("p j i -> p (j i)").bitcast(I32)
@@ -117,11 +116,10 @@ def tile_list_htabg_glu_resP_kernel(
         h_ops = {}
 
         def gather_x(i, j0, width):
-            h, c0 = divmod(j0, HALF)
             nc.vector.tensor_tensor(
-                picked[h][:, i, c0 : c0 + width],
+                picked[:, i, j0 : j0 + width],
                 x_plane[i][:].indirect(head_lists[:, j0 // 16 : (j0 + width) // 16]),
-                wgt[h][:, c0 : c0 + width],
+                wgt[:, j0 : j0 + width],
                 MULT,
             )
 
@@ -151,7 +149,7 @@ def tile_list_htabg_glu_resP_kernel(
             x_bf = tile("x_bf%d" % c, [P, PACK * width], BF16)
             x_codes = tile("x_codes%d" % c, [P, width], U32)
             x_scales = tile("x_scales%d" % c, [P, width], U8)
-            interleave(nc.scalar.copy, x_bf[:], picked[h][:, :, c0 : c0 + width])
+            interleave(nc.scalar.copy, x_bf[:], picked[:, :, j0 : j0 + width])
             nc.vector.quantize_mx(x_codes[:].bitcast(FP8X4), x_scales[:], x_bf[:])
             x_ops[c] = (x_codes, x_scales)
 
@@ -196,11 +194,12 @@ def tile_list_htabg_glu_resP_kernel(
             nc.vector.quantize_mx(h_codes[:].bitcast(FP8X4), h_scales[:], h_bf[:])
             h_ops[c] = (h_codes, h_scales)
 
-        def back(c):
-            j0, width = starts[c], CHUNKS[c]
+        def back(c, j0, width, copy):
             h, c0 = divmod(j0, HALF)
             h_codes, h_scales = h_ops[c]
-            y_out = tile("y_out%d" % c, [P, PACK, width], F32)
+            hc = slice(j0 - starts[c], j0 - starts[c] + width)
+            jc = slice(j0, j0 + width)
+            y_out = tile("y_out%d" % j0, [P, PACK, width], F32)
             per_bank = HALF // width
             for t0 in range(0, PACK, per_bank):
                 y = ps.tile([P, per_bank, width], F32, name="y", bufs=3)
@@ -209,28 +208,31 @@ def tile_list_htabg_glu_resP_kernel(
                     nc.tensor.matmul_mx(
                         y[:, e, :], lhsT=wd_codes[:, 2 * t * P : 2 * (t + 1) * P].bitcast(FP4X4),
                         lhsT_scale=wd_sc[:, t * P : (t + 1) * P],
-                        rhs=h_codes[:].bitcast(FP8X4), rhs_scale=h_scales[:], start=True, stop=True,
+                        rhs=h_codes[:, hc].bitcast(FP8X4), rhs_scale=h_scales[:, hc], start=True, stop=True,
                     )
                 nc.vector.tensor_tensor(
                     y_out[:, t0 : t0 + per_bank, :], y[:], res_half[h][:, t0 : t0 + per_bank, c0 : c0 + width], ADD
                 )
-            jc = slice(j0, j0 + width)
             nc.sync.dma_start(out_rows[:, :, jc], y_out[:])
-            o_bf = tile("o_bf%d" % c, [P, PACK * width], BF16)
-            o_codes = tile("o_codes%d" % c, [P, width], U32)
-            interleave(nc.vector.tensor_copy if c >= len(CHUNKS) - 1 else nc.scalar.copy, o_bf[:], y_out[:])
-            nc.vector.quantize_mx(o_codes[:].bitcast(FP8X4), out_plane[:, jc], o_bf[:])
+            interleave(copy, o_bf[c][:, PACK * hc.start : PACK * hc.stop], y_out[:])
+
+        def planes(c):
+            jc = slice(starts[c], starts[c] + CHUNKS[c])
+            o_codes = tile("o_codes%d" % c, [P, CHUNKS[c]], U32)
+            nc.vector.quantize_mx(o_codes[:].bitcast(FP8X4), out_plane[:, jc], o_bf[c][:])
             nc.sync.dma_start(out_words[:, jc], o_codes[:].bitcast(I32))
 
-        for i in range(PACK - 1):
-            for h in range(J // HALF):
-                gather_x(i, h * HALF, HALF)
+        o_bf = [tile("o_bf%d" % c, [P, PACK * CHUNKS[c]], BF16) for c in range(len(CHUNKS))]
+        for h in range(J // HALF):
+            gather_x(0, h * HALF, HALF)
+        for i in range(1, PACK - 1):
+            gather_x(i, 0, J)
         wa_codes, wa_scales = quantise_weight("wa", wa_raw, [nc.scalar.copy, nc.scalar.copy])
-        for j0 in range(0, J, 256):
-            gather_x(PACK - 1, j0, 256)
+        for j0, width in ((0, 256), (256, 256), (512, 512)):
+            gather_x(PACK - 1, j0, width)
         front(0)
-        gate_of(0)
         wb_codes, wb_scales = quantise_weight("wb", wb_raw, [nc.scalar.copy, nc.vector.tensor_copy])
+        gate_of(0)
         for h in range(J // HALF):
             gather_v(h)
         for step in range(1, len(CHUNKS) + 2):
@@ -240,7 +242,13 @@ def tile_list_htabg_glu_resP_kernel(
             if step - 1 < len(CHUNKS):
                 middle(step - 1)
             if step >= 2:
-                back(step - 2)
+                c = step - 2
+                if c < len(CHUNKS) - 1:
+                    back(c, starts[c], CHUNKS[c], nc.scalar.copy)
+                else:
+                    back(c, starts[c], BLOCK, nc.scalar.copy)
+                    back(c, starts[c] + BLOCK, BLOCK, nc.vector.tensor_copy)
+                planes(c)
         for q in range(4):
             queue = nc.sync if q < 2 else nc.scalar
             queue.dma_start(out_2[0, 4 * q : 4 * q + 4, :].bitcast(I32), out_plane[32 * q : 32 * q + 4, :].bitcast(I32))

@@ -4,6 +4,7 @@ import concourse.mybir as mybir
 from concourse.masks import make_identity
 
 K, L, R, N, T, J = 512, 512, 512, 512, 2048, 1024
+HEADS = 8
 FLOPS = 2 * J * (K * R + L * R + R * N)
 
 F32 = mybir.dt.float32
@@ -20,9 +21,14 @@ SILU = mybir.ActivationFunctionType.Silu
 
 P = 128
 PACK = 4
-HALF = 512
-CHUNKS = [256, 256, 256, 256]
-BLOCK = 128
+QUADRANTS = 4
+LIST_ROWS = 16
+BANK = 512
+BLOCK = BANK // PACK
+CHUNK = 256
+CHUNKS = J // CHUNK
+HALF = J // 2
+YA_BANKS, YB_BANKS, Y_BANKS = 2, 3, 3
 
 
 def tile_list_htabg_glu_resP_kernel(
@@ -33,98 +39,104 @@ def tile_list_htabg_glu_resP_kernel(
         sb = ctx.enter_context(tc.tile_pool(name="sb", bufs=1))
         ps = ctx.enter_context(tc.psum_pool(name="ps", bufs=1))
 
-        def tile(name, shape, dtype, tag=""):
-            return sb.tile(shape, dtype, name=name, tag=tag or name, align_bytes=64)
+        def tile(name, shape, dtype):
+            return sb.tile(shape, dtype, name=name, align_bytes=64)
 
-        tab_list = tile("tab_list", [P, J // 16], U16)
-        head_lists = tile("head_lists", [P, J // 16], U16)
-        tab_plane = tile("tab_plane", [P, T], U8)
-        wd_plane = tile("wd_plane", [P, N], U8)
-        wd_raw = tile("wd_raw", [P, 2 * N], U8)
-        x_plane = [tile("x_plane%d" % i, [P, T], F32) for i in range(PACK)]
+        def scale_rows(scale_tile, q):
+            return scale_tile[32 * q : 32 * q + 4, :].bitcast(I32)
+
+        def hbm_scale_rows(scales, q):
+            return scales[0, 4 * q : 4 * q + 4, :].bitcast(I32)
+
+        tab_list = tile("tab_list", [P, J // LIST_ROWS], U16)
+        head_lists = tile("head_lists", [P, J // LIST_ROWS], U16)
+        tab_scale_tile = tile("tab_scale_tile", [P, T], U8)
+        wd_raw_scales = tile("wd_raw_scales", [P, N], U8)
+        wd_raw_codes = tile("wd_raw_codes", [P, 2 * N], U8)
+        x_rows = [tile("x_rows%d" % i, [P, T], F32) for i in range(PACK)]
         wgt = tile("wgt", [P, J], F32)
         tab_codes = tile("tab_codes", [P, T], U32)
         wa_raw = tile("wa_raw", [P, PACK, R], F32)
         wb_raw = tile("wb_raw", [P, PACK, R], F32)
         res_half = [tile("res%d" % h, [P, PACK, HALF], F32) for h in range(J // HALF)]
 
-        nc.gpsimd.memset(tab_plane[:].bitcast(I32), 0)
-        nc.gpsimd.memset(wd_plane[:].bitcast(I32), 0)
+        nc.gpsimd.memset(tab_scale_tile[:].bitcast(I32), 0)
+        nc.gpsimd.memset(wd_raw_scales[:].bitcast(I32), 0)
 
-
+        blocks = J // P
         wgt_rows = tile("wgt_rows", [P, P], F32)
         ident = tile("ident", [P, P], F32)
-        nc.vector.memset(wgt_rows[64:, :], 0.0)
+        nc.vector.memset(wgt_rows[HEADS * blocks :, :], 0.0)
         make_identity(nc, ident[:])
         warm = tile("warm", [P, 1], F32)
         nc.scalar.activation(warm[:], ident[:, 0:1], SILU)
 
-        x_rows = xT.rearrange("(p i) t -> p i t", i=PACK)
-        res_rows = res.rearrange("(p t) j -> p t j", t=PACK)
-
-        nc.scalar.dma_start(wgt_rows[:64, :], wgt2.rearrange("(g q) (b j) -> q g b j", q=16, j=P)[0])
+        x_hbm = xT.rearrange("(p i) t -> p i t", i=PACK)
+        res_hbm = res.rearrange("(p t) j -> p t j", t=PACK)
+        nc.scalar.dma_start(wgt_rows[: HEADS * blocks, :], wgt2.rearrange("(g q) (b j) -> q g b j", q=LIST_ROWS, j=P)[0])
         nc.sync.dma_start(tab_list[:], offs)
-        nc.sync.dma_start(wd_raw[:].bitcast(I32), wd_words[0].bitcast(I32))
-        for q in range(4):
-            nc.sync.dma_start(tab_plane[32 * q : 32 * q + 4, :].bitcast(I32), tab_scales[0, 4 * q : 4 * q + 4, :].bitcast(I32))
-        nc.sync.dma_start(x_plane[0][:], x_rows[:, 0, :])
+        nc.sync.dma_start(wd_raw_codes[:].bitcast(I32), wd_words[0].bitcast(I32))
+        for q in range(QUADRANTS):
+            nc.sync.dma_start(scale_rows(tab_scale_tile, q), hbm_scale_rows(tab_scales, q))
+        nc.sync.dma_start(x_rows[0][:], x_hbm[:, 0, :])
         nc.sync.dma_start(head_lists[:], offs2)
-        nc.sync.dma_start(x_plane[1][:], x_rows[:, 1, :])
-        for q in range(4):
-            nc.sync.dma_start(wd_plane[32 * q : 32 * q + 4, :].bitcast(I32), wd_scales[0, 4 * q : 4 * q + 4, :].bitcast(I32))
-        nc.sync.dma_start(x_plane[2][:], x_rows[:, 2, :])
+        nc.sync.dma_start(x_rows[1][:], x_hbm[:, 1, :])
+        for q in range(QUADRANTS):
+            nc.sync.dma_start(scale_rows(wd_raw_scales, q), hbm_scale_rows(wd_scales, q))
         nc.sync.dma_start(wa_raw[:], wa.rearrange("(p i) r -> p i r", i=PACK))
-        nc.sync.dma_start(x_plane[3][:], x_rows[:, 3, :])
+        nc.sync.dma_start(x_rows[2][:], x_hbm[:, 2, :])
+        nc.sync.dma_start(x_rows[3][:], x_hbm[:, 3, :])
         nc.sync.dma_start(wb_raw[:], wb.rearrange("(p i) r -> p i r", i=PACK))
         nc.sync.dma_start(tab_codes[:].bitcast(I32), tab_words[0].rearrange("p t i -> p (t i)").bitcast(I32))
         for h in range(J // HALF):
-            nc.sync.dma_start(res_half[h][:], res_rows[:, :, h * HALF : (h + 1) * HALF])
+            nc.sync.dma_start(res_half[h][:], res_hbm[:, :, h * HALF : (h + 1) * HALF])
 
-        turned = ps.tile([P, P], F32, name="y", bufs=3)
-        nc.tensor.transpose(turned[:], wgt_rows[:], ident[:])
-        by_block = turned[:, :64].rearrange("p (g b) -> p b g", b=8)
+        wgt_turned = ps.tile([P, P], F32, name="y", bufs=Y_BANKS)
+        nc.tensor.transpose(wgt_turned[:], wgt_rows[:], ident[:])
+        by_block = wgt_turned[:, : HEADS * blocks].rearrange("p (g b) -> p b g", b=blocks)
         for h in range(J // HALF):
-            spread = tile("spread%d" % h, [P, PACK, 8, 16], F32)
-            nc.scalar.copy(spread[:], by_block[:, PACK * h : PACK * (h + 1), :].unsqueeze(3).to_broadcast([P, PACK, 8, 16]))
-            back_turned = ps.tile([P, PACK, P], F32, name="yb", bufs=3)
-            for b in range(PACK):
-                nc.tensor.transpose(back_turned[:, b, :], spread[:, b].rearrange("p g q -> p (g q)"), ident[:])
-            nc.scalar.copy(wgt[:, h * HALF : (h + 1) * HALF], back_turned[:].rearrange("p b j -> p (b j)"))
+            shape = [P, HALF // P, HEADS, LIST_ROWS]
+            repeated = tile("repeated%d" % h, shape, F32)
+            nc.scalar.copy(repeated[:], by_block[:, shape[1] * h : shape[1] * (h + 1), :].unsqueeze(3).to_broadcast(shape))
+            wgt_bank = ps.tile([P, HALF // P, P], F32, name="yb", bufs=YB_BANKS)
+            for b in range(HALF // P):
+                nc.tensor.transpose(wgt_bank[:, b, :], repeated[:, b].rearrange("p g q -> p (g q)"), ident[:])
+            nc.scalar.copy(wgt[:, h * HALF : (h + 1) * HALF], wgt_bank[:].rearrange("p b j -> p (b j)"))
 
         v_scales = tile("v_scales", [P, J], U8)
-        nc.vector.tensor_copy(v_scales[:], tab_plane[:].indirect(tab_list[:]))
+        nc.vector.tensor_copy(v_scales[:], tab_scale_tile[:].indirect(tab_list[:]))
 
         wd_codes = tile("wd_codes", [P, 2 * N], U8)
-        wd_sc = tile("wd_sc", [P, N], U8)
+        wd_dealt_scales = tile("wd_dealt_scales", [P, N], U8)
         nc.vector.tensor_copy(
             wd_codes[:].bitcast(U16).rearrange("p (t m) -> p t m", t=PACK),
-            wd_raw[:].bitcast(U16).rearrange("p (m t) -> p t m", t=PACK),
+            wd_raw_codes[:].bitcast(U16).rearrange("p (m t) -> p t m", t=PACK),
         )
         nc.vector.tensor_copy(
-            wd_sc[:].rearrange("p (t m) -> p t m", t=PACK),
-            wd_plane[:].rearrange("p (m t) -> p t m", t=PACK),
+            wd_dealt_scales[:].rearrange("p (t m) -> p t m", t=PACK),
+            wd_raw_scales[:].rearrange("p (m t) -> p t m", t=PACK),
         )
 
         picked = tile("picked", [P, PACK, J], F32)
         v_codes = [tile("v_codes%d" % h, [P, HALF], U32) for h in range(J // HALF)]
-        out_rows = out_0.rearrange("(p t) j -> p t j", t=PACK)
-        out_words = out_1[0].rearrange("p j i -> p (j i)").bitcast(I32)
-        out_plane = tile("out_plane", [P, J], U8)
-        starts = [sum(CHUNKS[:c]) for c in range(len(CHUNKS))]
+        out_hbm = out_0.rearrange("(p t) j -> p t j", t=PACK)
+        out_words_hbm = out_1[0].rearrange("p j i -> p (j i)").bitcast(I32)
+        out_scales = tile("out_scales", [P, J], U8)
+        x_quantised = {}
         gates = {}
-        x_ops = {}
-        h_ops = {}
+        h_quantised = {}
 
         def gather_x(i, j0, width):
             nc.vector.tensor_tensor(
                 picked[:, i, j0 : j0 + width],
-                x_plane[i][:].indirect(head_lists[:, j0 // 16 : (j0 + width) // 16]),
+                x_rows[i][:].indirect(head_lists[:, j0 // LIST_ROWS : (j0 + width) // LIST_ROWS]),
                 wgt[:, j0 : j0 + width],
                 MULT,
             )
 
         def gather_v(h):
-            nc.vector.tensor_copy(v_codes[h][:], tab_codes[:].indirect(tab_list[:, 32 * h : 32 * (h + 1)]))
+            entries = slice(h * HALF // LIST_ROWS, (h + 1) * HALF // LIST_ROWS)
+            nc.vector.tensor_copy(v_codes[h][:], tab_codes[:].indirect(tab_list[:, entries]))
 
         def quantise_weight(name, raw, copies):
             dealt = tile(name + "_bf", [P, PACK * R], BF16)
@@ -137,118 +149,131 @@ def tile_list_htabg_glu_resP_kernel(
             nc.vector.quantize_mx(codes[:].bitcast(FP8X4), scales[:], dealt[:])
             return codes, scales
 
-        def interleave(copy, dst, src):
+        def round_into_words(copy, dst, src):
             copy(
                 dst.rearrange("p (c e i) -> p c i e", e=4, i=PACK),
                 src.rearrange("p i (c e) -> p c i e", e=4),
             )
 
-        def front(c):
-            j0, width = starts[c], CHUNKS[c]
-            h, c0 = divmod(j0, HALF)
-            x_bf = tile("x_bf%d" % c, [P, PACK * width], BF16)
-            x_codes = tile("x_codes%d" % c, [P, width], U32)
-            x_scales = tile("x_scales%d" % c, [P, width], U8)
-            interleave(nc.scalar.copy, x_bf[:], picked[:, :, j0 : j0 + width])
+        def quantise_x(c):
+            x_bf = tile("x_bf%d" % c, [P, PACK * CHUNK], BF16)
+            x_codes = tile("x_codes%d" % c, [P, CHUNK], U32)
+            x_scales = tile("x_scales%d" % c, [P, CHUNK], U8)
+            round_into_words(nc.scalar.copy, x_bf[:], picked[:, :, c * CHUNK : (c + 1) * CHUNK])
             nc.vector.quantize_mx(x_codes[:].bitcast(FP8X4), x_scales[:], x_bf[:])
-            x_ops[c] = (x_codes, x_scales)
+            x_quantised[c] = (x_codes, x_scales)
 
-        def gate_of(c):
-            width = CHUNKS[c]
-            x_codes, x_scales = x_ops[c]
-            for b in range(width // BLOCK):
-                ya = ps.tile([P, PACK, BLOCK], F32, name="ya", bufs=2)
-                xc = slice(b * BLOCK, (b + 1) * BLOCK)
+        def make_gate(c):
+            x_codes, x_scales = x_quantised[c]
+            for b in range(CHUNK // BLOCK):
+                ya = ps.tile([P, PACK, BLOCK], F32, name="ya", bufs=YA_BANKS)
+                in_chunk = slice(b * BLOCK, (b + 1) * BLOCK)
                 for t in range(PACK):
-                    m = slice(t * P, (t + 1) * P)
+                    dealt_cols = slice(t * P, (t + 1) * P)
                     nc.tensor.matmul_mx(
-                        ya[:, t, :], lhsT=wa_codes[:, m].bitcast(FP8X4), lhsT_scale=wa_scales[:, m],
-                        rhs=x_codes[:, xc].bitcast(FP8X4), rhs_scale=x_scales[:, xc], start=True, stop=True,
+                        ya[:, t, :],
+                        lhsT=wa_codes[:, dealt_cols].bitcast(FP8X4),
+                        lhsT_scale=wa_scales[:, dealt_cols],
+                        rhs=x_codes[:, in_chunk].bitcast(FP8X4),
+                        rhs_scale=x_scales[:, in_chunk],
+                        start=True,
+                        stop=True,
                     )
                 gate = tile("gate%d_%d" % (c, b), [P, BLOCK, PACK], F32)
                 nc.scalar.activation(gate[:], ya[:].rearrange("p t n -> p n t"), SILU)
                 gates[c, b] = gate
 
-        def middle(c):
-            j0, width = starts[c], CHUNKS[c]
-            h, c0 = divmod(j0, HALF)
-            h_bf = tile("h_bf%d" % c, [P, PACK * width], BF16)
-            for b in range(width // BLOCK):
-                yb = ps.tile([P, PACK, BLOCK], F32, name="yb", bufs=3)
-                vc = slice(c0 + b * BLOCK, c0 + (b + 1) * BLOCK)
-                jc = slice(j0 + b * BLOCK, j0 + (b + 1) * BLOCK)
+        def make_h(c):
+            h, in_half = divmod(c * CHUNK, HALF)
+            h_bf = tile("h_bf%d" % c, [P, PACK * CHUNK], BF16)
+            for b in range(CHUNK // BLOCK):
+                yb = ps.tile([P, PACK, BLOCK], F32, name="yb", bufs=YB_BANKS)
+                code_cols = slice(in_half + b * BLOCK, in_half + (b + 1) * BLOCK)
+                places = slice(c * CHUNK + b * BLOCK, c * CHUNK + (b + 1) * BLOCK)
                 for t in range(PACK):
-                    m = slice(t * P, (t + 1) * P)
+                    dealt_cols = slice(t * P, (t + 1) * P)
                     nc.tensor.matmul_mx(
-                        yb[:, t, :], lhsT=wb_codes[:, m].bitcast(FP8X4), lhsT_scale=wb_scales[:, m],
-                        rhs=v_codes[h][:, vc].bitcast(FP8X4), rhs_scale=v_scales[:, jc], start=True, stop=True,
+                        yb[:, t, :],
+                        lhsT=wb_codes[:, dealt_cols].bitcast(FP8X4),
+                        lhsT_scale=wb_scales[:, dealt_cols],
+                        rhs=v_codes[h][:, code_cols].bitcast(FP8X4),
+                        rhs_scale=v_scales[:, places],
+                        start=True,
+                        stop=True,
                     )
                 nc.vector.tensor_tensor(
-                    h_bf[:, b * PACK * BLOCK : (b + 1) * PACK * BLOCK].rearrange("p (n t) -> p n t", t=PACK),
+                    h_bf[:, b * BANK : (b + 1) * BANK].rearrange("p (n t) -> p n t", t=PACK),
                     gates[c, b][:],
                     yb[:].rearrange("p t n -> p n t"),
                     MULT,
                 )
-            h_codes = tile("h_codes%d" % c, [P, width], U32)
-            h_scales = tile("h_scales%d" % c, [P, width], U8)
+            h_codes = tile("h_codes%d" % c, [P, CHUNK], U32)
+            h_scales = tile("h_scales%d" % c, [P, CHUNK], U8)
             nc.vector.quantize_mx(h_codes[:].bitcast(FP8X4), h_scales[:], h_bf[:])
-            h_ops[c] = (h_codes, h_scales)
+            h_quantised[c] = (h_codes, h_scales)
 
-        def back(c, j0, width, copy):
-            h, c0 = divmod(j0, HALF)
-            h_codes, h_scales = h_ops[c]
-            hc = slice(j0 - starts[c], j0 - starts[c] + width)
-            jc = slice(j0, j0 + width)
-            y_out = tile("y_out%d" % j0, [P, PACK, width], F32)
-            per_bank = HALF // width
+        def make_out(c, in_chunk, copy):
+            width = in_chunk.stop - in_chunk.start
+            j0 = c * CHUNK + in_chunk.start
+            h, in_half = divmod(j0, HALF)
+            h_codes, h_scales = h_quantised[c]
+            out_f32 = tile("out_f32_%d" % j0, [P, PACK, width], F32)
+            per_bank = BANK // width
             for t0 in range(0, PACK, per_bank):
-                y = ps.tile([P, per_bank, width], F32, name="y", bufs=3)
-                for e in range(per_bank):
-                    t = t0 + e
+                y = ps.tile([P, per_bank, width], F32, name="y", bufs=Y_BANKS)
+                for t in range(t0, t0 + per_bank):
                     nc.tensor.matmul_mx(
-                        y[:, e, :], lhsT=wd_codes[:, 2 * t * P : 2 * (t + 1) * P].bitcast(FP4X4),
-                        lhsT_scale=wd_sc[:, t * P : (t + 1) * P],
-                        rhs=h_codes[:, hc].bitcast(FP8X4), rhs_scale=h_scales[:, hc], start=True, stop=True,
+                        y[:, t - t0, :],
+                        lhsT=wd_codes[:, 2 * t * P : 2 * (t + 1) * P].bitcast(FP4X4),
+                        lhsT_scale=wd_dealt_scales[:, t * P : (t + 1) * P],
+                        rhs=h_codes[:, in_chunk].bitcast(FP8X4),
+                        rhs_scale=h_scales[:, in_chunk],
+                        start=True,
+                        stop=True,
                     )
-                nc.vector.tensor_tensor(
-                    y_out[:, t0 : t0 + per_bank, :], y[:], res_half[h][:, t0 : t0 + per_bank, c0 : c0 + width], ADD
-                )
-            nc.sync.dma_start(out_rows[:, :, jc], y_out[:])
-            interleave(copy, o_bf[c][:, PACK * hc.start : PACK * hc.stop], y_out[:])
+                rows = slice(t0, t0 + per_bank)
+                nc.vector.tensor_tensor(out_f32[:, rows, :], y[:], res_half[h][:, rows, in_half : in_half + width], ADD)
+                nc.sync.dma_start(out_hbm[:, rows, j0 : j0 + width], out_f32[:, rows, :])
+            round_into_words(copy, out_bf[c][:, PACK * in_chunk.start : PACK * in_chunk.stop], out_f32[:])
 
-        def planes(c):
-            jc = slice(starts[c], starts[c] + CHUNKS[c])
-            o_codes = tile("o_codes%d" % c, [P, CHUNKS[c]], U32)
-            nc.vector.quantize_mx(o_codes[:].bitcast(FP8X4), out_plane[:, jc], o_bf[c][:])
-            nc.sync.dma_start(out_words[:, jc], o_codes[:].bitcast(I32))
+        def quantise_out(c):
+            places = slice(c * CHUNK, (c + 1) * CHUNK)
+            out_codes = tile("out_codes%d" % c, [P, CHUNK], U32)
+            nc.vector.quantize_mx(out_codes[:].bitcast(FP8X4), out_scales[:, places], out_bf[c][:])
+            nc.sync.dma_start(out_words_hbm[:, places], out_codes[:].bitcast(I32))
 
-        o_bf = [tile("o_bf%d" % c, [P, PACK * CHUNKS[c]], BF16) for c in range(len(CHUNKS))]
+        out_bf = [tile("out_bf%d" % c, [P, PACK * CHUNK], BF16) for c in range(CHUNKS)]
+
         for h in range(J // HALF):
             gather_x(0, h * HALF, HALF)
-        for i in range(1, PACK - 1):
-            gather_x(i, 0, J)
-        wa_codes, wa_scales = quantise_weight("wa", wa_raw, [nc.scalar.copy, nc.scalar.copy])
-        for j0, width in ((0, 256), (256, 256), (512, 512)):
-            gather_x(PACK - 1, j0, width)
-        front(0)
-        wb_codes, wb_scales = quantise_weight("wb", wb_raw, [nc.scalar.copy, nc.vector.tensor_copy])
-        gate_of(0)
+        gather_x(1, 0, J)
+        wa_codes, wa_scales = quantise_weight("wa", wa_raw, [nc.scalar.copy, nc.vector.tensor_copy])
+        gather_x(2, 0, J)
+        gather_x(3, 0, CHUNK)
+        gather_x(3, CHUNK, CHUNK)
+        gather_x(3, HALF, HALF)
+        quantise_x(0)
+        wb_codes, wb_scales = quantise_weight("wb", wb_raw, [nc.vector.tensor_copy, nc.vector.tensor_copy])
+        make_gate(0)
         for h in range(J // HALF):
             gather_v(h)
-        for step in range(1, len(CHUNKS) + 2):
-            if step < len(CHUNKS):
-                front(step)
-                gate_of(step)
-            if step - 1 < len(CHUNKS):
-                middle(step - 1)
+
+        last = CHUNKS - 1
+        for step in range(1, CHUNKS + 2):
+            if step <= last:
+                quantise_x(step)
+                make_gate(step)
+            if step - 1 <= last:
+                make_h(step - 1)
             if step >= 2:
                 c = step - 2
-                if c < len(CHUNKS) - 1:
-                    back(c, starts[c], CHUNKS[c], nc.scalar.copy)
+                if c < last:
+                    make_out(c, slice(0, CHUNK), nc.scalar.copy)
                 else:
-                    back(c, starts[c], BLOCK, nc.scalar.copy)
-                    back(c, starts[c] + BLOCK, BLOCK, nc.vector.tensor_copy)
-                planes(c)
-        for q in range(4):
-            queue = nc.sync if q < 2 else nc.scalar
-            queue.dma_start(out_2[0, 4 * q : 4 * q + 4, :].bitcast(I32), out_plane[32 * q : 32 * q + 4, :].bitcast(I32))
+                    make_out(c, slice(0, BLOCK), nc.scalar.copy)
+                    make_out(c, slice(BLOCK, CHUNK), nc.vector.tensor_copy)
+                quantise_out(c)
+
+        for q in range(QUADRANTS):
+            queue = nc.sync if q < QUADRANTS // 2 else nc.scalar
+            queue.dma_start(hbm_scale_rows(out_2, q), scale_rows(out_scales, q))

@@ -22,12 +22,14 @@ SILU = mybir.ActivationFunctionType.Silu
 P = 128
 PACK = 4
 QUADRANTS = 4
+SCALE_ROWS = 16
 LIST_ROWS = 16
 BANK = 512
 BLOCK = BANK // PACK
 CHUNK = 256
 CHUNKS = J // CHUNK
 HALF = J // 2
+FIRST_PIECES = ((0, 256), (256, 256), (512, 512))
 YA_BANKS, YB_BANKS, Y_BANKS = 2, 3, 3
 
 
@@ -51,6 +53,7 @@ def tile_list_htabg_glu_resP_kernel(
         tab_list = tile("tab_list", [P, J // LIST_ROWS], U16)
         head_lists = tile("head_lists", [P, J // LIST_ROWS], U16)
         tab_scale_tile = tile("tab_scale_tile", [P, T], U8)
+        v_scales = tile("v_scales", [P, J], U8)
         wd_raw_scales = tile("wd_raw_scales", [P, N], U8)
         wd_raw_codes = tile("wd_raw_codes", [P, 2 * N], U8)
         x_rows = [tile("x_rows%d" % i, [P, T], F32) for i in range(PACK)]
@@ -60,51 +63,62 @@ def tile_list_htabg_glu_resP_kernel(
         wb_raw = tile("wb_raw", [P, PACK, R], F32)
         res_half = [tile("res%d" % h, [P, PACK, HALF], F32) for h in range(J // HALF)]
 
-        nc.gpsimd.memset(tab_scale_tile[:].bitcast(I32), 0)
-        nc.gpsimd.memset(wd_raw_scales[:].bitcast(I32), 0)
-
         blocks = J // P
         wgt_rows = tile("wgt_rows", [P, P], F32)
         ident = tile("ident", [P, P], F32)
-        nc.vector.memset(wgt_rows[HEADS * blocks :, :], 0.0)
         make_identity(nc, ident[:])
+        nc.vector.memset(wd_raw_scales[:].bitcast(I32), 0)
+        nc.vector.memset(wgt_rows[HEADS * blocks :, :], 0.0)
+        staged = P - SCALE_ROWS
+        nc.vector.memset(tab_scale_tile[:staged, :].bitcast(I32), 0)
+        nc.vector.memset(v_scales[:].bitcast(I32), 0)
         warm = tile("warm", [P, 1], F32)
         nc.scalar.activation(warm[:], ident[:, 0:1], SILU)
 
         x_hbm = xT.rearrange("(p i) t -> p i t", i=PACK)
         res_hbm = res.rearrange("(p t) j -> p t j", t=PACK)
-        nc.scalar.dma_start(wgt_rows[: HEADS * blocks, :], wgt2.rearrange("(g q) (b j) -> q g b j", q=LIST_ROWS, j=P)[0])
+        wb_hbm = wb.rearrange("(p i) r -> p i r", i=PACK)
+        nc.sync.dma_start(wgt_rows[: HEADS * blocks, :], wgt2.rearrange("(g q) (b j) -> q g b j", q=LIST_ROWS, j=P)[0])
         nc.sync.dma_start(tab_list[:], offs)
+        nc.sync.dma_start(tab_scale_tile[staged:, :].bitcast(I32), tab_scales[0].bitcast(I32))
         nc.sync.dma_start(wd_raw_codes[:].bitcast(I32), wd_words[0].bitcast(I32))
-        for q in range(QUADRANTS):
-            nc.sync.dma_start(scale_rows(tab_scale_tile, q), hbm_scale_rows(tab_scales, q))
         nc.sync.dma_start(x_rows[0][:], x_hbm[:, 0, :])
         nc.sync.dma_start(head_lists[:], offs2)
-        nc.sync.dma_start(x_rows[1][:], x_hbm[:, 1, :])
         for q in range(QUADRANTS):
             nc.sync.dma_start(scale_rows(wd_raw_scales, q), hbm_scale_rows(wd_scales, q))
-        nc.sync.dma_start(wa_raw[:], wa.rearrange("(p i) r -> p i r", i=PACK))
+        nc.sync.dma_start(x_rows[1][:], x_hbm[:, 1, :])
         nc.sync.dma_start(x_rows[2][:], x_hbm[:, 2, :])
+        nc.sync.dma_start(wa_raw[:], wa.rearrange("(p i) r -> p i r", i=PACK))
+
+        v_staged = tile("v_staged", [P, J], U8)
+        nc.vector.tensor_copy(v_staged[:], tab_scale_tile[:].indirect(tab_list[:]))
+        for q in range(QUADRANTS):
+            nc.sync.dma_start(scale_rows(v_scales, q), v_staged[staged + 4 * q : staged + 4 * q + 4, :].bitcast(I32))
+
         nc.sync.dma_start(x_rows[3][:], x_hbm[:, 3, :])
-        nc.sync.dma_start(wb_raw[:], wb.rearrange("(p i) r -> p i r", i=PACK))
-        nc.sync.dma_start(tab_codes[:].bitcast(I32), tab_words[0].rearrange("p t i -> p (t i)").bitcast(I32))
+
+        def load_tab():
+            nc.sync.dma_start(tab_codes[:].bitcast(I32), tab_words[0].rearrange("p t i -> p (t i)").bitcast(I32))
+
+        def load_wb():
+            nc.sync.dma_start(wb_raw[:], wb_hbm)
+
+        load_wb()
+        load_tab()
         for h in range(J // HALF):
             nc.sync.dma_start(res_half[h][:], res_hbm[:, :, h * HALF : (h + 1) * HALF])
 
         wgt_turned = ps.tile([P, P], F32, name="y", bufs=Y_BANKS)
         nc.tensor.transpose(wgt_turned[:], wgt_rows[:], ident[:])
         by_block = wgt_turned[:, : HEADS * blocks].rearrange("p (g b) -> p b g", b=blocks)
-        for h in range(J // HALF):
-            shape = [P, HALF // P, HEADS, LIST_ROWS]
-            repeated = tile("repeated%d" % h, shape, F32)
-            nc.scalar.copy(repeated[:], by_block[:, shape[1] * h : shape[1] * (h + 1), :].unsqueeze(3).to_broadcast(shape))
-            wgt_bank = ps.tile([P, HALF // P, P], F32, name="yb", bufs=YB_BANKS)
-            for b in range(HALF // P):
+        for j0, width in FIRST_PIECES:
+            shape = [P, width // P, HEADS, LIST_ROWS]
+            repeated = tile("repeated%d" % j0, shape, F32)
+            nc.scalar.copy(repeated[:], by_block[:, j0 // P : (j0 + width) // P, :].unsqueeze(3).to_broadcast(shape))
+            wgt_bank = ps.tile([P, width // P, P], F32, name="yb", bufs=YB_BANKS)
+            for b in range(width // P):
                 nc.tensor.transpose(wgt_bank[:, b, :], repeated[:, b].rearrange("p g q -> p (g q)"), ident[:])
-            nc.scalar.copy(wgt[:, h * HALF : (h + 1) * HALF], wgt_bank[:].rearrange("p b j -> p (b j)"))
-
-        v_scales = tile("v_scales", [P, J], U8)
-        nc.vector.tensor_copy(v_scales[:], tab_scale_tile[:].indirect(tab_list[:]))
+            nc.scalar.copy(wgt[:, j0 : j0 + width], wgt_bank[:].rearrange("p b j -> p (b j)"))
 
         wd_codes = tile("wd_codes", [P, 2 * N], U8)
         wd_dealt_scales = tile("wd_dealt_scales", [P, N], U8)
@@ -122,9 +136,15 @@ def tile_list_htabg_glu_resP_kernel(
         out_hbm = out_0.rearrange("(p t) j -> p t j", t=PACK)
         out_words_hbm = out_1[0].rearrange("p j i -> p (j i)").bitcast(I32)
         out_scales = tile("out_scales", [P, J], U8)
-        x_quantised = {}
+        x_codes = {}
+        x_scales = tile("x_scales", [P, J], U8)
+        h_bf = tile("h_bf", [P, PACK * J], BF16)
+        h_codes = tile("h_codes", [P, J], U32)
+        h_scales = tile("h_scales", [P, J], U8)
+        out_bf = tile("out_bf", [P, PACK * J], BF16)
+        out_codes = tile("out_codes", [P, J], U32)
         gates = {}
-        h_quantised = {}
+        out_f32 = [tile("out_f32_%d" % c, [P, PACK, CHUNK], F32) for c in range(CHUNKS)]
 
         def gather_x(i, j0, width):
             nc.vector.tensor_tensor(
@@ -138,141 +158,159 @@ def tile_list_htabg_glu_resP_kernel(
             entries = slice(h * HALF // LIST_ROWS, (h + 1) * HALF // LIST_ROWS)
             nc.vector.tensor_copy(v_codes[h][:], tab_codes[:].indirect(tab_list[:, entries]))
 
-        def quantise_weight(name, raw, copies):
-            dealt = tile(name + "_bf", [P, PACK * R], BF16)
-            codes = tile(name + "_codes", [P, R], U32)
-            scales = tile(name + "_scales", [P, R], U8)
-            src = raw[:].rearrange("p i (m u e) -> p u m i e", u=2, e=2)
+        def quantise_wa(copies):
+            dealt = tile("wa_bf", [P, PACK * R], BF16)
+            codes = tile("wa_codes", [P, R], U32)
+            scales = tile("wa_scales", [P, R], U8)
+            src = wa_raw[:].rearrange("p i (m u e) -> p u m i e", u=2, e=2)
             dst = dealt[:].rearrange("p (u e m i) -> p u m i e", u=2, e=2, i=PACK)
             for u in range(2):
                 copies[u](dst[:, u], src[:, u])
             nc.vector.quantize_mx(codes[:].bitcast(FP8X4), scales[:], dealt[:])
             return codes, scales
 
-        def round_into_words(copy, dst, src):
+        def quantise_wb(copies):
+            dealt = tile("wb_bf", [P, PACK * R], BF16)
+            codes = tile("wb_codes", [P, R], U32)
+            scales = tile("wb_scales", [P, R], U8)
+            src = wb_raw[:].rearrange("p i (m u e) -> p u m i e", u=2, e=2)
+            dst = dealt[:].rearrange("p (u e m i) -> p u m i e", u=2, e=2, i=PACK)
+            for u in range(2):
+                copies[u](dst[:, u], src[:, u])
+            nc.vector.quantize_mx(codes[:].bitcast(FP8X4), scales[:], dealt[:])
+            return codes, scales
+
+        def words(t, j0, width):
+            return t[:, PACK * j0 : PACK * (j0 + width)]
+
+        def round_into_words(copy, dst, src, rows=slice(0, PACK)):
             copy(
-                dst.rearrange("p (c e i) -> p c i e", e=4, i=PACK),
-                src.rearrange("p i (c e) -> p c i e", e=4),
+                dst.rearrange("p (c e i) -> p c i e", e=4, i=PACK)[:, :, rows, :],
+                src.rearrange("p i (c e) -> p c i e", e=4)[:, :, rows, :],
             )
 
-        def quantise_x(c):
+        def quantise_x(c, slot=None):
             x_bf = tile("x_bf%d" % c, [P, PACK * CHUNK], BF16)
-            x_codes = tile("x_codes%d" % c, [P, CHUNK], U32)
-            x_scales = tile("x_scales%d" % c, [P, CHUNK], U8)
-            round_into_words(nc.scalar.copy, x_bf[:], picked[:, :, c * CHUNK : (c + 1) * CHUNK])
-            nc.vector.quantize_mx(x_codes[:].bitcast(FP8X4), x_scales[:], x_bf[:])
-            x_quantised[c] = (x_codes, x_scales)
-
-        def make_gate(c):
-            x_codes, x_scales = x_quantised[c]
-            for b in range(CHUNK // BLOCK):
-                ya = ps.tile([P, PACK, BLOCK], F32, name="ya", bufs=YA_BANKS)
-                in_chunk = slice(b * BLOCK, (b + 1) * BLOCK)
-                for t in range(PACK):
-                    dealt_cols = slice(t * P, (t + 1) * P)
-                    nc.tensor.matmul_mx(
-                        ya[:, t, :],
-                        lhsT=wa_codes[:, dealt_cols].bitcast(FP8X4),
-                        lhsT_scale=wa_scales[:, dealt_cols],
-                        rhs=x_codes[:, in_chunk].bitcast(FP8X4),
-                        rhs_scale=x_scales[:, in_chunk],
-                        start=True,
-                        stop=True,
-                    )
-                gate = tile("gate%d_%d" % (c, b), [P, BLOCK, PACK], F32)
-                nc.scalar.activation(gate[:], ya[:].rearrange("p t n -> p n t"), SILU)
-                gates[c, b] = gate
-
-        def make_h(c):
-            h, in_half = divmod(c * CHUNK, HALF)
-            h_bf = tile("h_bf%d" % c, [P, PACK * CHUNK], BF16)
-            for b in range(CHUNK // BLOCK):
-                yb = ps.tile([P, PACK, BLOCK], F32, name="yb", bufs=YB_BANKS)
-                code_cols = slice(in_half + b * BLOCK, in_half + (b + 1) * BLOCK)
-                places = slice(c * CHUNK + b * BLOCK, c * CHUNK + (b + 1) * BLOCK)
-                for t in range(PACK):
-                    dealt_cols = slice(t * P, (t + 1) * P)
-                    nc.tensor.matmul_mx(
-                        yb[:, t, :],
-                        lhsT=wb_codes[:, dealt_cols].bitcast(FP8X4),
-                        lhsT_scale=wb_scales[:, dealt_cols],
-                        rhs=v_codes[h][:, code_cols].bitcast(FP8X4),
-                        rhs_scale=v_scales[:, places],
-                        start=True,
-                        stop=True,
-                    )
-                nc.vector.tensor_tensor(
-                    h_bf[:, b * BANK : (b + 1) * BANK].rearrange("p (n t) -> p n t", t=PACK),
-                    gates[c, b][:],
-                    yb[:].rearrange("p t n -> p n t"),
-                    MULT,
-                )
-            h_codes = tile("h_codes%d" % c, [P, CHUNK], U32)
-            h_scales = tile("h_scales%d" % c, [P, CHUNK], U8)
-            nc.vector.quantize_mx(h_codes[:].bitcast(FP8X4), h_scales[:], h_bf[:])
-            h_quantised[c] = (h_codes, h_scales)
-
-        def make_out(c, in_chunk, copy):
-            width = in_chunk.stop - in_chunk.start
-            j0 = c * CHUNK + in_chunk.start
-            h, in_half = divmod(j0, HALF)
-            h_codes, h_scales = h_quantised[c]
-            out_f32 = tile("out_f32_%d" % j0, [P, PACK, width], F32)
-            per_bank = BANK // width
-            for t0 in range(0, PACK, per_bank):
-                y = ps.tile([P, per_bank, width], F32, name="y", bufs=Y_BANKS)
-                for t in range(t0, t0 + per_bank):
-                    nc.tensor.matmul_mx(
-                        y[:, t - t0, :],
-                        lhsT=wd_codes[:, 2 * t * P : 2 * (t + 1) * P].bitcast(FP4X4),
-                        lhsT_scale=wd_dealt_scales[:, t * P : (t + 1) * P],
-                        rhs=h_codes[:, in_chunk].bitcast(FP8X4),
-                        rhs_scale=h_scales[:, in_chunk],
-                        start=True,
-                        stop=True,
-                    )
-                rows = slice(t0, t0 + per_bank)
-                nc.vector.tensor_tensor(out_f32[:, rows, :], y[:], res_half[h][:, rows, in_half : in_half + width], ADD)
-                nc.sync.dma_start(out_hbm[:, rows, j0 : j0 + width], out_f32[:, rows, :])
-            round_into_words(copy, out_bf[c][:, PACK * in_chunk.start : PACK * in_chunk.stop], out_f32[:])
-
-        def quantise_out(c):
+            x_codes[c] = tile(slot or "x_codes%d" % c, [P, CHUNK], U32)
             places = slice(c * CHUNK, (c + 1) * CHUNK)
-            out_codes = tile("out_codes%d" % c, [P, CHUNK], U32)
-            nc.vector.quantize_mx(out_codes[:].bitcast(FP8X4), out_scales[:, places], out_bf[c][:])
-            nc.sync.dma_start(out_words_hbm[:, places], out_codes[:].bitcast(I32))
+            round_into_words(nc.scalar.copy, x_bf[:], picked[:, :, places])
+            nc.vector.quantize_mx(x_codes[c][:].bitcast(FP8X4), x_scales[:, places], x_bf[:])
 
-        out_bf = [tile("out_bf%d" % c, [P, PACK * CHUNK], BF16) for c in range(CHUNKS)]
+        def quantise(codes, scales, src, j0, width):
+            nc.vector.quantize_mx(codes[:, j0 : j0 + width].bitcast(FP8X4), scales[:, j0 : j0 + width], words(src, j0, width))
 
-        for h in range(J // HALF):
-            gather_x(0, h * HALF, HALF)
+        def make_gate(b, slot=None):
+            places = slice(b * BLOCK, (b + 1) * BLOCK)
+            c, in_chunk = divmod(b * BLOCK, CHUNK)
+            ya = ps.tile([P, PACK, BLOCK], F32, name="ya", bufs=YA_BANKS)
+            for t in range(PACK):
+                dealt_cols = slice(t * P, (t + 1) * P)
+                nc.tensor.matmul_mx(
+                    ya[:, t, :],
+                    lhsT=wa_codes[:, dealt_cols].bitcast(FP8X4),
+                    lhsT_scale=wa_scales[:, dealt_cols],
+                    rhs=x_codes[c][:, in_chunk : in_chunk + BLOCK].bitcast(FP8X4),
+                    rhs_scale=x_scales[:, places],
+                    start=True,
+                    stop=True,
+                )
+            gate = tile(slot or "gate%d" % b, [P, BLOCK, PACK], F32)
+            nc.scalar.activation(gate[:], ya[:].rearrange("p t n -> p n t"), SILU)
+            gates[b] = gate
+
+        def make_h(b):
+            h, in_half = divmod(b * BLOCK, HALF)
+            yb = ps.tile([P, PACK, BLOCK], F32, name="yb", bufs=YB_BANKS)
+            for t in range(PACK):
+                dealt_cols = slice(t * P, (t + 1) * P)
+                nc.tensor.matmul_mx(
+                    yb[:, t, :],
+                    lhsT=wb_codes[:, dealt_cols].bitcast(FP8X4),
+                    lhsT_scale=wb_scales[:, dealt_cols],
+                    rhs=v_codes[h][:, in_half : in_half + BLOCK].bitcast(FP8X4),
+                    rhs_scale=v_scales[:, b * BLOCK : (b + 1) * BLOCK],
+                    start=True,
+                    stop=True,
+                )
+            nc.vector.tensor_tensor(
+                words(h_bf, b * BLOCK, BLOCK).rearrange("p (n t) -> p n t", t=PACK),
+                gates[b][:],
+                yb[:].rearrange("p t n -> p n t"),
+                MULT,
+            )
+
+        def make_out(b, copy):
+            j0 = b * BLOCK
+            h, in_half = divmod(j0, HALF)
+            c, in_chunk = divmod(j0, CHUNK)
+            places = slice(j0, j0 + BLOCK)
+            y = ps.tile([P, PACK, BLOCK], F32, name="y", bufs=Y_BANKS)
+            for t in range(PACK):
+                nc.tensor.matmul_mx(
+                    y[:, t, :],
+                    lhsT=wd_codes[:, 2 * t * P : 2 * (t + 1) * P].bitcast(FP4X4),
+                    lhsT_scale=wd_dealt_scales[:, t * P : (t + 1) * P],
+                    rhs=h_codes[:, places].bitcast(FP8X4),
+                    rhs_scale=h_scales[:, places],
+                    start=True,
+                    stop=True,
+                )
+            sums = out_f32[c][:, :, in_chunk : in_chunk + BLOCK]
+            nc.vector.tensor_tensor(sums, y[:], res_half[h][:, :, in_half : in_half + BLOCK], ADD)
+            if c >= CHUNKS - 2:
+                nc.sync.dma_start(out_hbm[:, :, places], sums)
+            elif in_chunk + BLOCK == CHUNK:
+                nc.sync.dma_start(out_hbm[:, :, c * CHUNK : (c + 1) * CHUNK], out_f32[c][:])
+            round_into_words(copy, words(out_bf, j0, BLOCK), sums)
+
+        def quantise_out(j0, width, queue=nc.sync):
+            quantise(out_codes, out_scales, out_bf, j0, width)
+            queue.dma_start(out_words_hbm[:, j0 : j0 + width], out_codes[:, j0 : j0 + width].bitcast(I32))
+
+        for j0, width in FIRST_PIECES:
+            gather_x(0, j0, width)
         gather_x(1, 0, J)
-        wa_codes, wa_scales = quantise_weight("wa", wa_raw, [nc.scalar.copy, nc.vector.tensor_copy])
         gather_x(2, 0, J)
+        wa_codes, wa_scales = quantise_wa([nc.scalar.copy, nc.vector.tensor_copy])
         gather_x(3, 0, CHUNK)
         gather_x(3, CHUNK, CHUNK)
         gather_x(3, HALF, HALF)
         quantise_x(0)
-        wb_codes, wb_scales = quantise_weight("wb", wb_raw, [nc.vector.tensor_copy, nc.vector.tensor_copy])
+        wb_codes, wb_scales = quantise_wb([nc.vector.tensor_copy, nc.vector.tensor_copy])
         make_gate(0)
-        for h in range(J // HALF):
-            gather_v(h)
-
+        make_gate(1)
+        quantise_x(1, None)
+        make_gate(2)
+        make_gate(3)
+        quantise_x(2, None)
+        gather_v(0)
+        gather_v(1)
+        make_h(0)
+        quantise_x(3, None)
+        make_h(1)
+        make_gate(4)
+        make_gate(5)
+        make_h(2)
+        quantise(h_codes, h_scales, h_bf, 0, CHUNK)
+        make_gate(6)
+        make_gate(7)
+        make_h(3)
+        make_out(0, nc.scalar.copy)
+        quantise(h_codes, h_scales, h_bf, CHUNK, CHUNK)
         last = CHUNKS - 1
-        for step in range(1, CHUNKS + 2):
-            if step <= last:
-                quantise_x(step)
-                make_gate(step)
-            if step - 1 <= last:
-                make_h(step - 1)
-            if step >= 2:
-                c = step - 2
-                if c < last:
-                    make_out(c, slice(0, CHUNK), nc.scalar.copy)
-                else:
-                    make_out(c, slice(0, BLOCK), nc.scalar.copy)
-                    make_out(c, slice(BLOCK, CHUNK), nc.vector.tensor_copy)
-                quantise_out(c)
+        for c in range(2, CHUNKS):
+            make_out(2 * c - 3, nc.scalar.copy)
+            make_h(2 * c)
+            make_out(2 * c - 2, nc.scalar.copy)
+            make_h(2 * c + 1)
+            quantise_out((c - 2) * CHUNK, CHUNK)
+            quantise(h_codes, h_scales, h_bf, c * CHUNK, CHUNK)
+        make_out(2 * last - 1, nc.scalar.copy)
+        make_out(2 * last, nc.scalar.copy)
+        make_out(2 * last + 1, nc.vector.tensor_copy)
+        quantise_out((last - 1) * CHUNK, CHUNK)
+        quantise_out(last * CHUNK, CHUNK, nc.scalar)
+
 
         for q in range(QUADRANTS):
             queue = nc.sync if q < QUADRANTS // 2 else nc.scalar

@@ -31,7 +31,7 @@ CHUNKS = J // CHUNK
 HALF = J // 2
 FIRST_PIECES = ((0, 256), (256, 256), (512, 512))
 YA_BANKS, YB_BANKS, Y_BANKS = 2, 3, 3
-
+PLACES = {"wa_raw": 0, "x_bf1": 0, "x_codes0": 8192, "x_bf2": 8192, "x_codes1": 10240, "x_bf3": 10240, "gate0": 12288, "v_codes2": 12288, "x_codes2": 13312, "gate2": 14336, "v_codes3": 14336, "x_codes3": 15360}
 
 def tile_list_htabg_glu_resP_kernel(
     tc, tab_words, tab_scales, xT, wgt2, wa, wb, wd_words, wd_scales, res, offs, offs2, out_0, out_1, out_2
@@ -39,10 +39,14 @@ def tile_list_htabg_glu_resP_kernel(
     nc = tc.nc
     with ExitStack() as ctx:
         sb = ctx.enter_context(tc.tile_pool(name="sb", bufs=1))
+        placed = ctx.enter_context(tc.tile_pool(name="placed", bufs=1))
         ps = ctx.enter_context(tc.psum_pool(name="ps", bufs=1))
 
         def tile(name, shape, dtype):
-            return sb.tile(shape, dtype, name=name, align_bytes=64)
+            at = PLACES.get(name)
+            if at is None:
+                return sb.tile(shape, dtype, name=name, align_bytes=64)
+            return placed.tile(shape, dtype, name=name, align_bytes=64, offset=at)
 
         def scale_rows(scale_tile, q):
             return scale_tile[32 * q : 32 * q + 4, :].bitcast(I32)
@@ -53,6 +57,7 @@ def tile_list_htabg_glu_resP_kernel(
         tab_list = tile("tab_list", [P, J // LIST_ROWS], U16)
         head_lists = tile("head_lists", [P, J // LIST_ROWS], U16)
         tab_scale_tile = tile("tab_scale_tile", [P, T], U8)
+        v_staged = tile("v_staged", [P, J], U8)
         v_scales = tile("v_scales", [P, J], U8)
         wd_raw_scales = tile("wd_raw_scales", [P, N], U8)
         wd_raw_codes = tile("wd_raw_codes", [P, 2 * N], U8)
@@ -78,35 +83,65 @@ def tile_list_htabg_glu_resP_kernel(
         x_hbm = xT.rearrange("(p i) t -> p i t", i=PACK)
         res_hbm = res.rearrange("(p t) j -> p t j", t=PACK)
         wb_hbm = wb.rearrange("(p i) r -> p i r", i=PACK)
-        nc.sync.dma_start(wgt_rows[: HEADS * blocks, :], wgt2.rearrange("(g q) (b j) -> q g b j", q=LIST_ROWS, j=P)[0])
-        nc.sync.dma_start(tab_list[:], offs)
-        nc.sync.dma_start(tab_scale_tile[staged:, :].bitcast(I32), tab_scales[0].bitcast(I32))
-        nc.sync.dma_start(wd_raw_codes[:].bitcast(I32), wd_words[0].bitcast(I32))
-        nc.sync.dma_start(x_rows[0][:], x_hbm[:, 0, :])
-        nc.sync.dma_start(head_lists[:], offs2)
-        for q in range(QUADRANTS):
-            nc.sync.dma_start(scale_rows(wd_raw_scales, q), hbm_scale_rows(wd_scales, q))
-        nc.sync.dma_start(x_rows[1][:], x_hbm[:, 1, :])
-        nc.sync.dma_start(x_rows[2][:], x_hbm[:, 2, :])
-        nc.sync.dma_start(wa_raw[:], wa.rearrange("(p i) r -> p i r", i=PACK))
 
-        v_staged = tile("v_staged", [P, J], U8)
-        nc.vector.tensor_copy(v_staged[:], tab_scale_tile[:].indirect(tab_list[:]))
-        for q in range(QUADRANTS):
-            nc.sync.dma_start(scale_rows(v_scales, q), v_staged[staged + 4 * q : staged + 4 * q + 4, :].bitcast(I32))
+        def load_x(i):
+            nc.sync.dma_start(x_rows[i][:], x_hbm[:, i, :])
 
-        nc.sync.dma_start(x_rows[3][:], x_hbm[:, 3, :])
-
-        def load_tab():
-            nc.sync.dma_start(tab_codes[:].bitcast(I32), tab_words[0].rearrange("p t i -> p (t i)").bitcast(I32))
+        def load_wa():
+            nc.sync.dma_start(wa_raw[:], wa.rearrange("(p i) r -> p i r", i=PACK))
 
         def load_wb():
             nc.sync.dma_start(wb_raw[:], wb_hbm)
 
+        def load_tab():
+            nc.sync.dma_start(tab_codes[:].bitcast(I32), tab_words[0].rearrange("p t i -> p (t i)").bitcast(I32))
+
+        def load_wd_codes():
+            nc.sync.dma_start(wd_raw_codes[:].bitcast(I32), wd_words[0].bitcast(I32))
+
+        def load_wd_scales():
+            for q in range(QUADRANTS):
+                nc.sync.dma_start(scale_rows(wd_raw_scales, q), hbm_scale_rows(wd_scales, q))
+
+        def load_res(h):
+            nc.sync.dma_start(res_half[h][:], res_hbm[:, :, h * HALF : (h + 1) * HALF])
+
+        def gather_v_scales():
+            nc.vector.tensor_copy(v_staged[:], tab_scale_tile[:].indirect(tab_list[:]))
+
+        def carry_v_scales():
+            for q in range(QUADRANTS):
+                nc.sync.dma_start(scale_rows(v_scales, q), v_staged[staged + 4 * q : staged + 4 * q + 4, :].bitcast(I32))
+
+        def load_tab_list():
+            nc.sync.dma_start(tab_list[:], offs)
+
+        def load_tab_scales():
+            nc.sync.dma_start(tab_scale_tile[staged:, :].bitcast(I32), tab_scales[0].bitcast(I32))
+
+        def load_wgt():
+            nc.sync.dma_start(wgt_rows[: HEADS * blocks, :], wgt2.rearrange("(g q) (b j) -> q g b j", q=LIST_ROWS, j=P)[0])
+
+        def load_head_lists():
+            nc.sync.dma_start(head_lists[:], offs2)
+
+        load_tab_list()
+        load_tab_scales()
+        load_wgt()
+        load_wd_codes()
+        load_x(0)
+        load_head_lists()
+        load_wd_scales()
+        load_x(1)
+        load_x(2)
+        load_x(3)
+        gather_v_scales()
+        carry_v_scales()
+        load_wa()
         load_wb()
         load_tab()
-        for h in range(J // HALF):
-            nc.sync.dma_start(res_half[h][:], res_hbm[:, :, h * HALF : (h + 1) * HALF])
+        load_res(0)
+        load_res(1)
 
         wgt_turned = ps.tile([P, P], F32, name="y", bufs=Y_BANKS)
         nc.tensor.transpose(wgt_turned[:], wgt_rows[:], ident[:])
@@ -122,66 +157,71 @@ def tile_list_htabg_glu_resP_kernel(
 
         wd_codes = tile("wd_codes", [P, 2 * N], U8)
         wd_dealt_scales = tile("wd_dealt_scales", [P, N], U8)
-        nc.vector.tensor_copy(
-            wd_codes[:].bitcast(U16).rearrange("p (t m) -> p t m", t=PACK),
-            wd_raw_codes[:].bitcast(U16).rearrange("p (m t) -> p t m", t=PACK),
-        )
-        nc.vector.tensor_copy(
-            wd_dealt_scales[:].rearrange("p (t m) -> p t m", t=PACK),
-            wd_raw_scales[:].rearrange("p (m t) -> p t m", t=PACK),
-        )
-
-        picked = tile("picked", [P, PACK, J], F32)
-        v_codes = [tile("v_codes%d" % h, [P, HALF], U32) for h in range(J // HALF)]
+        picked = [tile("picked%d" % c, [P, PACK, J // 1], F32) for c in range(1)]
+        v_codes = [tile("v_codes%d" % c, [P, CHUNK], U32) for c in range(CHUNKS)]
         out_hbm = out_0.rearrange("(p t) j -> p t j", t=PACK)
         out_words_hbm = out_1[0].rearrange("p j i -> p (j i)").bitcast(I32)
         out_scales = tile("out_scales", [P, J], U8)
-        x_codes = {}
         x_scales = tile("x_scales", [P, J], U8)
-        h_bf = tile("h_bf", [P, PACK * J], BF16)
         h_codes = tile("h_codes", [P, J], U32)
         h_scales = tile("h_scales", [P, J], U8)
-        out_bf = tile("out_bf", [P, PACK * J], BF16)
         out_codes = tile("out_codes", [P, J], U32)
-        gates = {}
-        out_f32 = [tile("out_f32_%d" % c, [P, PACK, CHUNK], F32) for c in range(CHUNKS)]
+        wa_bf = tile("wa_bf", [P, PACK * R], BF16)
+        wa_codes = tile("wa_codes", [P, R], U32)
+        wa_scales = tile("wa_scales", [P, R], U8)
+        wb_bf = tile("wb_bf", [P, PACK * R], BF16)
+        wb_codes = tile("wb_codes", [P, R], U32)
+        wb_scales = tile("wb_scales", [P, R], U8)
+        x_bf = [tile("x_bf%d" % c, [P, PACK * CHUNK], BF16) for c in range(CHUNKS)]
+        x_codes = [tile("x_codes%d" % c, [P, CHUNK], U32) for c in range(CHUNKS)]
+        out_bf = [tile("out_bf%d" % c, [P, PACK * CHUNK], BF16) for c in range(CHUNKS)]
+        gates = [tile("gate%d" % b, [P, BLOCK, PACK], F32) for b in range(blocks)]
+        shared = [tile("shared%d" % c, [P, PACK * CHUNK + 3 * BLOCK], F32) for c in range(CHUNKS)]
+        sums = [t[:, : PACK * CHUNK].rearrange("p (t j) -> p t j", t=PACK) for t in shared]
+        h_first = tile("h_first", [P, PACK * CHUNK], BF16)
+        h_bf = [h_first[:]] + [t[:, PACK * CHUNK - BLOCK :].bitcast(BF16) for t in shared[:2]] + [tile("h_last", [P, PACK * CHUNK], BF16)[:]]
+        y_banks = {}
+
+        def gpsimd_round(dst, src):
+            nc.gpsimd.tensor_scalar(dst, src, 1.0, 0.0, MULT, ADD)
+
+        def deal_wd_codes(copy):
+            copy(
+                wd_codes[:].bitcast(U16).rearrange("p (t m) -> p t m", t=PACK),
+                wd_raw_codes[:].bitcast(U16).rearrange("p (m t) -> p t m", t=PACK),
+            )
+
+        def deal_wd_scales(copy):
+            copy(
+                wd_dealt_scales[:].rearrange("p (t m) -> p t m", t=PACK),
+                wd_raw_scales[:].rearrange("p (m t) -> p t m", t=PACK),
+            )
 
         def gather_x(i, j0, width):
+            c, at = divmod(j0, J // len(picked))
             nc.vector.tensor_tensor(
-                picked[:, i, j0 : j0 + width],
+                picked[c][:, i, at : at + width],
                 x_rows[i][:].indirect(head_lists[:, j0 // LIST_ROWS : (j0 + width) // LIST_ROWS]),
                 wgt[:, j0 : j0 + width],
                 MULT,
             )
 
-        def gather_v(h):
-            entries = slice(h * HALF // LIST_ROWS, (h + 1) * HALF // LIST_ROWS)
-            nc.vector.tensor_copy(v_codes[h][:], tab_codes[:].indirect(tab_list[:, entries]))
+        def gather_v(c):
+            entries = slice(c * CHUNK // LIST_ROWS, (c + 1) * CHUNK // LIST_ROWS)
+            nc.vector.tensor_copy(v_codes[c][:], tab_codes[:].indirect(tab_list[:, entries]))
 
-        def quantise_wa(copies):
-            dealt = tile("wa_bf", [P, PACK * R], BF16)
-            codes = tile("wa_codes", [P, R], U32)
-            scales = tile("wa_scales", [P, R], U8)
+        def round_wa(u, copy):
             src = wa_raw[:].rearrange("p i (m u e) -> p u m i e", u=2, e=2)
-            dst = dealt[:].rearrange("p (u e m i) -> p u m i e", u=2, e=2, i=PACK)
-            for u in range(2):
-                copies[u](dst[:, u], src[:, u])
-            nc.vector.quantize_mx(codes[:].bitcast(FP8X4), scales[:], dealt[:])
-            return codes, scales
+            dst = wa_bf[:].rearrange("p (u e m i) -> p u m i e", u=2, e=2, i=PACK)
+            copy(dst[:, u], src[:, u])
 
-        def quantise_wb(copies):
-            dealt = tile("wb_bf", [P, PACK * R], BF16)
-            codes = tile("wb_codes", [P, R], U32)
-            scales = tile("wb_scales", [P, R], U8)
+        def round_wb(u, copy):
             src = wb_raw[:].rearrange("p i (m u e) -> p u m i e", u=2, e=2)
-            dst = dealt[:].rearrange("p (u e m i) -> p u m i e", u=2, e=2, i=PACK)
-            for u in range(2):
-                copies[u](dst[:, u], src[:, u])
-            nc.vector.quantize_mx(codes[:].bitcast(FP8X4), scales[:], dealt[:])
-            return codes, scales
+            dst = wb_bf[:].rearrange("p (u e m i) -> p u m i e", u=2, e=2, i=PACK)
+            copy(dst[:, u], src[:, u])
 
-        def words(t, j0, width):
-            return t[:, PACK * j0 : PACK * (j0 + width)]
+        def quantise(codes, scales, src):
+            nc.vector.quantize_mx(codes.bitcast(FP8X4), scales, src)
 
         def round_into_words(copy, dst, src, rows=slice(0, PACK)):
             copy(
@@ -189,128 +229,181 @@ def tile_list_htabg_glu_resP_kernel(
                 src.rearrange("p i (c e) -> p c i e", e=4)[:, :, rows, :],
             )
 
-        def quantise_x(c, slot=None):
-            x_bf = tile("x_bf%d" % c, [P, PACK * CHUNK], BF16)
-            x_codes[c] = tile(slot or "x_codes%d" % c, [P, CHUNK], U32)
+        def round_x(c, copy, rows=slice(0, PACK)):
+            k, at = divmod(c * CHUNK, J // len(picked))
+            round_into_words(copy, x_bf[c][:], picked[k][:, :, at : at + CHUNK], rows)
+
+        def round_x_block(b, copy):
+            c, at = divmod(b * BLOCK, CHUNK)
+            round_into_words(copy, x_bf[c][:, PACK * at : PACK * (at + BLOCK)], picked[0][:, :, b * BLOCK : (b + 1) * BLOCK])
+
+        def round_x_gpsimd(j0, width):
+            c, at = divmod(j0, CHUNK)
+            gpsimd_round(
+                x_bf[c][:, PACK * at : PACK * (at + width)].rearrange("p (j i) -> p j i", i=PACK),
+                picked[0][:, :, j0 : j0 + width].rearrange("p i j -> p j i"),
+            )
+
+        def quantise_x(c):
+            quantise(x_codes[c][:], x_scales[:, c * CHUNK : (c + 1) * CHUNK], x_bf[c][:])
+
+        def quantise_h(c):
             places = slice(c * CHUNK, (c + 1) * CHUNK)
-            round_into_words(nc.scalar.copy, x_bf[:], picked[:, :, places])
-            nc.vector.quantize_mx(x_codes[c][:].bitcast(FP8X4), x_scales[:, places], x_bf[:])
+            quantise(h_codes[:, places], h_scales[:, places], h_bf[c])
 
-        def quantise(codes, scales, src, j0, width):
-            nc.vector.quantize_mx(codes[:, j0 : j0 + width].bitcast(FP8X4), scales[:, j0 : j0 + width], words(src, j0, width))
-
-        def make_gate(b, slot=None):
-            places = slice(b * BLOCK, (b + 1) * BLOCK)
-            c, in_chunk = divmod(b * BLOCK, CHUNK)
-            ya = ps.tile([P, PACK, BLOCK], F32, name="ya", bufs=YA_BANKS)
+        def product(bank, codes, scales, fmt, moving_codes, moving_scales):
+            width = codes.shape[1] // PACK
             for t in range(PACK):
-                dealt_cols = slice(t * P, (t + 1) * P)
                 nc.tensor.matmul_mx(
-                    ya[:, t, :],
-                    lhsT=wa_codes[:, dealt_cols].bitcast(FP8X4),
-                    lhsT_scale=wa_scales[:, dealt_cols],
-                    rhs=x_codes[c][:, in_chunk : in_chunk + BLOCK].bitcast(FP8X4),
-                    rhs_scale=x_scales[:, places],
+                    bank[:, t, :],
+                    lhsT=codes[:, t * width : (t + 1) * width].bitcast(fmt),
+                    lhsT_scale=scales[:, t * P : (t + 1) * P],
+                    rhs=moving_codes.bitcast(FP8X4),
+                    rhs_scale=moving_scales,
                     start=True,
                     stop=True,
                 )
-            gate = tile(slot or "gate%d" % b, [P, BLOCK, PACK], F32)
-            nc.scalar.activation(gate[:], ya[:].rearrange("p t n -> p n t"), SILU)
-            gates[b] = gate
+
+        def make_gate(b):
+            c, at = divmod(b * BLOCK, CHUNK)
+            ya = ps.tile([P, PACK, BLOCK], F32, name="ya", bufs=YA_BANKS)
+            product(ya, wa_codes[:], wa_scales, FP8X4, x_codes[c][:, at : at + BLOCK], x_scales[:, b * BLOCK : (b + 1) * BLOCK])
+            nc.scalar.activation(gates[b][:], ya[:].rearrange("p t n -> p n t"), SILU)
 
         def make_h(b):
-            h, in_half = divmod(b * BLOCK, HALF)
+            c, at = divmod(b * BLOCK, CHUNK)
             yb = ps.tile([P, PACK, BLOCK], F32, name="yb", bufs=YB_BANKS)
-            for t in range(PACK):
-                dealt_cols = slice(t * P, (t + 1) * P)
-                nc.tensor.matmul_mx(
-                    yb[:, t, :],
-                    lhsT=wb_codes[:, dealt_cols].bitcast(FP8X4),
-                    lhsT_scale=wb_scales[:, dealt_cols],
-                    rhs=v_codes[h][:, in_half : in_half + BLOCK].bitcast(FP8X4),
-                    rhs_scale=v_scales[:, b * BLOCK : (b + 1) * BLOCK],
-                    start=True,
-                    stop=True,
-                )
+            product(yb, wb_codes[:], wb_scales, FP8X4, v_codes[c][:, at : at + BLOCK], v_scales[:, b * BLOCK : (b + 1) * BLOCK])
             nc.vector.tensor_tensor(
-                words(h_bf, b * BLOCK, BLOCK).rearrange("p (n t) -> p n t", t=PACK),
+                h_bf[c][:, PACK * at : PACK * (at + BLOCK)].rearrange("p (n t) -> p n t", t=PACK),
                 gates[b][:],
                 yb[:].rearrange("p t n -> p n t"),
                 MULT,
             )
 
-        def make_out(b, copy):
-            j0 = b * BLOCK
-            h, in_half = divmod(j0, HALF)
-            c, in_chunk = divmod(j0, CHUNK)
-            places = slice(j0, j0 + BLOCK)
+        def make_y(b):
+            places = slice(b * BLOCK, (b + 1) * BLOCK)
             y = ps.tile([P, PACK, BLOCK], F32, name="y", bufs=Y_BANKS)
-            for t in range(PACK):
-                nc.tensor.matmul_mx(
-                    y[:, t, :],
-                    lhsT=wd_codes[:, 2 * t * P : 2 * (t + 1) * P].bitcast(FP4X4),
-                    lhsT_scale=wd_dealt_scales[:, t * P : (t + 1) * P],
-                    rhs=h_codes[:, places].bitcast(FP8X4),
-                    rhs_scale=h_scales[:, places],
-                    start=True,
-                    stop=True,
-                )
-            sums = out_f32[c][:, :, in_chunk : in_chunk + BLOCK]
-            nc.vector.tensor_tensor(sums, y[:], res_half[h][:, :, in_half : in_half + BLOCK], ADD)
-            if c >= CHUNKS - 2:
-                nc.sync.dma_start(out_hbm[:, :, places], sums)
-            elif in_chunk + BLOCK == CHUNK:
-                nc.sync.dma_start(out_hbm[:, :, c * CHUNK : (c + 1) * CHUNK], out_f32[c][:])
-            round_into_words(copy, words(out_bf, j0, BLOCK), sums)
+            product(y, wd_codes[:], wd_dealt_scales, FP4X4, h_codes[:, places], h_scales[:, places])
+            return y
 
-        def quantise_out(j0, width, queue=nc.sync):
-            quantise(out_codes, out_scales, out_bf, j0, width)
-            queue.dma_start(out_words_hbm[:, j0 : j0 + width], out_codes[:, j0 : j0 + width].bitcast(I32))
+        def res_block(b):
+            h, in_half = divmod(b * BLOCK, HALF)
+            return res_half[h][:, :, in_half : in_half + BLOCK]
 
+        def sums_block(b):
+            c, at = divmod(b * BLOCK, CHUNK)
+            return sums[c][:, :, at : at + BLOCK]
+
+        def store_block(b):
+            nc.sync.dma_start(out_hbm[:, :, b * BLOCK : (b + 1) * BLOCK], sums_block(b))
+
+        def store_chunk(c):
+            nc.sync.dma_start(out_hbm[:, :, c * CHUNK : (c + 1) * CHUNK], sums[c])
+
+        def add_res(b):
+            nc.vector.tensor_tensor(sums_block(b), make_y(b)[:], res_block(b), ADD)
+
+        def copy_y(b):
+            y_banks[b] = tile("y_copy%d" % b, [P, PACK, BLOCK], F32)
+            nc.scalar.copy(y_banks[b][:], make_y(b)[:])
+
+        def add_res_gpsimd(b):
+            nc.gpsimd.tensor_tensor(sums_block(b), y_banks[b][:], res_block(b), ADD)
+
+        def round_out(b, copy):
+            c, at = divmod(b * BLOCK, CHUNK)
+            round_into_words(copy, out_bf[c][:, PACK * at : PACK * (at + BLOCK)], sums_block(b))
+
+        def quantise_out(c):
+            places = slice(c * CHUNK, (c + 1) * CHUNK)
+            quantise(out_codes[:, places], out_scales[:, places], out_bf[c][:])
+
+        def store_words(queue, first, last):
+            places = slice(first * CHUNK, (last + 1) * CHUNK)
+            queue.dma_start(out_words_hbm[:, places], out_codes[:, places].bitcast(I32))
+
+        on_scalar, on_vector = nc.scalar.copy, nc.vector.tensor_copy
+        deal_wd_codes(on_vector)
         for j0, width in FIRST_PIECES:
             gather_x(0, j0, width)
         gather_x(1, 0, J)
         gather_x(2, 0, J)
-        wa_codes, wa_scales = quantise_wa([nc.scalar.copy, nc.vector.tensor_copy])
         gather_x(3, 0, CHUNK)
         gather_x(3, CHUNK, CHUNK)
         gather_x(3, HALF, HALF)
+        round_x(0, on_scalar)
+        round_wa(0, on_scalar)
+        deal_wd_scales(on_vector)
+        round_wa(1, on_vector)
         quantise_x(0)
-        wb_codes, wb_scales = quantise_wb([nc.vector.tensor_copy, nc.vector.tensor_copy])
+        quantise(wa_codes[:], wa_scales[:], wa_bf[:])
+        round_x(1, on_scalar)
+        round_wb(0, on_vector)
+        round_wb(1, on_vector)
+        quantise_x(1)
+        quantise(wb_codes[:], wb_scales[:], wb_bf[:])
         make_gate(0)
         make_gate(1)
-        quantise_x(1, None)
+        round_x(2, on_scalar)
+        gather_v(0)
         make_gate(2)
         make_gate(3)
-        quantise_x(2, None)
-        gather_v(0)
         gather_v(1)
+        round_x(3, on_scalar)
         make_h(0)
-        quantise_x(3, None)
+        gather_v(2)
         make_h(1)
+        quantise_x(2)
+        quantise_h(0)
         make_gate(4)
         make_gate(5)
         make_h(2)
-        quantise(h_codes, h_scales, h_bf, 0, CHUNK)
+        make_h(3)
+        add_res(0)
+        store_block(0)
+        copy_y(1)
+        gather_v(3)
+        quantise_x(3)
+        quantise_h(1)
+        add_res_gpsimd(1)
+        store_block(1)
         make_gate(6)
         make_gate(7)
-        make_h(3)
-        make_out(0, nc.scalar.copy)
-        quantise(h_codes, h_scales, h_bf, CHUNK, CHUNK)
-        last = CHUNKS - 1
-        for c in range(2, CHUNKS):
-            make_out(2 * c - 3, nc.scalar.copy)
-            make_h(2 * c)
-            make_out(2 * c - 2, nc.scalar.copy)
-            make_h(2 * c + 1)
-            quantise_out((c - 2) * CHUNK, CHUNK)
-            quantise(h_codes, h_scales, h_bf, c * CHUNK, CHUNK)
-        make_out(2 * last - 1, nc.scalar.copy)
-        make_out(2 * last, nc.scalar.copy)
-        make_out(2 * last + 1, nc.vector.tensor_copy)
-        quantise_out((last - 1) * CHUNK, CHUNK)
-        quantise_out(last * CHUNK, CHUNK, nc.scalar)
-
+        make_h(4)
+        make_h(5)
+        add_res(2)
+        store_block(2)
+        copy_y(3)
+        round_out(0, on_scalar)
+        quantise_h(2)
+        add_res_gpsimd(3)
+        store_block(3)
+        round_out(1, on_scalar)
+        make_h(6)
+        round_out(2, on_scalar)
+        make_h(7)
+        add_res(4)
+        store_block(4)
+        round_out(3, on_scalar)
+        quantise_h(3)
+        quantise_out(0)
+        add_res(5)
+        store_block(5)
+        round_out(4, on_scalar)
+        quantise_out(1)
+        store_words(nc.sync, 0, 1)
+        add_res(6)
+        store_block(6)
+        round_out(5, on_scalar)
+        add_res(7)
+        store_block(7)
+        round_out(6, on_scalar)
+        quantise_out(2)
+        store_words(nc.sync, 2, 2)
+        round_out(7, on_vector)
+        quantise_out(3)
+        store_words(nc.scalar, 3, 3)
 
         for q in range(QUADRANTS):
             queue = nc.sync if q < QUADRANTS // 2 else nc.scalar

@@ -31,7 +31,7 @@ CHUNKS = J // CHUNK
 HALF = J // 2
 FIRST_PIECES = ((0, 256), (256, 256), (512, 512))
 YA_BANKS, YB_BANKS, Y_BANKS = 2, 3, 3
-PLACES = {"wa_raw": 0, "x_bf1": 0, "x_codes0": 8192, "x_bf2": 8192, "x_codes1": 10240, "x_bf3": 10240, "gate0": 12288, "v_codes2": 12288, "x_codes2": 13312, "gate2": 14336, "v_codes3": 14336, "x_codes3": 15360}
+PLACES = {"wa_raw": 0, "x_bf1": 0, "wb_bf": 8192, "x_bf2": 8192, "x_codes1": 12288, "x_bf3": 12288, "gate0": 14336, "v_codes2": 14336, "x_codes2": 15360, "gate1": 16384, "v_codes3": 16384, "yb_copy3": 18432, "x_codes3": 18432, "yb_copy5": 20480, "out_codes0": 20480, "yb_copy7": 22528, "out_codes1": 22528}
 
 def tile_list_htabg_glu_resP_kernel(
     tc, tab_words, tab_scales, xT, wgt2, wa, wb, wd_words, wd_scales, res, offs, offs2, out_0, out_1, out_2
@@ -165,7 +165,7 @@ def tile_list_htabg_glu_resP_kernel(
         x_scales = tile("x_scales", [P, J], U8)
         h_codes = tile("h_codes", [P, J], U32)
         h_scales = tile("h_scales", [P, J], U8)
-        out_codes = tile("out_codes", [P, J], U32)
+        out_codes = [tile("out_codes%d" % c, [P, CHUNK], U32) for c in range(CHUNKS)]
         wa_bf = tile("wa_bf", [P, PACK * R], BF16)
         wa_codes = tile("wa_codes", [P, R], U32)
         wa_scales = tile("wa_scales", [P, R], U8)
@@ -175,12 +175,18 @@ def tile_list_htabg_glu_resP_kernel(
         x_bf = [tile("x_bf%d" % c, [P, PACK * CHUNK], BF16) for c in range(CHUNKS)]
         x_codes = [tile("x_codes%d" % c, [P, CHUNK], U32) for c in range(CHUNKS)]
         out_bf = [tile("out_bf%d" % c, [P, PACK * CHUNK], BF16) for c in range(CHUNKS)]
-        gates = [tile("gate%d" % b, [P, BLOCK, PACK], F32) for b in range(blocks)]
-        shared = [tile("shared%d" % c, [P, PACK * CHUNK + 3 * BLOCK], F32) for c in range(CHUNKS)]
-        sums = [t[:, : PACK * CHUNK].rearrange("p (t j) -> p t j", t=PACK) for t in shared]
-        h_first = tile("h_first", [P, PACK * CHUNK], BF16)
-        h_bf = [h_first[:]] + [t[:, PACK * CHUNK - BLOCK :].bitcast(BF16) for t in shared[:2]] + [tile("h_last", [P, PACK * CHUNK], BF16)[:]]
+        sums = [tile("sums%d" % c, [P, PACK, CHUNK], F32)[:] for c in range(CHUNKS)]
+        words = PACK * CHUNK
+        lap = 32
+        h_chain = tile("h_chain", [P, 2 * lap + CHUNKS * words - (CHUNKS - 1) * lap], BF16)
+        h_at = [2 * lap + (CHUNKS - 1 - c) * (words - lap) for c in range(CHUNKS)]
+        h_bf = [h_chain[:, at : at + words] for at in h_at]
+        gates = {b: tile("gate%d" % b, [P, BLOCK, PACK], F32)[:] for b in (0, 1, 2, 4, 6, 7)}
+        for c in (1, 2):
+            at = h_at[c + 1] - c * lap
+            gates[2 * c + 1] = h_chain[:, at : at + words].bitcast(F32).rearrange("p (n t) -> p n t", t=PACK)
         y_banks = {}
+        ys = {}
 
         def gpsimd_round(dst, src):
             nc.gpsimd.tensor_scalar(dst, src, 1.0, 0.0, MULT, ADD)
@@ -268,24 +274,33 @@ def tile_list_htabg_glu_resP_kernel(
             c, at = divmod(b * BLOCK, CHUNK)
             ya = ps.tile([P, PACK, BLOCK], F32, name="ya", bufs=YA_BANKS)
             product(ya, wa_codes[:], wa_scales, FP8X4, x_codes[c][:, at : at + BLOCK], x_scales[:, b * BLOCK : (b + 1) * BLOCK])
-            nc.scalar.activation(gates[b][:], ya[:].rearrange("p t n -> p n t"), SILU)
+            nc.scalar.activation(gates[b], ya[:].rearrange("p t n -> p n t"), SILU)
 
-        def make_h(b):
+        def make_yb(b):
             c, at = divmod(b * BLOCK, CHUNK)
             yb = ps.tile([P, PACK, BLOCK], F32, name="yb", bufs=YB_BANKS)
             product(yb, wb_codes[:], wb_scales, FP8X4, v_codes[c][:, at : at + BLOCK], v_scales[:, b * BLOCK : (b + 1) * BLOCK])
-            nc.vector.tensor_tensor(
-                h_bf[c][:, PACK * at : PACK * (at + BLOCK)].rearrange("p (n t) -> p n t", t=PACK),
-                gates[b][:],
-                yb[:].rearrange("p t n -> p n t"),
-                MULT,
-            )
+            return yb[:].rearrange("p t n -> p n t")
+
+        def h_block(b):
+            c, at = divmod(b * BLOCK, CHUNK)
+            return h_bf[c][:, PACK * at : PACK * (at + BLOCK)].rearrange("p (n t) -> p n t", t=PACK)
+
+        def make_h(b):
+            nc.vector.tensor_tensor(h_block(b), gates[b], make_yb(b), MULT)
+
+        def copy_yb(b):
+            y_banks[b] = tile("yb_copy%d" % b, [P, BLOCK, PACK], F32)
+            nc.scalar.copy(y_banks[b][:], make_yb(b))
+
+        def make_h_gpsimd(b):
+            nc.gpsimd.tensor_tensor(h_block(b), gates[b], y_banks[b][:], MULT)
 
         def make_y(b):
             places = slice(b * BLOCK, (b + 1) * BLOCK)
             y = ps.tile([P, PACK, BLOCK], F32, name="y", bufs=Y_BANKS)
             product(y, wd_codes[:], wd_dealt_scales, FP4X4, h_codes[:, places], h_scales[:, places])
-            return y
+            ys[b] = y
 
         def res_block(b):
             h, in_half = divmod(b * BLOCK, HALF)
@@ -302,11 +317,11 @@ def tile_list_htabg_glu_resP_kernel(
             nc.sync.dma_start(out_hbm[:, :, c * CHUNK : (c + 1) * CHUNK], sums[c])
 
         def add_res(b):
-            nc.vector.tensor_tensor(sums_block(b), make_y(b)[:], res_block(b), ADD)
+            nc.vector.tensor_tensor(sums_block(b), ys[b][:], res_block(b), ADD)
 
         def copy_y(b):
             y_banks[b] = tile("y_copy%d" % b, [P, PACK, BLOCK], F32)
-            nc.scalar.copy(y_banks[b][:], make_y(b)[:])
+            nc.scalar.copy(y_banks[b][:], ys[b][:])
 
         def add_res_gpsimd(b):
             nc.gpsimd.tensor_tensor(sums_block(b), y_banks[b][:], res_block(b), ADD)
@@ -317,11 +332,10 @@ def tile_list_htabg_glu_resP_kernel(
 
         def quantise_out(c):
             places = slice(c * CHUNK, (c + 1) * CHUNK)
-            quantise(out_codes[:, places], out_scales[:, places], out_bf[c][:])
+            quantise(out_codes[c][:], out_scales[:, places], out_bf[c][:])
 
-        def store_words(queue, first, last):
-            places = slice(first * CHUNK, (last + 1) * CHUNK)
-            queue.dma_start(out_words_hbm[:, places], out_codes[:, places].bitcast(I32))
+        def store_words(queue, c):
+            queue.dma_start(out_words_hbm[:, c * CHUNK : (c + 1) * CHUNK], out_codes[c][:].bitcast(I32))
 
         on_scalar, on_vector = nc.scalar.copy, nc.vector.tensor_copy
         deal_wd_codes(on_vector)
@@ -345,54 +359,64 @@ def tile_list_htabg_glu_resP_kernel(
         quantise(wb_codes[:], wb_scales[:], wb_bf[:])
         make_gate(0)
         make_gate(1)
-        round_x(2, on_scalar)
+        round_x_gpsimd(2 * CHUNK, CHUNK)
         gather_v(0)
         make_gate(2)
         make_gate(3)
         gather_v(1)
-        round_x(3, on_scalar)
         make_h(0)
-        gather_v(2)
-        make_h(1)
         quantise_x(2)
-        quantise_h(0)
+        make_h(1)
+        copy_yb(3)
         make_gate(4)
         make_gate(5)
+        round_x(3, on_scalar)
+        gather_v(2)
+        quantise_h(0)
+        make_y(0)
+        make_h_gpsimd(3)
         make_h(2)
-        make_h(3)
+        copy_yb(5)
+        gather_v(3)
         add_res(0)
         store_block(0)
-        copy_y(1)
-        gather_v(3)
+        make_y(1)
         quantise_x(3)
         quantise_h(1)
-        add_res_gpsimd(1)
-        store_block(1)
+        make_y(2)
+        make_h_gpsimd(5)
         make_gate(6)
         make_gate(7)
+        copy_yb(7)
         make_h(4)
-        make_h(5)
+        add_res(1)
+        store_block(1)
+        round_out(0, on_scalar)
         add_res(2)
         store_block(2)
-        copy_y(3)
-        round_out(0, on_scalar)
-        quantise_h(2)
-        add_res_gpsimd(3)
-        store_block(3)
+        make_y(3)
         round_out(1, on_scalar)
+        quantise_h(2)
+        quantise_out(0)
+        store_words(nc.sync, 0)
+        make_y(4)
+        make_h_gpsimd(7)
         make_h(6)
         round_out(2, on_scalar)
-        make_h(7)
+        add_res(3)
+        store_block(3)
         add_res(4)
         store_block(4)
+        make_y(5)
         round_out(3, on_scalar)
         quantise_h(3)
-        quantise_out(0)
+        make_y(6)
+        make_y(7)
+        quantise_out(1)
+        store_words(nc.sync, 1)
+        round_out(4, on_scalar)
         add_res(5)
         store_block(5)
-        round_out(4, on_scalar)
-        quantise_out(1)
-        store_words(nc.sync, 0, 1)
         add_res(6)
         store_block(6)
         round_out(5, on_scalar)
@@ -400,10 +424,10 @@ def tile_list_htabg_glu_resP_kernel(
         store_block(7)
         round_out(6, on_scalar)
         quantise_out(2)
-        store_words(nc.sync, 2, 2)
+        store_words(nc.sync, 2)
         round_out(7, on_vector)
         quantise_out(3)
-        store_words(nc.scalar, 3, 3)
+        store_words(nc.scalar, 3)
 
         for q in range(QUADRANTS):
             queue = nc.sync if q < QUADRANTS // 2 else nc.scalar

@@ -31,7 +31,7 @@ CHUNKS = J // CHUNK
 HALF = J // 2
 FIRST_PIECES = ((0, 256), (256, 256), (512, 512))
 YA_BANKS, YB_BANKS, Y_BANKS = 2, 3, 3
-PLACES = {"wa_raw": 0, "x_bf1": 0, "wb_bf": 8192, "x_bf2": 8192, "x_codes1": 12288, "x_bf3": 12288, "gate0": 14336, "v_codes2": 14336, "x_codes2": 15360, "gate1": 16384, "v_codes3": 16384, "yb_copy3": 18432, "x_codes3": 18432, "yb_copy5": 20480, "out_codes0": 20480, "yb_copy7": 22528, "out_codes1": 22528}
+PLACES = {"wa_raw": 0, "x_bf1": 0, "wb_bf": 8192, "x_bf2": 8192, "gate0": 12288, "x_codes2": 12288, "x_bf3": 13312, "gate1": 15360, "v_codes2": 15360, "yb_copy3": 17408, "x_codes3": 17408, "v_codes3": 18432, "yb_copy5": 19456, "out_codes0": 19456}
 
 def tile_list_htabg_glu_resP_kernel(
     tc, tab_words, tab_scales, xT, wgt2, wa, wb, wd_words, wd_scales, res, offs, offs2, out_0, out_1, out_2
@@ -365,56 +365,55 @@ def tile_list_htabg_glu_resP_kernel(
         make_gate(3)
         gather_v(1)
         make_h(0)
-        quantise_x(2)
         make_h(1)
         copy_yb(3)
-        make_gate(4)
-        make_gate(5)
         round_x(3, on_scalar)
-        gather_v(2)
+        quantise_x(2)
         quantise_h(0)
         make_y(0)
         make_h_gpsimd(3)
         make_h(2)
+        gather_v(2)
+        make_gate(4)
+        make_gate(5)
+        make_y(1)
         copy_yb(5)
-        gather_v(3)
         add_res(0)
         store_block(0)
-        make_y(1)
-        quantise_x(3)
-        quantise_h(1)
-        make_y(2)
-        make_h_gpsimd(5)
-        make_gate(6)
-        make_gate(7)
-        copy_yb(7)
-        make_h(4)
         add_res(1)
         store_block(1)
+        quantise_h(1)
+        make_y(2)
+        make_y(3)
+        make_h_gpsimd(5)
+        quantise_x(3)
+        make_gate(6)
+        make_gate(7)
         round_out(0, on_scalar)
+        make_h(4)
+        gather_v(3)
+        round_out(1, on_scalar)
         add_res(2)
         store_block(2)
-        make_y(3)
-        round_out(1, on_scalar)
-        quantise_h(2)
-        quantise_out(0)
-        store_words(nc.sync, 0)
-        make_y(4)
-        make_h_gpsimd(7)
-        make_h(6)
-        round_out(2, on_scalar)
         add_res(3)
         store_block(3)
+        round_out(2, on_scalar)
+        quantise_h(2)
+        make_y(4)
+        quantise_out(0)
+        store_words(nc.sync, 0)
+        round_out(3, on_scalar)
+        make_h(6)
+        make_h(7)
+        make_y(5)
         add_res(4)
         store_block(4)
-        make_y(5)
-        round_out(3, on_scalar)
         quantise_h(3)
         make_y(6)
         make_y(7)
+        round_out(4, on_scalar)
         quantise_out(1)
         store_words(nc.sync, 1)
-        round_out(4, on_scalar)
         add_res(5)
         store_block(5)
         add_res(6)

@@ -31,7 +31,8 @@ CHUNKS = J // CHUNK
 HALF = J // 2
 FIRST_PIECES = ((0, 256), (256, 256), (512, 512))
 YA_BANKS, YB_BANKS, Y_BANKS = 2, 3, 3
-PLACES = {"wa_raw": 0, "x_bf1": 0, "wb_bf": 8192, "x_bf2": 8192, "gate0": 12288, "x_codes2": 12288, "x_bf3": 13312, "gate1": 15360, "v_codes2": 15360, "yb_copy3": 17408, "x_codes3": 17408, "v_codes3": 18432, "yb_copy5": 19456, "out_codes0": 19456}
+PLACES = {"wa_raw": 0, "x_bf1": 0, "wb_raw": 8192, "x_bf2": 8192, "x_bf3": 10240, "h_bf1": 10240, "gate0": 16384, "x_codes2": 16384, "x_codes3": 17408, "gate1": 18432, "v_codes2": 18432, "yb_copy3": 20480, "v_codes3": 20480, "yb_copy5": 22528, "out_codes0": 22528, "yb_copy7": 24576, "out_codes1": 24576, "res0": 26624, "gate3": 30720, "h_bf2": 29696, "res256": 32768, "gate5": 36864, "h_bf3": 35840}
+SPLIT = 32
 
 def tile_list_htabg_glu_resP_kernel(
     tc, tab_words, tab_scales, xT, wgt2, wa, wb, wd_words, wd_scales, res, offs, offs2, out_0, out_1, out_2
@@ -66,7 +67,7 @@ def tile_list_htabg_glu_resP_kernel(
         tab_codes = tile("tab_codes", [P, T], U32)
         wa_raw = tile("wa_raw", [P, PACK, R], F32)
         wb_raw = tile("wb_raw", [P, PACK, R], F32)
-        res_half = [tile("res%d" % h, [P, PACK, HALF], F32) for h in range(J // HALF)]
+        res_pieces = [tile("res%d" % j0, [P, PACK, width], F32) for j0, width in FIRST_PIECES]
 
         blocks = J // P
         wgt_rows = tile("wgt_rows", [P, P], F32)
@@ -103,8 +104,9 @@ def tile_list_htabg_glu_resP_kernel(
             for q in range(QUADRANTS):
                 nc.sync.dma_start(scale_rows(wd_raw_scales, q), hbm_scale_rows(wd_scales, q))
 
-        def load_res(h):
-            nc.sync.dma_start(res_half[h][:], res_hbm[:, :, h * HALF : (h + 1) * HALF])
+        def load_res(k):
+            j0, width = FIRST_PIECES[k]
+            nc.sync.dma_start(res_pieces[k][:], res_hbm[:, :, j0 : j0 + width])
 
         def gather_v_scales():
             nc.vector.tensor_copy(v_staged[:], tab_scale_tile[:].indirect(tab_list[:]))
@@ -142,6 +144,7 @@ def tile_list_htabg_glu_resP_kernel(
         load_tab()
         load_res(0)
         load_res(1)
+        load_res(2)
 
         wgt_turned = ps.tile([P, P], F32, name="y", bufs=Y_BANKS)
         nc.tensor.transpose(wgt_turned[:], wgt_rows[:], ident[:])
@@ -176,15 +179,8 @@ def tile_list_htabg_glu_resP_kernel(
         x_codes = [tile("x_codes%d" % c, [P, CHUNK], U32) for c in range(CHUNKS)]
         out_bf = [tile("out_bf%d" % c, [P, PACK * CHUNK], BF16) for c in range(CHUNKS)]
         sums = [tile("sums%d" % c, [P, PACK, CHUNK], F32)[:] for c in range(CHUNKS)]
-        words = PACK * CHUNK
-        lap = 32
-        h_chain = tile("h_chain", [P, 2 * lap + CHUNKS * words - (CHUNKS - 1) * lap], BF16)
-        h_at = [2 * lap + (CHUNKS - 1 - c) * (words - lap) for c in range(CHUNKS)]
-        h_bf = [h_chain[:, at : at + words] for at in h_at]
-        gates = {b: tile("gate%d" % b, [P, BLOCK, PACK], F32)[:] for b in (0, 1, 2, 4, 6, 7)}
-        for c in (1, 2):
-            at = h_at[c + 1] - c * lap
-            gates[2 * c + 1] = h_chain[:, at : at + words].bitcast(F32).rearrange("p (n t) -> p n t", t=PACK)
+        h_bf = [tile("h_bf%d" % c, [P, PACK * CHUNK], BF16)[:] for c in range(CHUNKS)]
+        gates = [tile("gate%d" % b, [P, BLOCK, PACK], F32)[:] for b in range(blocks)]
         y_banks = {}
         ys = {}
 
@@ -296,6 +292,12 @@ def tile_list_htabg_glu_resP_kernel(
         def make_h_gpsimd(b):
             nc.gpsimd.tensor_tensor(h_block(b), gates[b], y_banks[b][:], MULT)
 
+        def make_h_shared(b, split):
+            yb = make_yb(b)
+            y_banks[b] = tile("yb_copy%d" % b, [P, BLOCK - split, PACK], F32)
+            nc.scalar.copy(y_banks[b][:], yb[:, split:, :])
+            return yb
+
         def make_y(b):
             places = slice(b * BLOCK, (b + 1) * BLOCK)
             y = ps.tile([P, PACK, BLOCK], F32, name="y", bufs=Y_BANKS)
@@ -303,8 +305,9 @@ def tile_list_htabg_glu_resP_kernel(
             ys[b] = y
 
         def res_block(b):
-            h, in_half = divmod(b * BLOCK, HALF)
-            return res_half[h][:, :, in_half : in_half + BLOCK]
+            k = max(n for n, piece in enumerate(FIRST_PIECES) if piece[0] <= b * BLOCK)
+            at = b * BLOCK - FIRST_PIECES[k][0]
+            return res_pieces[k][:, :, at : at + BLOCK]
 
         def sums_block(b):
             c, at = divmod(b * BLOCK, CHUNK)
@@ -334,6 +337,10 @@ def tile_list_htabg_glu_resP_kernel(
             places = slice(c * CHUNK, (c + 1) * CHUNK)
             quantise(out_codes[c][:], out_scales[:, places], out_bf[c][:])
 
+        def quantise_out_block(b):
+            c, at = divmod(b * BLOCK, CHUNK)
+            quantise(out_codes[c][:, at : at + BLOCK], out_scales[:, b * BLOCK : (b + 1) * BLOCK], out_bf[c][:, PACK * at : PACK * (at + BLOCK)])
+
         def store_words(queue, c):
             queue.dma_start(out_words_hbm[:, c * CHUNK : (c + 1) * CHUNK], out_codes[c][:].bitcast(I32))
 
@@ -360,24 +367,27 @@ def tile_list_htabg_glu_resP_kernel(
         make_gate(0)
         make_gate(1)
         round_x_gpsimd(2 * CHUNK, CHUNK)
+        round_x_gpsimd(3 * CHUNK, BLOCK)
         gather_v(0)
         make_gate(2)
         make_gate(3)
+        round_x_block(7, on_scalar)
         gather_v(1)
         make_h(0)
         make_h(1)
         copy_yb(3)
-        round_x(3, on_scalar)
         quantise_x(2)
+        quantise_x(3)
         quantise_h(0)
         make_y(0)
         make_h_gpsimd(3)
-        make_h(2)
         gather_v(2)
+        make_h(2)
         make_gate(4)
         make_gate(5)
         make_y(1)
         copy_yb(5)
+        make_gate(6)
         add_res(0)
         store_block(0)
         add_res(1)
@@ -386,13 +396,12 @@ def tile_list_htabg_glu_resP_kernel(
         make_y(2)
         make_y(3)
         make_h_gpsimd(5)
-        quantise_x(3)
-        make_gate(6)
-        make_gate(7)
         round_out(0, on_scalar)
-        make_h(4)
-        gather_v(3)
         round_out(1, on_scalar)
+        make_gate(7)
+        gather_v(3)
+        make_h(4)
+        yb7 = make_h_shared(7, SPLIT)
         add_res(2)
         store_block(2)
         add_res(3)
@@ -400,11 +409,12 @@ def tile_list_htabg_glu_resP_kernel(
         round_out(2, on_scalar)
         quantise_h(2)
         make_y(4)
+        nc.gpsimd.tensor_tensor(h_block(7)[:, SPLIT:, :], gates[7][:, SPLIT:, :], y_banks[7][:], MULT)
         quantise_out(0)
         store_words(nc.sync, 0)
         round_out(3, on_scalar)
         make_h(6)
-        make_h(7)
+        nc.vector.tensor_tensor(h_block(7)[:, :SPLIT, :], gates[7][:, :SPLIT, :], yb7[:, :SPLIT, :], MULT)
         make_y(5)
         add_res(4)
         store_block(4)
@@ -425,7 +435,8 @@ def tile_list_htabg_glu_resP_kernel(
         quantise_out(2)
         store_words(nc.sync, 2)
         round_out(7, on_vector)
-        quantise_out(3)
+        quantise_out_block(6)
+        quantise_out_block(7)
         store_words(nc.scalar, 3)
 
         for q in range(QUADRANTS):

@@ -31,8 +31,8 @@ CHUNKS = J // CHUNK
 HALF = J // 2
 FIRST_PIECES = ((0, 256), (256, 256), (512, 512))
 YA_BANKS, YB_BANKS, Y_BANKS = 2, 3, 3
-PLACES = {"wa_raw": 0, "x_bf1": 0, "wb_raw": 8192, "x_bf2": 8192, "x_bf3": 10240, "h_bf1": 10240, "gate0": 16384, "x_codes2": 16384, "x_codes3": 17408, "gate1": 18432, "v_codes2": 18432, "yb_copy3": 20480, "v_codes3": 20480, "yb_copy5": 22528, "out_codes0": 22528, "yb_copy7": 24576, "out_codes1": 24576, "res0": 26624, "gate3": 30720, "h_bf2": 29696, "res256": 32768, "gate5": 36864, "h_bf3": 35840}
-SPLIT = 32
+PLACES = {"wa_raw": 0, "x_bf1": 0, "wb_raw": 8192, "x_bf2": 8192, "x_bf3": 10240, "h_bf1": 10240, "gate0": 16384, "x_codes2": 16384, "x_codes3": 17408, "gate1": 18432, "v_codes2": 18432, "yb_copy3": 20480, "v_codes3": 20480, "yb_copy5": 24576, "out_codes0": 24576, "yb_copy7": 28672, "out_codes1": 28672, "res0": 32768, "gate3": 36864, "h_bf2": 35840, "res256": 40960, "gate5": 45056, "h_bf3": 44032}
+SPLIT = 48
 
 def tile_list_htabg_glu_resP_kernel(
     tc, tab_words, tab_scales, xT, wgt2, wa, wb, wd_words, wd_scales, res, offs, offs2, out_0, out_1, out_2
@@ -168,7 +168,13 @@ def tile_list_htabg_glu_resP_kernel(
         x_scales = tile("x_scales", [P, J], U8)
         h_codes = tile("h_codes", [P, J], U32)
         h_scales = tile("h_scales", [P, J], U8)
-        out_codes = [tile("out_codes%d" % c, [P, CHUNK], U32) for c in range(CHUNKS)]
+        code_tiles = [(0, tile("out_codes0", [P, BLOCK], U32)), (BLOCK, tile("out_codes1", [P, HALF - BLOCK], U32))]
+        code_tiles = code_tiles + [(c * CHUNK, tile("out_codes%d" % c, [P, CHUNK], U32)) for c in (2, 3)]
+
+        def out_codes(j0, width):
+            first, t = [entry for entry in code_tiles if entry[0] <= j0][-1]
+            return t[:, j0 - first : j0 - first + width]
+
         wa_bf = tile("wa_bf", [P, PACK * R], BF16)
         wa_codes = tile("wa_codes", [P, R], U32)
         wa_scales = tile("wa_scales", [P, R], U8)
@@ -180,7 +186,13 @@ def tile_list_htabg_glu_resP_kernel(
         out_bf = [tile("out_bf%d" % c, [P, PACK * CHUNK], BF16) for c in range(CHUNKS)]
         sums = [tile("sums%d" % c, [P, PACK, CHUNK], F32)[:] for c in range(CHUNKS)]
         h_bf = [tile("h_bf%d" % c, [P, PACK * CHUNK], BF16)[:] for c in range(CHUNKS)]
-        gates = [tile("gate%d" % b, [P, BLOCK, PACK], F32)[:] for b in range(blocks)]
+        gates = {b: tile("gate%d" % b, [P, BLOCK, PACK], F32)[:] for b in (0, 1, 6, 7)}
+        gate_pairs = {c: tile("gate%d" % (2 * c + 1), [P, CHUNK, PACK], F32) for c in (1, 2)}
+        for c in (1, 2):
+            gates[2 * c] = gate_pairs[c][:, :BLOCK, :]
+            gates[2 * c + 1] = gate_pairs[c][:, BLOCK:, :]
+        OWN = 96
+        shared_banks = {}
         y_banks = {}
         ys = {}
 
@@ -286,11 +298,15 @@ def tile_list_htabg_glu_resP_kernel(
             nc.vector.tensor_tensor(h_block(b), gates[b], make_yb(b), MULT)
 
         def copy_yb(b):
-            y_banks[b] = tile("yb_copy%d" % b, [P, BLOCK, PACK], F32)
-            nc.scalar.copy(y_banks[b][:], make_yb(b))
+            y_banks[b] = tile("yb_copy%d" % b, [P, CHUNK - OWN, PACK], F32)
+            nc.scalar.copy(y_banks[b][:, BLOCK - OWN :, :], make_yb(b))
+            shared_banks[b - 1] = make_yb(b - 1)
+            nc.scalar.copy(y_banks[b][:, : BLOCK - OWN, :], shared_banks[b - 1][:, OWN:, :])
 
         def make_h_gpsimd(b):
-            nc.gpsimd.tensor_tensor(h_block(b), gates[b], y_banks[b][:], MULT)
+            c = b // 2
+            out = h_bf[c][:, PACK * OWN :].rearrange("p (n t) -> p n t", t=PACK)
+            nc.gpsimd.tensor_tensor(out, gate_pairs[c][:, OWN:, :], y_banks[b][:], MULT)
 
         def make_h_shared(b, split):
             yb = make_yb(b)
@@ -335,25 +351,27 @@ def tile_list_htabg_glu_resP_kernel(
 
         def quantise_out(c):
             places = slice(c * CHUNK, (c + 1) * CHUNK)
-            quantise(out_codes[c][:], out_scales[:, places], out_bf[c][:])
+            quantise(out_codes(c * CHUNK, CHUNK), out_scales[:, places], out_bf[c][:])
 
         def quantise_out_block(b):
             c, at = divmod(b * BLOCK, CHUNK)
-            quantise(out_codes[c][:, at : at + BLOCK], out_scales[:, b * BLOCK : (b + 1) * BLOCK], out_bf[c][:, PACK * at : PACK * (at + BLOCK)])
+            quantise(out_codes(b * BLOCK, BLOCK), out_scales[:, b * BLOCK : (b + 1) * BLOCK], out_bf[c][:, PACK * at : PACK * (at + BLOCK)])
 
         def store_words(queue, c):
-            queue.dma_start(out_words_hbm[:, c * CHUNK : (c + 1) * CHUNK], out_codes[c][:].bitcast(I32))
+            first, t = code_tiles[c]
+            queue.dma_start(out_words_hbm[:, first : first + t.shape[1]], t[:].bitcast(I32))
 
         on_scalar, on_vector = nc.scalar.copy, nc.vector.tensor_copy
         deal_wd_codes(on_vector)
         for j0, width in FIRST_PIECES:
             gather_x(0, j0, width)
         gather_x(1, 0, J)
+        round_x(0, on_scalar, slice(0, 2))
         gather_x(2, 0, J)
         gather_x(3, 0, CHUNK)
         gather_x(3, CHUNK, CHUNK)
         gather_x(3, HALF, HALF)
-        round_x(0, on_scalar)
+        round_x(0, on_scalar, slice(2, PACK))
         round_wa(0, on_scalar)
         deal_wd_scales(on_vector)
         round_wa(1, on_vector)
@@ -382,7 +400,7 @@ def tile_list_htabg_glu_resP_kernel(
         make_y(0)
         make_h_gpsimd(3)
         gather_v(2)
-        make_h(2)
+        nc.vector.tensor_tensor(h_block(2)[:, :OWN, :], gates[2][:, :OWN, :], shared_banks[2][:, :OWN, :], MULT)
         make_gate(4)
         make_gate(5)
         make_y(1)
@@ -397,11 +415,11 @@ def tile_list_htabg_glu_resP_kernel(
         make_y(3)
         make_h_gpsimd(5)
         round_out(0, on_scalar)
-        round_out(1, on_scalar)
         make_gate(7)
         gather_v(3)
-        make_h(4)
+        nc.vector.tensor_tensor(h_block(4)[:, :OWN, :], gates[4][:, :OWN, :], shared_banks[4][:, :OWN, :], MULT)
         yb7 = make_h_shared(7, SPLIT)
+        round_out(1, on_scalar)
         add_res(2)
         store_block(2)
         add_res(3)
@@ -410,7 +428,7 @@ def tile_list_htabg_glu_resP_kernel(
         quantise_h(2)
         make_y(4)
         nc.gpsimd.tensor_tensor(h_block(7)[:, SPLIT:, :], gates[7][:, SPLIT:, :], y_banks[7][:], MULT)
-        quantise_out(0)
+        quantise_out_block(0)
         store_words(nc.sync, 0)
         round_out(3, on_scalar)
         make_h(6)
@@ -422,6 +440,7 @@ def tile_list_htabg_glu_resP_kernel(
         make_y(6)
         make_y(7)
         round_out(4, on_scalar)
+        quantise_out_block(1)
         quantise_out(1)
         store_words(nc.sync, 1)
         add_res(5)

@@ -18,6 +18,8 @@ FP4X4 = mybir.dt.float4_e2m1fn_x4
 MULT = mybir.AluOpType.mult
 ADD = mybir.AluOpType.add
 SILU = mybir.ActivationFunctionType.Silu
+ITEM_BYTES = {"f32": 4, "bf16": 2, "u32": 4, "u8": 1}
+DTYPES = {"f32": F32, "bf16": BF16, "u32": U32, "u8": U8}
 
 P = 128
 PACK = 4
@@ -29,25 +31,39 @@ BLOCK = BANK // PACK
 CHUNK = 256
 CHUNKS = J // CHUNK
 HALF = J // 2
-FIRST_PIECES = ((0, 256), (256, 256), (512, 512))
-YA_BANKS, YB_BANKS, Y_BANKS = 2, 3, 3
-PLACES = {"wa_raw": 0, "x_bf1": 0, "wb_raw": 8192, "x_bf2": 8192, "x_bf3": 10240, "h_bf1": 10240, "gate0": 16384, "x_codes2": 16384, "x_codes3": 17408, "gate1": 18432, "v_codes2": 18432, "yb_copy3": 20480, "v_codes3": 20480, "yb_copy5": 24576, "out_codes0": 24576, "yb_copy7": 28672, "out_codes1": 28672, "res0": 32768, "gate3": 36864, "h_bf2": 35840, "res256": 40960, "gate5": 45056, "h_bf3": 44032}
-SPLIT = 48
+WGT_PIECES = ((0, 256), (256, 256), (512, 512))
+RES_PIECES = ((0, 256), (256, 256), (512, 512))
+RES_PLACES = (("x_rows2", 0), ("x_rows2", 4096), ("x_rows3", 0))
+FIRST_SHARE, SECOND_SHARE = 176, 192
+WA_SCALAR, WB_SCALAR = 64, 48
+
 
 def tile_list_htabg_glu_resP_kernel(
     tc, tab_words, tab_scales, xT, wgt2, wa, wb, wd_words, wd_scales, res, offs, offs2, out_0, out_1, out_2
 ):
     nc = tc.nc
     with ExitStack() as ctx:
+        lists = ctx.enter_context(tc.tile_pool(name="lists", bufs=1))
         sb = ctx.enter_context(tc.tile_pool(name="sb", bufs=1))
-        placed = ctx.enter_context(tc.tile_pool(name="placed", bufs=1))
         ps = ctx.enter_context(tc.psum_pool(name="ps", bufs=1))
+        spans = {"end": (0, 0)}
 
-        def tile(name, shape, dtype):
-            at = PLACES.get(name)
-            if at is None:
-                return sb.tile(shape, dtype, name=name, align_bytes=64)
-            return placed.tile(shape, dtype, name=name, align_bytes=64, offset=at)
+        def tile(name, shape, kind, over=None, at=0, room=0):
+            size = ITEM_BYTES[kind]
+            for extent in shape[1:]:
+                size = size * extent
+            size = max(size, room)
+            if over is None:
+                start = spans["end"][0]
+                spans["end"] = (start + (size + 63) // 64 * 64, 0)
+            else:
+                start = spans[over][0] + at
+                assert at + size <= spans[over][1]
+            spans[name] = (start, size)
+            return sb.tile(shape, DTYPES[kind], name=name, align_bytes=64, offset=start)
+
+        def bank_tile(name, bank, shape=(P, PACK, BLOCK)):
+            return ps.tile(list(shape), F32, name=name, offset=bank * BANK * 4)
 
         def scale_rows(scale_tile, q):
             return scale_tile[32 * q : 32 * q + 4, :].bitcast(I32)
@@ -55,184 +71,128 @@ def tile_list_htabg_glu_resP_kernel(
         def hbm_scale_rows(scales, q):
             return scales[0, 4 * q : 4 * q + 4, :].bitcast(I32)
 
-        tab_list = tile("tab_list", [P, J // LIST_ROWS], U16)
-        head_lists = tile("head_lists", [P, J // LIST_ROWS], U16)
-        tab_scale_tile = tile("tab_scale_tile", [P, T], U8)
-        v_staged = tile("v_staged", [P, J], U8)
-        v_scales = tile("v_scales", [P, J], U8)
-        wd_raw_scales = tile("wd_raw_scales", [P, N], U8)
-        wd_raw_codes = tile("wd_raw_codes", [P, 2 * N], U8)
-        x_rows = [tile("x_rows%d" % i, [P, T], F32) for i in range(PACK)]
-        wgt = tile("wgt", [P, J], F32)
-        tab_codes = tile("tab_codes", [P, T], U32)
-        wa_raw = tile("wa_raw", [P, PACK, R], F32)
-        wb_raw = tile("wb_raw", [P, PACK, R], F32)
-        res_pieces = [tile("res%d" % j0, [P, PACK, width], F32) for j0, width in FIRST_PIECES]
-
+        tab_list = lists.tile([P, J // LIST_ROWS], U16, name="tab_list")
+        head_lists = lists.tile([P, J // LIST_ROWS], U16, name="head_lists")
+        tab_scale_tile = tile("tab_scale_tile", [P, T], "u8", room=PACK * R * 4)
+        v_staged = tile("v_staged", [P, J], "u8")
+        v_scales = tile("v_scales", [P, J], "u8")
+        x_rows = [tile("x_rows%d" % i, [P, T], "f32") for i in range(PACK)]
+        wgt = tile("wgt", [P, J], "f32")
+        tab_codes = tile("tab_codes", [P, T], "u32")
+        wa_raw = tile("wa_raw", [P, PACK, R], "f32")
+        wb_raw = tile("wb_raw", [P, PACK, R], "f32", "tab_scale_tile")
+        wd_raw_scales = tile("wd_raw_scales", [P, N], "u8", "x_rows0", 2048, room=2048)
+        wd_raw_codes = tile("wd_raw_codes", [P, 2 * N], "u8", "x_rows0", room=2048)
+        res_pieces = [tile("res%d" % j0, [P, PACK, width], "f32", over, at) for (j0, width), (over, at) in zip(RES_PIECES, RES_PLACES)]
         blocks = J // P
-        wgt_rows = tile("wgt_rows", [P, P], F32)
-        ident = tile("ident", [P, P], F32)
-        make_identity(nc, ident[:])
-        nc.vector.memset(wd_raw_scales[:].bitcast(I32), 0)
-        nc.vector.memset(wgt_rows[HEADS * blocks :, :], 0.0)
+        wgt_rows = tile("wgt_rows", [P, P], "f32")
+        ident = tile("ident", [P, P], "f32")
+        warm = tile("warm", [P, 1], "f32")
         staged = P - SCALE_ROWS
-        nc.vector.memset(tab_scale_tile[:staged, :].bitcast(I32), 0)
-        nc.vector.memset(v_scales[:].bitcast(I32), 0)
-        warm = tile("warm", [P, 1], F32)
-        nc.scalar.activation(warm[:], ident[:, 0:1], SILU)
 
         x_hbm = xT.rearrange("(p i) t -> p i t", i=PACK)
         res_hbm = res.rearrange("(p t) j -> p t j", t=PACK)
-        wb_hbm = wb.rearrange("(p i) r -> p i r", i=PACK)
+        out_hbm = out_0.rearrange("(p t) j -> p t j", t=PACK)
+        out_words_hbm = out_1[0].rearrange("p j i -> p (j i)").bitcast(I32)
 
         def load_x(i):
             nc.sync.dma_start(x_rows[i][:], x_hbm[:, i, :])
 
-        def load_wa():
-            nc.sync.dma_start(wa_raw[:], wa.rearrange("(p i) r -> p i r", i=PACK))
+        def load_weight(raw, w):
+            nc.sync.dma_start(raw[:], w.rearrange("(p i) r -> p i r", i=PACK))
 
-        def load_wb():
-            nc.sync.dma_start(wb_raw[:], wb_hbm)
+        def load_res(k):
+            j0, width = RES_PIECES[k]
+            nc.sync.dma_start(res_pieces[k][:], res_hbm[:, :, j0 : j0 + width])
 
         def load_tab():
             nc.sync.dma_start(tab_codes[:].bitcast(I32), tab_words[0].rearrange("p t i -> p (t i)").bitcast(I32))
 
-        def load_wd_codes():
-            nc.sync.dma_start(wd_raw_codes[:].bitcast(I32), wd_words[0].bitcast(I32))
+        def load_wd_codes(queue):
+            queue.dma_start(wd_raw_codes[:].bitcast(I32), wd_words[0].bitcast(I32))
 
-        def load_wd_scales():
+        def load_wd_scales(queue):
             for q in range(QUADRANTS):
-                nc.sync.dma_start(scale_rows(wd_raw_scales, q), hbm_scale_rows(wd_scales, q))
+                queue.dma_start(scale_rows(wd_raw_scales, q), hbm_scale_rows(wd_scales, q))
 
-        def load_res(k):
-            j0, width = FIRST_PIECES[k]
-            nc.sync.dma_start(res_pieces[k][:], res_hbm[:, :, j0 : j0 + width])
-
-        def gather_v_scales():
-            nc.vector.tensor_copy(v_staged[:], tab_scale_tile[:].indirect(tab_list[:]))
+        def load_wgt(queue):
+            queue.dma_start(wgt_rows[: HEADS * blocks, :], wgt2.rearrange("(g q) (b j) -> q g b j", q=LIST_ROWS, j=P)[0])
 
         def carry_v_scales():
             for q in range(QUADRANTS):
                 nc.sync.dma_start(scale_rows(v_scales, q), v_staged[staged + 4 * q : staged + 4 * q + 4, :].bitcast(I32))
 
-        def load_tab_list():
-            nc.sync.dma_start(tab_list[:], offs)
+        def spread_wgt():
+            wgt_turned = bank_tile("wgt_turned", 0, [P, P])
+            nc.tensor.transpose(wgt_turned[:], wgt_rows[:], ident[:])
+            by_block = wgt_turned[:, : HEADS * blocks].rearrange("p (g b) -> p b g", b=blocks)
+            banks = []
+            for j0, width in WGT_PIECES:
+                shape = [P, width // P, HEADS, LIST_ROWS]
+                repeated = tile("repeated%d" % j0, shape, "f32")
+                nc.scalar.copy(repeated[:], by_block[:, j0 // P : (j0 + width) // P, :].unsqueeze(3).to_broadcast(shape))
+                bank = bank_tile("wgt_bank%d" % j0, 1 + len(banks), [P, width // P, P])
+                for b in range(width // P):
+                    nc.tensor.transpose(bank[:, b, :], repeated[:, b].rearrange("p g q -> p (g q)"), ident[:])
+                banks.append(bank)
+                if len(banks) > 1:
+                    k0, kw = WGT_PIECES[len(banks) - 2]
+                    nc.scalar.copy(wgt[:, k0 : k0 + kw], banks[-2][:].rearrange("p b j -> p (b j)"))
+            k0, kw = WGT_PIECES[-1]
+            nc.scalar.copy(wgt[:, k0 : k0 + kw], banks[-1][:].rearrange("p b j -> p (b j)"))
 
-        def load_tab_scales():
-            nc.sync.dma_start(tab_scale_tile[staged:, :].bitcast(I32), tab_scales[0].bitcast(I32))
+        on_scalar, on_vector = nc.scalar.copy, nc.vector.tensor_copy
 
-        def load_wgt():
-            nc.sync.dma_start(wgt_rows[: HEADS * blocks, :], wgt2.rearrange("(g q) (b j) -> q g b j", q=LIST_ROWS, j=P)[0])
-
-        def load_head_lists():
-            nc.sync.dma_start(head_lists[:], offs2)
-
-        load_tab_list()
-        load_tab_scales()
-        load_wgt()
-        load_wd_codes()
-        load_x(0)
-        load_head_lists()
-        load_wd_scales()
-        load_x(1)
-        load_x(2)
-        load_x(3)
-        gather_v_scales()
-        carry_v_scales()
-        load_wa()
-        load_wb()
-        load_tab()
-        load_res(0)
-        load_res(1)
-        load_res(2)
-
-        wgt_turned = ps.tile([P, P], F32, name="y", bufs=Y_BANKS)
-        nc.tensor.transpose(wgt_turned[:], wgt_rows[:], ident[:])
-        by_block = wgt_turned[:, : HEADS * blocks].rearrange("p (g b) -> p b g", b=blocks)
-        for j0, width in FIRST_PIECES:
-            shape = [P, width // P, HEADS, LIST_ROWS]
-            repeated = tile("repeated%d" % j0, shape, F32)
-            nc.scalar.copy(repeated[:], by_block[:, j0 // P : (j0 + width) // P, :].unsqueeze(3).to_broadcast(shape))
-            wgt_bank = ps.tile([P, width // P, P], F32, name="yb", bufs=YB_BANKS)
-            for b in range(width // P):
-                nc.tensor.transpose(wgt_bank[:, b, :], repeated[:, b].rearrange("p g q -> p (g q)"), ident[:])
-            nc.scalar.copy(wgt[:, j0 : j0 + width], wgt_bank[:].rearrange("p b j -> p (b j)"))
-
-        wd_codes = tile("wd_codes", [P, 2 * N], U8)
-        wd_dealt_scales = tile("wd_dealt_scales", [P, N], U8)
-        picked = [tile("picked%d" % c, [P, PACK, J // 1], F32) for c in range(1)]
-        v_codes = [tile("v_codes%d" % c, [P, CHUNK], U32) for c in range(CHUNKS)]
-        out_hbm = out_0.rearrange("(p t) j -> p t j", t=PACK)
-        out_words_hbm = out_1[0].rearrange("p j i -> p (j i)").bitcast(I32)
-        out_scales = tile("out_scales", [P, J], U8)
-        x_scales = tile("x_scales", [P, J], U8)
-        h_codes = tile("h_codes", [P, J], U32)
-        h_scales = tile("h_scales", [P, J], U8)
-        code_tiles = [(0, tile("out_codes0", [P, BLOCK], U32)), (BLOCK, tile("out_codes1", [P, HALF - BLOCK], U32))]
-        code_tiles = code_tiles + [(c * CHUNK, tile("out_codes%d" % c, [P, CHUNK], U32)) for c in (2, 3)]
-
-        def out_codes(j0, width):
-            first, t = [entry for entry in code_tiles if entry[0] <= j0][-1]
-            return t[:, j0 - first : j0 - first + width]
-
-        wa_bf = tile("wa_bf", [P, PACK * R], BF16)
-        wa_codes = tile("wa_codes", [P, R], U32)
-        wa_scales = tile("wa_scales", [P, R], U8)
-        wb_bf = tile("wb_bf", [P, PACK * R], BF16)
-        wb_codes = tile("wb_codes", [P, R], U32)
-        wb_scales = tile("wb_scales", [P, R], U8)
-        x_bf = [tile("x_bf%d" % c, [P, PACK * CHUNK], BF16) for c in range(CHUNKS)]
-        x_codes = [tile("x_codes%d" % c, [P, CHUNK], U32) for c in range(CHUNKS)]
-        out_bf = [tile("out_bf%d" % c, [P, PACK * CHUNK], BF16) for c in range(CHUNKS)]
-        sums = [tile("sums%d" % c, [P, PACK, CHUNK], F32)[:] for c in range(CHUNKS)]
-        h_bf = [tile("h_bf%d" % c, [P, PACK * CHUNK], BF16)[:] for c in range(CHUNKS)]
-        gates = {b: tile("gate%d" % b, [P, BLOCK, PACK], F32)[:] for b in (0, 1, 6, 7)}
-        gate_pairs = {c: tile("gate%d" % (2 * c + 1), [P, CHUNK, PACK], F32) for c in (1, 2)}
-        for c in (1, 2):
-            gates[2 * c] = gate_pairs[c][:, :BLOCK, :]
-            gates[2 * c + 1] = gate_pairs[c][:, BLOCK:, :]
-        OWN = 96
-        shared_banks = {}
-        y_banks = {}
-        ys = {}
-
-        def gpsimd_round(dst, src):
+        def on_gpsimd(dst, src):
             nc.gpsimd.tensor_scalar(dst, src, 1.0, 0.0, MULT, ADD)
 
-        def deal_wd_codes(copy):
+        wd_dealt = {}
+        picked = tile("picked", [P, PACK, J], "f32")
+        out_scales = tile("out_scales", [P, J], "u8")
+        x_scales = {}
+        h_scales = tile("h_scales", [P, J], "u8")
+        wa_bf = tile("wa_bf", [P, PACK * R], "bf16")
+        wa_codes = tile("wa_codes", [P, R], "u32")
+        wa_scales = tile("wa_scales", [P, R], "u8")
+        wb_bf = tile("wb_bf", [P, PACK * R], "bf16")
+        wb_codes = tile("wb_codes", [P, R], "u32")
+        wb_scales = tile("wb_scales", [P, R], "u8")
+        sums = [tile("sums%d" % c, [P, PACK, CHUNK], "f32") for c in range(CHUNKS)]
+        out_bf = tile("out_bf", [P, PACK * J], "bf16")
+        h_codes = {}
+        x_bf, x_codes, v_codes, h_bf, gates, yb_copies, out_codes, yb_banks, y_banks = {}, {}, {}, {}, {}, {}, {}, {}, {}
+
+        def deal_wd_codes(copy, over=None, at=0):
+            wd_dealt["codes"] = tile("wd_codes", [P, 2 * N], "u8", over, at)
             copy(
-                wd_codes[:].bitcast(U16).rearrange("p (t m) -> p t m", t=PACK),
+                wd_dealt["codes"][:].bitcast(U16).rearrange("p (t m) -> p t m", t=PACK),
                 wd_raw_codes[:].bitcast(U16).rearrange("p (m t) -> p t m", t=PACK),
             )
 
-        def deal_wd_scales(copy):
+        def deal_wd_scales(copy, over=None, at=0):
+            wd_dealt["scales"] = tile("wd_dealt_scales", [P, N], "u8", over, at)
             copy(
-                wd_dealt_scales[:].rearrange("p (t m) -> p t m", t=PACK),
+                wd_dealt["scales"][:].rearrange("p (t m) -> p t m", t=PACK),
                 wd_raw_scales[:].rearrange("p (m t) -> p t m", t=PACK),
             )
 
         def gather_x(i, j0, width):
-            c, at = divmod(j0, J // len(picked))
             nc.vector.tensor_tensor(
-                picked[c][:, i, at : at + width],
+                picked[:, i, j0 : j0 + width],
                 x_rows[i][:].indirect(head_lists[:, j0 // LIST_ROWS : (j0 + width) // LIST_ROWS]),
                 wgt[:, j0 : j0 + width],
                 MULT,
             )
 
-        def gather_v(c):
+        def gather_v(c, over=None, at=0):
+            v_codes[c] = tile("v_codes%d" % c, [P, CHUNK], "u32", over, at)
             entries = slice(c * CHUNK // LIST_ROWS, (c + 1) * CHUNK // LIST_ROWS)
             nc.vector.tensor_copy(v_codes[c][:], tab_codes[:].indirect(tab_list[:, entries]))
 
-        def round_wa(u, copy):
-            src = wa_raw[:].rearrange("p i (m u e) -> p u m i e", u=2, e=2)
-            dst = wa_bf[:].rearrange("p (u e m i) -> p u m i e", u=2, e=2, i=PACK)
-            copy(dst[:, u], src[:, u])
-
-        def round_wb(u, copy):
-            src = wb_raw[:].rearrange("p i (m u e) -> p u m i e", u=2, e=2)
-            dst = wb_bf[:].rearrange("p (u e m i) -> p u m i e", u=2, e=2, i=PACK)
-            copy(dst[:, u], src[:, u])
+        def round_weight(copy, bf, raw, m0, m1):
+            src = raw[:].rearrange("p i (m t) -> p m i t", t=PACK)[:, m0:m1]
+            dst = bf[:].rearrange("p (t m i) -> p m i t", t=PACK, i=PACK)[:, m0:m1]
+            copy(dst, src)
 
         def quantise(codes, scales, src):
             nc.vector.quantize_mx(codes.bitcast(FP8X4), scales, src)
@@ -243,33 +203,39 @@ def tile_list_htabg_glu_resP_kernel(
                 src.rearrange("p i (c e) -> p c i e", e=4)[:, :, rows, :],
             )
 
-        def round_x(c, copy, rows=slice(0, PACK)):
-            k, at = divmod(c * CHUNK, J // len(picked))
-            round_into_words(copy, x_bf[c][:], picked[k][:, :, at : at + CHUNK], rows)
+        def new_x_bf(c, over=None, at=0):
+            x_bf[c] = tile("x_bf%d" % c, [P, PACK * CHUNK], "bf16", over, at)
 
-        def round_x_block(b, copy):
-            c, at = divmod(b * BLOCK, CHUNK)
-            round_into_words(copy, x_bf[c][:, PACK * at : PACK * (at + BLOCK)], picked[0][:, :, b * BLOCK : (b + 1) * BLOCK])
+        def round_x(c, copy, rows=slice(0, PACK), first=0, width=CHUNK):
+            j0 = c * CHUNK + first
+            round_into_words(copy, x_bf[c][:, PACK * first : PACK * (first + width)], picked[:, :, j0 : j0 + width], rows)
 
-        def round_x_gpsimd(j0, width):
-            c, at = divmod(j0, CHUNK)
-            gpsimd_round(
-                x_bf[c][:, PACK * at : PACK * (at + width)].rearrange("p (j i) -> p j i", i=PACK),
-                picked[0][:, :, j0 : j0 + width].rearrange("p i j -> p j i"),
+        def round_x_gpsimd(c, first=0, width=CHUNK):
+            j0 = c * CHUNK + first
+            on_gpsimd(
+                x_bf[c][:, PACK * first : PACK * (first + width)].rearrange("p (j i) -> p j i", i=PACK),
+                picked[:, :, j0 : j0 + width].rearrange("p i j -> p j i"),
             )
 
-        def quantise_x(c):
-            quantise(x_codes[c][:], x_scales[:, c * CHUNK : (c + 1) * CHUNK], x_bf[c][:])
+        def quantise_x(c, over=None, at=0):
+            x_codes[c] = tile("x_codes%d" % c, [P, CHUNK], "u32")
+            x_scales[c] = tile("x_scales%d" % c, [P, CHUNK], "u8", over, at)
+            quantise(x_codes[c][:], x_scales[c][:], x_bf[c][:])
 
-        def quantise_h(c):
-            places = slice(c * CHUNK, (c + 1) * CHUNK)
-            quantise(h_codes[:, places], h_scales[:, places], h_bf[c])
+        def group_of(tiles, j0):
+            first = max(k for k in tiles if k <= j0)
+            return tiles[first], j0 - first
 
-        def product(bank, codes, scales, fmt, moving_codes, moving_scales):
+        def quantise_h(first, over=None, at=0):
+            width = h_bf[first].shape[1] // PACK
+            h_codes[first] = tile("h_codes%d" % first, [P, width], "u32", over, at)
+            quantise(h_codes[first][:], h_scales[:, first : first + width], h_bf[first][:])
+
+        def product(bank, codes, scales, fmt, moving_codes, moving_scales, rows=range(PACK)):
             width = codes.shape[1] // PACK
-            for t in range(PACK):
+            for k, t in enumerate(rows):
                 nc.tensor.matmul_mx(
-                    bank[:, t, :],
+                    bank[:, k, :],
                     lhsT=codes[:, t * width : (t + 1) * width].bitcast(fmt),
                     lhsT_scale=scales[:, t * P : (t + 1) * P],
                     rhs=moving_codes.bitcast(FP8X4),
@@ -278,186 +244,240 @@ def tile_list_htabg_glu_resP_kernel(
                     stop=True,
                 )
 
-        def make_gate(b):
-            c, at = divmod(b * BLOCK, CHUNK)
-            ya = ps.tile([P, PACK, BLOCK], F32, name="ya", bufs=YA_BANKS)
-            product(ya, wa_codes[:], wa_scales, FP8X4, x_codes[c][:, at : at + BLOCK], x_scales[:, b * BLOCK : (b + 1) * BLOCK])
-            nc.scalar.activation(gates[b], ya[:].rearrange("p t n -> p n t"), SILU)
+        def new_gates(first, width, over=None, at=0):
+            gates[first] = tile("gates%d" % first, [P, width, PACK], "f32", over, at)
 
-        def make_yb(b):
+        def gate_places(j0, width):
+            group, at = group_of(gates, j0)
+            return group[:, at : at + width, :]
+
+        def make_gate(b, bank):
             c, at = divmod(b * BLOCK, CHUNK)
-            yb = ps.tile([P, PACK, BLOCK], F32, name="yb", bufs=YB_BANKS)
+            ya = bank_tile("ya%d" % b, bank)
+            product(ya, wa_codes[:], wa_scales, FP8X4, x_codes[c][:, at : at + BLOCK], x_scales[c][:, at : at + BLOCK])
+            nc.scalar.activation(gate_places(b * BLOCK, BLOCK), ya[:].rearrange("p t n -> p n t"), SILU)
+
+        def make_yb(b, bank):
+            c, at = divmod(b * BLOCK, CHUNK)
+            yb = bank_tile("yb%d" % b, bank)
             product(yb, wb_codes[:], wb_scales, FP8X4, v_codes[c][:, at : at + BLOCK], v_scales[:, b * BLOCK : (b + 1) * BLOCK])
-            return yb[:].rearrange("p t n -> p n t")
+            yb_banks[b] = yb[:].rearrange("p t n -> p n t")
 
-        def h_block(b):
-            c, at = divmod(b * BLOCK, CHUNK)
-            return h_bf[c][:, PACK * at : PACK * (at + BLOCK)].rearrange("p (n t) -> p n t", t=PACK)
+        def yb_places(j0, width):
+            b, at = divmod(j0, BLOCK)
+            return yb_banks[b][:, at : at + width, :]
 
-        def make_h(b):
-            nc.vector.tensor_tensor(h_block(b), gates[b], make_yb(b), MULT)
+        def new_h_bf(first, width, over=None, at=0):
+            h_bf[first] = tile("h_bf%d" % first, [P, PACK * width], "bf16", over, at)
 
-        def copy_yb(b):
-            y_banks[b] = tile("yb_copy%d" % b, [P, CHUNK - OWN, PACK], F32)
-            nc.scalar.copy(y_banks[b][:, BLOCK - OWN :, :], make_yb(b))
-            shared_banks[b - 1] = make_yb(b - 1)
-            nc.scalar.copy(y_banks[b][:, : BLOCK - OWN, :], shared_banks[b - 1][:, OWN:, :])
+        def h_places(j0, width):
+            group, at = group_of(h_bf, j0)
+            return group[:, PACK * at : PACK * (at + width)].rearrange("p (n t) -> p n t", t=PACK)
 
-        def make_h_gpsimd(b):
-            c = b // 2
-            out = h_bf[c][:, PACK * OWN :].rearrange("p (n t) -> p n t", t=PACK)
-            nc.gpsimd.tensor_tensor(out, gate_pairs[c][:, OWN:, :], y_banks[b][:], MULT)
+        def make_h(j0, width=BLOCK):
+            nc.vector.tensor_tensor(h_places(j0, width), gate_places(j0, width), yb_places(j0, width), MULT)
 
-        def make_h_shared(b, split):
-            yb = make_yb(b)
-            y_banks[b] = tile("yb_copy%d" % b, [P, BLOCK - split, PACK], F32)
-            nc.scalar.copy(y_banks[b][:], yb[:, split:, :])
-            return yb
+        def new_yb_copy(first, width, over=None, at=0):
+            yb_copies[first] = tile("yb_copy%d" % first, [P, width, PACK], "f32", over, at)
 
-        def make_y(b):
+        def copy_yb(j0, width):
+            group, at = group_of(yb_copies, j0)
+            nc.scalar.copy(group[:, at : at + width, :], yb_places(j0, width))
+
+        def make_h_gpsimd(first):
+            width = yb_copies[first].shape[1]
+            nc.gpsimd.tensor_tensor(h_places(first, width), gate_places(first, width), yb_copies[first][:], MULT)
+
+        def make_y(b, bank):
             places = slice(b * BLOCK, (b + 1) * BLOCK)
-            y = ps.tile([P, PACK, BLOCK], F32, name="y", bufs=Y_BANKS)
-            product(y, wd_codes[:], wd_dealt_scales, FP4X4, h_codes[:, places], h_scales[:, places])
-            ys[b] = y
+            codes, at = group_of(h_codes, b * BLOCK)
+            y_banks[b] = bank_tile("y%d" % b, bank)
+            product(y_banks[b], wd_dealt["codes"][:], wd_dealt["scales"], FP4X4, codes[:, at : at + BLOCK], h_scales[:, places])
 
-        def res_block(b):
-            k = max(n for n, piece in enumerate(FIRST_PIECES) if piece[0] <= b * BLOCK)
-            at = b * BLOCK - FIRST_PIECES[k][0]
-            return res_pieces[k][:, :, at : at + BLOCK]
+        def res_places(j0, width):
+            k = max(n for n, piece in enumerate(RES_PIECES) if piece[0] <= j0)
+            at = j0 - RES_PIECES[k][0]
+            return res_pieces[k][:, :, at : at + width]
 
         def sums_block(b):
             c, at = divmod(b * BLOCK, CHUNK)
             return sums[c][:, :, at : at + BLOCK]
 
+        def add_res(b):
+            nc.vector.tensor_tensor(sums_block(b), y_banks[b][:], res_places(b * BLOCK, BLOCK), ADD)
+
         def store_block(b):
             nc.sync.dma_start(out_hbm[:, :, b * BLOCK : (b + 1) * BLOCK], sums_block(b))
 
         def store_chunk(c):
-            nc.sync.dma_start(out_hbm[:, :, c * CHUNK : (c + 1) * CHUNK], sums[c])
+            nc.sync.dma_start(out_hbm[:, :, c * CHUNK : (c + 1) * CHUNK], sums[c][:])
 
-        def add_res(b):
-            nc.vector.tensor_tensor(sums_block(b), ys[b][:], res_block(b), ADD)
+        def round_out(b, copy, first=0, width=BLOCK):
+            j0 = b * BLOCK + first
+            round_into_words(copy, out_bf[:, PACK * j0 : PACK * (j0 + width)], sums_block(b)[:, :, first : first + width])
 
-        def copy_y(b):
-            y_banks[b] = tile("y_copy%d" % b, [P, PACK, BLOCK], F32)
-            nc.scalar.copy(y_banks[b][:], ys[b][:])
+        def new_out_codes(j0, width, over=None, at=0):
+            out_codes[j0] = tile("out_codes%d" % j0, [P, width], "u32", over, at)
 
-        def add_res_gpsimd(b):
-            nc.gpsimd.tensor_tensor(sums_block(b), y_banks[b][:], res_block(b), ADD)
+        def quantise_out(j0, width):
+            codes, at = group_of(out_codes, j0)
+            quantise(codes[:, at : at + width], out_scales[:, j0 : j0 + width], out_bf[:, PACK * j0 : PACK * (j0 + width)])
 
-        def round_out(b, copy):
-            c, at = divmod(b * BLOCK, CHUNK)
-            round_into_words(copy, out_bf[c][:, PACK * at : PACK * (at + BLOCK)], sums_block(b))
+        def store_words(queue, first):
+            codes = out_codes[first]
+            queue.dma_start(out_words_hbm[:, first : first + codes.shape[1]], codes[:].bitcast(I32))
 
-        def quantise_out(c):
-            places = slice(c * CHUNK, (c + 1) * CHUNK)
-            quantise(out_codes(c * CHUNK, CHUNK), out_scales[:, places], out_bf[c][:])
+        def store_scales():
+            for q in range(QUADRANTS):
+                queue = nc.sync if q < QUADRANTS // 2 else nc.scalar
+                queue.dma_start(hbm_scale_rows(out_2, q), scale_rows(out_scales, q))
 
-        def quantise_out_block(b):
-            c, at = divmod(b * BLOCK, CHUNK)
-            quantise(out_codes(b * BLOCK, BLOCK), out_scales[:, b * BLOCK : (b + 1) * BLOCK], out_bf[c][:, PACK * at : PACK * (at + BLOCK)])
 
-        def store_words(queue, c):
-            first, t = code_tiles[c]
-            queue.dma_start(out_words_hbm[:, first : first + t.shape[1]], t[:].bitcast(I32))
+        nc.sync.dma_start(tab_list[:], offs)
+        nc.sync.dma_start(tab_scale_tile[staged:, :].bitcast(I32), tab_scales[0].bitcast(I32))
+        load_wgt(nc.scalar)
+        load_x(0)
+        nc.vector.memset(wgt_rows[HEADS * blocks :, :], 0.0)
+        nc.vector.memset(tab_scale_tile[:staged, :].bitcast(I32), 0)
+        nc.vector.memset(v_scales[:].bitcast(I32), 0)
+        make_identity(nc, ident[:])
+        nc.scalar.activation(warm[:], ident[:, 0:1], SILU)
+        nc.sync.dma_start(head_lists[:], offs2)
+        load_x(1)
+        load_x(2)
+        load_x(3)
+        nc.vector.tensor_copy(v_staged[:], tab_scale_tile[:].indirect(tab_list[:]))
 
-        on_scalar, on_vector = nc.scalar.copy, nc.vector.tensor_copy
-        deal_wd_codes(on_vector)
-        for j0, width in FIRST_PIECES:
+        load_weight(wa_raw, wa)
+        load_tab()
+        spread_wgt()
+        for j0, width in WGT_PIECES:
             gather_x(0, j0, width)
         gather_x(1, 0, J)
+        new_x_bf(0)
         round_x(0, on_scalar, slice(0, 2))
         gather_x(2, 0, J)
+        nc.gpsimd.memset(wd_raw_scales[:].bitcast(I32), 0)
+        carry_v_scales()
+        load_weight(wb_raw, wb)
+        load_wd_codes(nc.sync)
+        load_wd_scales(nc.sync)
+        load_res(0)
+        load_res(1)
         gather_x(3, 0, CHUNK)
-        gather_x(3, CHUNK, CHUNK)
-        gather_x(3, HALF, HALF)
+        gather_x(3, CHUNK, J - CHUNK)
+        load_res(2)
         round_x(0, on_scalar, slice(2, PACK))
-        round_wa(0, on_scalar)
-        deal_wd_scales(on_vector)
-        round_wa(1, on_vector)
         quantise_x(0)
+        round_weight(on_scalar, wa_bf, wa_raw, 0, WA_SCALAR)
+        round_weight(on_vector, wa_bf, wa_raw, WA_SCALAR, P)
         quantise(wa_codes[:], wa_scales[:], wa_bf[:])
+        new_x_bf(3, "wa_raw", 6144)
+        round_x_gpsimd(3)
+        new_x_bf(1, "wa_raw", 2048)
         round_x(1, on_scalar)
-        round_wb(0, on_vector)
-        round_wb(1, on_vector)
-        quantise_x(1)
-        quantise(wb_codes[:], wb_scales[:], wb_bf[:])
-        make_gate(0)
-        make_gate(1)
-        round_x_gpsimd(2 * CHUNK, CHUNK)
-        round_x_gpsimd(3 * CHUNK, BLOCK)
-        gather_v(0)
-        make_gate(2)
-        make_gate(3)
-        round_x_block(7, on_scalar)
-        gather_v(1)
-        make_h(0)
-        make_h(1)
-        copy_yb(3)
-        quantise_x(2)
-        quantise_x(3)
-        quantise_h(0)
-        make_y(0)
-        make_h_gpsimd(3)
+        new_x_bf(2, "wa_raw", 4096)
+        round_x(2, on_scalar)
+        gather_v(0, "wa_raw")
+        gather_v(1, "wa_raw", 1024)
         gather_v(2)
-        nc.vector.tensor_tensor(h_block(2)[:, :OWN, :], gates[2][:, :OWN, :], shared_banks[2][:, :OWN, :], MULT)
-        make_gate(4)
-        make_gate(5)
-        make_y(1)
-        copy_yb(5)
-        make_gate(6)
+        new_gates(0, 128)
+        make_gate(0, 0)
+        quantise_x(1, "v_staged")
+        quantise_x(2, "v_staged", 256)
+        round_weight(on_scalar, wb_bf, wb_raw, 0, WB_SCALAR)
+        round_weight(on_vector, wb_bf, wb_raw, WB_SCALAR, P)
+        new_gates(128, 128, "wb_raw", 6144)
+        make_gate(1, 1)
+        new_gates(256, 256, "wb_raw")
+        make_gate(2, 0)
+        make_gate(3, 3)
+        new_gates(512, 128, "wb_raw", 4096)
+        make_gate(4, 2)
+        deal_wd_codes(on_vector)
+        quantise(wb_codes[:], wb_scales[:], wb_bf[:])
+        quantise_x(3, "wd_raw_codes")
+        gather_v(3, "wd_raw_codes", 256)
+        make_yb(0, 4)
+        make_yb(1, 6)
+        make_yb(3, 5)
+        make_yb(2, 7)
+        make_yb(4, 1)
+        new_h_bf(0, 256)
+        make_h(0)
+        new_yb_copy(512 - FIRST_SHARE, FIRST_SHARE)
+        copy_yb(384, 128)
+        copy_yb(512 - FIRST_SHARE, FIRST_SHARE - 128)
+        make_h(128)
+        new_gates(640, 256)
+        new_gates(896, 128)
+        make_gate(7, 4)
+        make_yb(7, 2)
+        deal_wd_scales(on_vector, "gates0")
+        quantise_h(0)
+        make_gate(5, 6)
+        make_gate(6, 5)
+        make_y(0, 0)
+        make_y(1, 3)
+        new_h_bf(256, 256)
+        make_h_gpsimd(512 - FIRST_SHARE)
+        new_h_bf(512, 128)
+        make_h(512)
+        make_h(256, 256 - FIRST_SHARE)
+        make_yb(5, 4)
+        make_yb(6, 1)
+        new_h_bf(896, 128)
+        make_h(896)
+        new_yb_copy(640, SECOND_SHARE)
+        copy_yb(640, 128)
+        copy_yb(768, SECOND_SHARE - 128)
         add_res(0)
         store_block(0)
         add_res(1)
         store_block(1)
-        quantise_h(1)
-        make_y(2)
-        make_y(3)
-        make_h_gpsimd(5)
         round_out(0, on_scalar)
-        make_gate(7)
-        gather_v(3)
-        nc.vector.tensor_tensor(h_block(4)[:, :OWN, :], gates[4][:, :OWN, :], shared_banks[4][:, :OWN, :], MULT)
-        yb7 = make_h_shared(7, SPLIT)
+        quantise_h(512, "yb_copy%d" % (512 - FIRST_SHARE))
+        quantise_h(256)
+        quantise_h(896, "yb_copy%d" % (512 - FIRST_SHARE), 512)
+        make_y(4, 5)
+        make_y(2, 6)
+        make_y(3, 7)
+        make_y(7, 2)
+        new_h_bf(640, 256, "res0")
+        make_h_gpsimd(640)
+        make_h(640 + SECOND_SHARE, 256 - SECOND_SHARE)
         round_out(1, on_scalar)
+        add_res(4)
+        store_block(4)
         add_res(2)
         store_block(2)
+        round_out(4, on_scalar)
         add_res(3)
         store_block(3)
         round_out(2, on_scalar)
-        quantise_h(2)
-        make_y(4)
-        nc.gpsimd.tensor_tensor(h_block(7)[:, SPLIT:, :], gates[7][:, SPLIT:, :], y_banks[7][:], MULT)
-        quantise_out_block(0)
+        quantise_h(640)
+        make_y(5, 0)
+        make_y(6, 3)
+        new_out_codes(0, 256, "yb_copy640")
+        quantise_out(0, 256)
         store_words(nc.sync, 0)
+        add_res(7)
+        store_block(7)
         round_out(3, on_scalar)
-        make_h(6)
-        nc.vector.tensor_tensor(h_block(7)[:, :SPLIT, :], gates[7][:, :SPLIT, :], yb7[:, :SPLIT, :], MULT)
-        make_y(5)
-        add_res(4)
-        store_block(4)
-        quantise_h(3)
-        make_y(6)
-        make_y(7)
-        round_out(4, on_scalar)
-        quantise_out_block(1)
-        quantise_out(1)
-        store_words(nc.sync, 1)
+        new_out_codes(256, 384, "yb_copy640", 1024)
+        quantise_out(512, 128)
         add_res(5)
         store_block(5)
+        round_out(7, on_scalar)
         add_res(6)
         store_block(6)
         round_out(5, on_scalar)
-        add_res(7)
-        store_block(7)
-        round_out(6, on_scalar)
-        quantise_out(2)
-        store_words(nc.sync, 2)
-        round_out(7, on_vector)
-        quantise_out_block(6)
-        quantise_out_block(7)
-        store_words(nc.scalar, 3)
-
-        for q in range(QUADRANTS):
-            queue = nc.sync if q < QUADRANTS // 2 else nc.scalar
-            queue.dma_start(hbm_scale_rows(out_2, q), scale_rows(out_scales, q))
+        quantise_out(256, 256)
+        store_words(nc.sync, 256)
+        new_out_codes(640, 384)
+        quantise_out(896, 128)
+        round_out(6, on_vector)
+        quantise_out(640, 128)
+        quantise_out(768, 128)
+        store_words(nc.scalar, 640)
+        store_scales()

@@ -32,9 +32,8 @@ CHUNK = 256
 CHUNKS = J // CHUNK
 HALF = J // 2
 WGT_PIECES = ((0, 256), (256, 256), (512, 512))
-RES_PIECES = ((0, 256), (256, 256), (512, 512))
-RES_PLACES = (("x_rows2", 0), ("x_rows2", 4096), ("x_rows3", 0))
-FIRST_SHARE, SECOND_SHARE = 176, 192
+RES_TILES = (((0, 0), 2, "x_rows2", 0), ((0, 2), 2, "x_rows2", 2048), ((2, 0), 4, "x_rows2", 4096), ((1, 0), 4, "x_rows3", 0), ((3, 0), 4, "x_rows3", 4096))
+FIRST_SHARE, SECOND_SHARE = 160, 160
 WA_SCALAR, WB_SCALAR = 64, 48
 
 
@@ -83,7 +82,7 @@ def tile_list_htabg_glu_resP_kernel(
         wb_raw = tile("wb_raw", [P, PACK, R], "f32", "tab_scale_tile")
         wd_raw_scales = tile("wd_raw_scales", [P, N], "u8", "x_rows0", 2048, room=2048)
         wd_raw_codes = tile("wd_raw_codes", [P, 2 * N], "u8", "x_rows0", room=2048)
-        res_pieces = [tile("res%d" % j0, [P, PACK, width], "f32", over, at) for (j0, width), (over, at) in zip(RES_PIECES, RES_PLACES)]
+        res_tiles = {key: tile("res%d_%d" % key, [P, rows, CHUNK], "f32", over, at) for key, rows, over, at in RES_TILES}
         blocks = J // P
         wgt_rows = tile("wgt_rows", [P, P], "f32")
         ident = tile("ident", [P, P], "f32")
@@ -101,9 +100,9 @@ def tile_list_htabg_glu_resP_kernel(
         def load_weight(raw, w):
             nc.sync.dma_start(raw[:], w.rearrange("(p i) r -> p i r", i=PACK))
 
-        def load_res(k):
-            j0, width = RES_PIECES[k]
-            nc.sync.dma_start(res_pieces[k][:], res_hbm[:, :, j0 : j0 + width])
+        def load_res(c, row):
+            rows = res_tiles[c, row].shape[1]
+            nc.sync.dma_start(res_tiles[c, row][:], res_hbm[:, row : row + rows, c * CHUNK : (c + 1) * CHUNK])
 
         def load_tab():
             nc.sync.dma_start(tab_codes[:].bitcast(I32), tab_words[0].rearrange("p t i -> p (t i)").bitcast(I32))
@@ -159,7 +158,7 @@ def tile_list_htabg_glu_resP_kernel(
         wb_scales = tile("wb_scales", [P, R], "u8")
         sums = [tile("sums%d" % c, [P, PACK, CHUNK], "f32") for c in range(CHUNKS)]
         out_bf = tile("out_bf", [P, PACK * J], "bf16")
-        h_codes = {}
+        h_codes, ya_banks = {}, {}
         x_bf, x_codes, v_codes, h_bf, gates, yb_copies, out_codes, yb_banks, y_banks = {}, {}, {}, {}, {}, {}, {}, {}, {}
 
         def deal_wd_codes(copy, over=None, at=0):
@@ -251,11 +250,17 @@ def tile_list_htabg_glu_resP_kernel(
             group, at = group_of(gates, j0)
             return group[:, at : at + width, :]
 
-        def make_gate(b, bank):
+        def make_ya(b, bank):
             c, at = divmod(b * BLOCK, CHUNK)
-            ya = bank_tile("ya%d" % b, bank)
-            product(ya, wa_codes[:], wa_scales, FP8X4, x_codes[c][:, at : at + BLOCK], x_scales[c][:, at : at + BLOCK])
-            nc.scalar.activation(gate_places(b * BLOCK, BLOCK), ya[:].rearrange("p t n -> p n t"), SILU)
+            ya_banks[b] = bank_tile("ya%d" % b, bank)
+            product(ya_banks[b], wa_codes[:], wa_scales, FP8X4, x_codes[c][:, at : at + BLOCK], x_scales[c][:, at : at + BLOCK])
+
+        def apply_silu(b):
+            nc.scalar.activation(gate_places(b * BLOCK, BLOCK), ya_banks[b][:].rearrange("p t n -> p n t"), SILU)
+
+        def make_gate(b, bank):
+            make_ya(b, bank)
+            apply_silu(b)
 
         def make_yb(b, bank):
             c, at = divmod(b * BLOCK, CHUNK)
@@ -294,17 +299,26 @@ def tile_list_htabg_glu_resP_kernel(
             y_banks[b] = bank_tile("y%d" % b, bank)
             product(y_banks[b], wd_dealt["codes"][:], wd_dealt["scales"], FP4X4, codes[:, at : at + BLOCK], h_scales[:, places])
 
-        def res_places(j0, width):
-            k = max(n for n, piece in enumerate(RES_PIECES) if piece[0] <= j0)
-            at = j0 - RES_PIECES[k][0]
-            return res_pieces[k][:, :, at : at + width]
+        def make_y_rows(c, u, bank):
+            y_banks[c, u] = bank_tile("y%d_%d" % (c, u), bank, (P, 2, CHUNK))
+            scales = h_scales[:, c * CHUNK : (c + 1) * CHUNK]
+            product(y_banks[c, u], wd_dealt["codes"][:], wd_dealt["scales"], FP4X4, h_codes[c * CHUNK][:], scales, range(2 * u, 2 * u + 2))
+
+        def add_rows(c, u):
+            rows = slice(2 * u, 2 * u + 2)
+            nc.vector.tensor_tensor(sums[c][:, rows, :], y_banks[c, u][:], res_rows(c, u), ADD)
+            nc.sync.dma_start(out_hbm[:, rows, c * CHUNK : (c + 1) * CHUNK], sums[c][:, rows, :])
+
+        def res_rows(c, u):
+            row = max(r for k, r in res_tiles if k == c and r <= 2 * u)
+            return res_tiles[c, row][:, 2 * u - row : 2 * u - row + 2, :]
 
         def sums_block(b):
             c, at = divmod(b * BLOCK, CHUNK)
             return sums[c][:, :, at : at + BLOCK]
 
         def add_res(b):
-            nc.vector.tensor_tensor(sums_block(b), y_banks[b][:], res_places(b * BLOCK, BLOCK), ADD)
+            nc.vector.tensor_tensor(sums_block(b), y_banks[b][:], res_tiles[b // 2, 0][:, :, b % 2 * BLOCK : (b % 2 + 1) * BLOCK], ADD)
 
         def store_block(b):
             nc.sync.dma_start(out_hbm[:, :, b * BLOCK : (b + 1) * BLOCK], sums_block(b))
@@ -362,11 +376,13 @@ def tile_list_htabg_glu_resP_kernel(
         load_weight(wb_raw, wb)
         load_wd_codes(nc.sync)
         load_wd_scales(nc.sync)
-        load_res(0)
-        load_res(1)
+        load_res(0, 0)
+        load_res(0, 2)
+        load_res(2, 0)
         gather_x(3, 0, CHUNK)
         gather_x(3, CHUNK, J - CHUNK)
-        load_res(2)
+        load_res(1, 0)
+        load_res(3, 0)
         round_x(0, on_scalar, slice(2, PACK))
         quantise_x(0)
         round_weight(on_scalar, wa_bf, wa_raw, 0, WA_SCALAR)
@@ -390,10 +406,11 @@ def tile_list_htabg_glu_resP_kernel(
         new_gates(128, 128, "wb_raw", 6144)
         make_gate(1, 1)
         new_gates(256, 256, "wb_raw")
-        make_gate(2, 0)
+        make_gate(2, 2)
         make_gate(3, 3)
         new_gates(512, 128, "wb_raw", 4096)
-        make_gate(4, 2)
+        make_gate(4, 7)
+        make_ya(5, 0)
         deal_wd_codes(on_vector)
         quantise(wb_codes[:], wb_scales[:], wb_bf[:])
         quantise_x(3, "wd_raw_codes")
@@ -401,83 +418,72 @@ def tile_list_htabg_glu_resP_kernel(
         make_yb(0, 4)
         make_yb(1, 6)
         make_yb(3, 5)
-        make_yb(2, 7)
-        make_yb(4, 1)
+        make_yb(2, 1)
+        make_yb(4, 2)
         new_h_bf(0, 256)
         make_h(0)
         new_yb_copy(512 - FIRST_SHARE, FIRST_SHARE)
         copy_yb(384, 128)
         copy_yb(512 - FIRST_SHARE, FIRST_SHARE - 128)
         make_h(128)
-        new_gates(640, 256)
-        new_gates(896, 128)
-        make_gate(7, 4)
-        make_yb(7, 2)
+        make_yb(5, 3)
+        new_gates(640, 128, "gates128")
+        apply_silu(5)
         deal_wd_scales(on_vector, "gates0")
         quantise_h(0)
-        make_gate(5, 6)
-        make_gate(6, 5)
-        make_y(0, 0)
-        make_y(1, 3)
+        new_gates(768, 256)
+        make_gate(6, 7)
+        make_gate(7, 4)
+        make_y_rows(0, 0, 6)
+        make_y_rows(0, 1, 5)
         new_h_bf(256, 256)
         make_h_gpsimd(512 - FIRST_SHARE)
-        new_h_bf(512, 128)
+        new_h_bf(512, 256)
         make_h(512)
         make_h(256, 256 - FIRST_SHARE)
-        make_yb(5, 4)
-        make_yb(6, 1)
-        new_h_bf(896, 128)
-        make_h(896)
-        new_yb_copy(640, SECOND_SHARE)
-        copy_yb(640, 128)
-        copy_yb(768, SECOND_SHARE - 128)
-        add_res(0)
-        store_block(0)
-        add_res(1)
-        store_block(1)
+        make_yb(7, 0)
+        make_yb(6, 2)
+        make_h(640)
+        new_yb_copy(1024 - SECOND_SHARE, SECOND_SHARE)
+        copy_yb(896, 128)
+        copy_yb(1024 - SECOND_SHARE, SECOND_SHARE - 128)
+        add_rows(0, 0)
+        add_rows(0, 1)
         round_out(0, on_scalar)
-        quantise_h(512, "yb_copy%d" % (512 - FIRST_SHARE))
-        quantise_h(256)
-        quantise_h(896, "yb_copy%d" % (512 - FIRST_SHARE), 512)
-        make_y(4, 5)
-        make_y(2, 6)
-        make_y(3, 7)
-        make_y(7, 2)
-        new_h_bf(640, 256, "res0")
-        make_h_gpsimd(640)
-        make_h(640 + SECOND_SHARE, 256 - SECOND_SHARE)
+        quantise_h(512, "res0_0")
+        quantise_h(256, "res0_0", 1024)
+        make_y_rows(2, 0, 1)
+        make_y_rows(2, 1, 7)
+        make_y_rows(1, 0, 3)
+        make_y_rows(1, 1, 4)
+        new_h_bf(768, 256, "res0_2")
+        make_h_gpsimd(1024 - SECOND_SHARE)
+        make_h(768, 256 - SECOND_SHARE)
         round_out(1, on_scalar)
-        add_res(4)
-        store_block(4)
-        add_res(2)
-        store_block(2)
+        add_rows(2, 0)
+        add_rows(2, 1)
         round_out(4, on_scalar)
-        add_res(3)
-        store_block(3)
-        round_out(2, on_scalar)
-        quantise_h(640)
-        make_y(5, 0)
-        make_y(6, 3)
-        new_out_codes(0, 256, "yb_copy640")
+        add_rows(1, 0)
+        round_out(5, on_scalar)
+        quantise_h(768, "res2_0")
+        make_y_rows(3, 0, 6)
+        make_y_rows(3, 1, 5)
+        new_out_codes(0, 256, "yb_copy%d" % (1024 - SECOND_SHARE))
         quantise_out(0, 256)
         store_words(nc.sync, 0)
-        add_res(7)
-        store_block(7)
+        add_rows(1, 1)
+        round_out(2, on_scalar)
+        add_rows(3, 0)
         round_out(3, on_scalar)
-        new_out_codes(256, 384, "yb_copy640", 1024)
-        quantise_out(512, 128)
-        add_res(5)
-        store_block(5)
-        round_out(7, on_scalar)
-        add_res(6)
-        store_block(6)
-        round_out(5, on_scalar)
+        add_rows(3, 1)
+        new_out_codes(256, 512, "res2_0")
+        quantise_out(512, 256)
+        round_out(6, on_scalar)
+        round_out(7, on_vector)
         quantise_out(256, 256)
         store_words(nc.sync, 256)
-        new_out_codes(640, 384)
+        new_out_codes(768, 256)
         quantise_out(896, 128)
-        round_out(6, on_vector)
-        quantise_out(640, 128)
         quantise_out(768, 128)
-        store_words(nc.scalar, 640)
+        store_words(nc.scalar, 768)
         store_scales()

@@ -32,7 +32,7 @@ CHUNK = 256
 CHUNKS = J // CHUNK
 HALF = J // 2
 WGT_PIECES = ((0, 256), (256, 256), (512, 512))
-RES_TILES = (((0, 0), 2, "x_rows2", 0), ((0, 2), 2, "x_rows2", 2048), ((2, 0), 4, "x_rows2", 4096), ((1, 0), 4, "x_rows3", 0), ((3, 0), 4, "x_rows3", 4096))
+RES_TILES = (((0, 0), 2, "x_rows2", 0), ((0, 2), 2, "x_rows2", 2048), ((2, 0), 4, "x_rows3", 0), ((1, 0), 4, "x_rows3", 4096), ((3, 0), 4, "wa_bf", 0))
 FIRST_SHARE, SECOND_SHARE = 160, 160
 WA_SCALAR, WB_SCALAR = 64, 48
 
@@ -78,11 +78,10 @@ def tile_list_htabg_glu_resP_kernel(
         x_rows = [tile("x_rows%d" % i, [P, T], "f32") for i in range(PACK)]
         wgt = tile("wgt", [P, J], "f32")
         tab_codes = tile("tab_codes", [P, T], "u32")
-        wa_raw = tile("wa_raw", [P, PACK, R], "f32")
+        wa_raw = tile("wa_raw", [P, PACK, R], "f32", room=9216)
         wb_raw = tile("wb_raw", [P, PACK, R], "f32", "tab_scale_tile")
-        wd_raw_scales = tile("wd_raw_scales", [P, N], "u8", "x_rows0", 2048, room=2048)
-        wd_raw_codes = tile("wd_raw_codes", [P, 2 * N], "u8", "x_rows0", room=2048)
-        res_tiles = {key: tile("res%d_%d" % key, [P, rows, CHUNK], "f32", over, at) for key, rows, over, at in RES_TILES}
+        wd_raw_scales = tile("wd_raw_scales", [P, N], "u8", "x_rows2", 6144)
+        wd_raw_codes = tile("wd_raw_codes", [P, 2 * N], "u8", "x_rows2", 4096, room=2048)
         blocks = J // P
         wgt_rows = tile("wgt_rows", [P, P], "f32")
         ident = tile("ident", [P, P], "f32")
@@ -156,6 +155,7 @@ def tile_list_htabg_glu_resP_kernel(
         wb_bf = tile("wb_bf", [P, PACK * R], "bf16")
         wb_codes = tile("wb_codes", [P, R], "u32")
         wb_scales = tile("wb_scales", [P, R], "u8")
+        res_tiles = {key: tile("res%d_%d" % key, [P, rows, CHUNK], "f32", over, at) for key, rows, over, at in RES_TILES}
         sums = [tile("sums%d" % c, [P, PACK, CHUNK], "f32") for c in range(CHUNKS)]
         out_bf = tile("out_bf", [P, PACK * J], "bf16")
         h_codes, ya_banks = {}, {}
@@ -183,10 +183,12 @@ def tile_list_htabg_glu_resP_kernel(
                 MULT,
             )
 
-        def gather_v(c, over=None, at=0):
-            v_codes[c] = tile("v_codes%d" % c, [P, CHUNK], "u32", over, at)
-            entries = slice(c * CHUNK // LIST_ROWS, (c + 1) * CHUNK // LIST_ROWS)
-            nc.vector.tensor_copy(v_codes[c][:], tab_codes[:].indirect(tab_list[:, entries]))
+        def gather_v(first, chunks, over=None, at=0):
+            codes = tile("v_codes%d" % first, [P, chunks * CHUNK], "u32", over, at)
+            entries = slice(first * CHUNK // LIST_ROWS, (first + chunks) * CHUNK // LIST_ROWS)
+            nc.vector.tensor_copy(codes[:], tab_codes[:].indirect(tab_list[:, entries]))
+            for k in range(chunks):
+                v_codes[first + k] = codes[:, k * CHUNK : (k + 1) * CHUNK]
 
         def round_weight(copy, bf, raw, m0, m1):
             src = raw[:].rearrange("p i (m t) -> p m i t", t=PACK)[:, m0:m1]
@@ -364,6 +366,8 @@ def tile_list_htabg_glu_resP_kernel(
 
         load_weight(wa_raw, wa)
         load_tab()
+        carry_v_scales()
+        load_weight(wb_raw, wb)
         spread_wgt()
         for j0, width in WGT_PIECES:
             gather_x(0, j0, width)
@@ -371,36 +375,32 @@ def tile_list_htabg_glu_resP_kernel(
         new_x_bf(0)
         round_x(0, on_scalar, slice(0, 2))
         gather_x(2, 0, J)
-        nc.gpsimd.memset(wd_raw_scales[:].bitcast(I32), 0)
-        carry_v_scales()
-        load_weight(wb_raw, wb)
         load_wd_codes(nc.sync)
+        nc.gpsimd.memset(wd_raw_scales[:].bitcast(I32), 0)
         load_wd_scales(nc.sync)
         load_res(0, 0)
         load_res(0, 2)
-        load_res(2, 0)
         gather_x(3, 0, CHUNK)
         gather_x(3, CHUNK, J - CHUNK)
+        load_res(2, 0)
         load_res(1, 0)
-        load_res(3, 0)
         round_x(0, on_scalar, slice(2, PACK))
         quantise_x(0)
         round_weight(on_scalar, wa_bf, wa_raw, 0, WA_SCALAR)
         round_weight(on_vector, wa_bf, wa_raw, WA_SCALAR, P)
         quantise(wa_codes[:], wa_scales[:], wa_bf[:])
-        new_x_bf(3, "wa_raw", 6144)
+        load_res(3, 0)
+        new_x_bf(3, "wa_raw", 4096)
         round_x_gpsimd(3)
-        new_x_bf(1, "wa_raw", 2048)
+        new_x_bf(1, "wa_raw")
         round_x(1, on_scalar)
-        new_x_bf(2, "wa_raw", 4096)
+        new_x_bf(2, "wa_raw", 2048)
         round_x(2, on_scalar)
-        gather_v(0, "wa_raw")
-        gather_v(1, "wa_raw", 1024)
-        gather_v(2)
+        gather_v(0, 3, "wa_raw", 6144)
         new_gates(0, 128)
         make_gate(0, 0)
-        quantise_x(1, "v_staged")
-        quantise_x(2, "v_staged", 256)
+        quantise_x(1)
+        quantise_x(2)
         round_weight(on_scalar, wb_bf, wb_raw, 0, WB_SCALAR)
         round_weight(on_vector, wb_bf, wb_raw, WB_SCALAR, P)
         new_gates(128, 128, "wb_raw", 6144)
@@ -414,7 +414,7 @@ def tile_list_htabg_glu_resP_kernel(
         deal_wd_codes(on_vector)
         quantise(wb_codes[:], wb_scales[:], wb_bf[:])
         quantise_x(3, "wd_raw_codes")
-        gather_v(3, "wd_raw_codes", 256)
+        gather_v(3, 1, "wd_raw_codes", 256)
         make_yb(0, 4)
         make_yb(1, 6)
         make_yb(3, 5)

@@ -33,7 +33,7 @@ CHUNKS = J // CHUNK
 HALF = J // 2
 WGT_PIECES = ((0, 256), (256, 256), (512, 512))
 RES_TILES = (((0, 0), 2, "x_rows2", 0), ((0, 2), 2, "x_rows2", 2048), ((2, 0), 4, "x_rows3", 0), ((1, 0), 4, "x_rows3", 4096), ((3, 0), 4, "wa_bf", 0))
-FIRST_SHARE, SECOND_SHARE = 160, 160
+FIRST_SHARE, SECOND_SHARE = 176, 128
 WA_SCALAR, WB_SCALAR = 64, 48
 
 
@@ -61,6 +61,10 @@ def tile_list_htabg_glu_resP_kernel(
             spans[name] = (start, size)
             return sb.tile(shape, DTYPES[kind], name=name, align_bytes=64, offset=start)
 
+        def reserve(name, size):
+            spans[name] = (spans["end"][0], size)
+            spans["end"] = (spans["end"][0] + size, 0)
+
         def bank_tile(name, bank, shape=(P, PACK, BLOCK)):
             return ps.tile(list(shape), F32, name=name, offset=bank * BANK * 4)
 
@@ -72,16 +76,16 @@ def tile_list_htabg_glu_resP_kernel(
 
         tab_list = lists.tile([P, J // LIST_ROWS], U16, name="tab_list")
         head_lists = lists.tile([P, J // LIST_ROWS], U16, name="head_lists")
-        tab_scale_tile = tile("tab_scale_tile", [P, T], "u8", room=PACK * R * 4)
+        tab_scale_tile = tile("tab_scale_tile", [P, T], "u8")
         v_staged = tile("v_staged", [P, J], "u8")
         v_scales = tile("v_scales", [P, J], "u8")
         x_rows = [tile("x_rows%d" % i, [P, T], "f32") for i in range(PACK)]
         wgt = tile("wgt", [P, J], "f32")
         tab_codes = tile("tab_codes", [P, T], "u32")
         wa_raw = tile("wa_raw", [P, PACK, R], "f32", room=9216)
-        wb_raw = tile("wb_raw", [P, PACK, R], "f32", "tab_scale_tile")
-        wd_raw_scales = tile("wd_raw_scales", [P, N], "u8", "x_rows2", 6144)
-        wd_raw_codes = tile("wd_raw_codes", [P, 2 * N], "u8", "x_rows2", 4096, room=2048)
+        wb_raw = tile("wb_raw", [P, PACK, R], "f32")
+        wd_raw_scales = tile("wd_raw_scales", [P, N], "u8")
+        wd_raw_codes = tile("wd_raw_codes", [P, 2 * N], "u8", room=2048)
         blocks = J // P
         wgt_rows = tile("wgt_rows", [P, P], "f32")
         ident = tile("ident", [P, P], "f32")
@@ -353,6 +357,7 @@ def tile_list_htabg_glu_resP_kernel(
         nc.sync.dma_start(tab_scale_tile[staged:, :].bitcast(I32), tab_scales[0].bitcast(I32))
         load_wgt(nc.scalar)
         load_x(0)
+        nc.vector.memset(wd_raw_scales[:].bitcast(I32), 0)
         nc.vector.memset(wgt_rows[HEADS * blocks :, :], 0.0)
         nc.vector.memset(tab_scale_tile[:staged, :].bitcast(I32), 0)
         nc.vector.memset(v_scales[:].bitcast(I32), 0)
@@ -366,8 +371,10 @@ def tile_list_htabg_glu_resP_kernel(
 
         load_weight(wa_raw, wa)
         load_tab()
-        carry_v_scales()
         load_weight(wb_raw, wb)
+        load_wd_codes(nc.sync)
+        load_wd_scales(nc.sync)
+        carry_v_scales()
         spread_wgt()
         for j0, width in WGT_PIECES:
             gather_x(0, j0, width)
@@ -375,9 +382,6 @@ def tile_list_htabg_glu_resP_kernel(
         new_x_bf(0)
         round_x(0, on_scalar, slice(0, 2))
         gather_x(2, 0, J)
-        load_wd_codes(nc.sync)
-        nc.gpsimd.memset(wd_raw_scales[:].bitcast(I32), 0)
-        load_wd_scales(nc.sync)
         load_res(0, 0)
         load_res(0, 2)
         gather_x(3, 0, CHUNK)
@@ -430,11 +434,12 @@ def tile_list_htabg_glu_resP_kernel(
         new_gates(640, 128, "gates128")
         apply_silu(5)
         deal_wd_scales(on_vector, "gates0")
-        quantise_h(0)
+        reserve("codes", 3072)
+        quantise_h(0, "codes", 512)
         new_gates(768, 256)
-        make_gate(6, 7)
         make_gate(7, 4)
-        make_y_rows(0, 0, 6)
+        make_gate(6, 6)
+        make_y_rows(0, 0, 7)
         make_y_rows(0, 1, 5)
         new_h_bf(256, 256)
         make_h_gpsimd(512 - FIRST_SHARE)
@@ -446,17 +451,16 @@ def tile_list_htabg_glu_resP_kernel(
         make_h(640)
         new_yb_copy(1024 - SECOND_SHARE, SECOND_SHARE)
         copy_yb(896, 128)
-        copy_yb(1024 - SECOND_SHARE, SECOND_SHARE - 128)
         add_rows(0, 0)
         add_rows(0, 1)
         round_out(0, on_scalar)
-        quantise_h(512, "res0_0")
-        quantise_h(256, "res0_0", 1024)
+        quantise_h(512, "codes")
+        quantise_h(256, "codes", 1024)
         make_y_rows(2, 0, 1)
-        make_y_rows(2, 1, 7)
+        make_y_rows(2, 1, 6)
         make_y_rows(1, 0, 3)
         make_y_rows(1, 1, 4)
-        new_h_bf(768, 256, "res0_2")
+        new_h_bf(768, 256, "h_bf512")
         make_h_gpsimd(1024 - SECOND_SHARE)
         make_h(768, 256 - SECOND_SHARE)
         round_out(1, on_scalar)
@@ -465,18 +469,18 @@ def tile_list_htabg_glu_resP_kernel(
         round_out(4, on_scalar)
         add_rows(1, 0)
         round_out(5, on_scalar)
-        quantise_h(768, "res2_0")
-        make_y_rows(3, 0, 6)
+        quantise_h(768, "codes", 1024)
+        make_y_rows(3, 0, 7)
         make_y_rows(3, 1, 5)
-        new_out_codes(0, 256, "yb_copy%d" % (1024 - SECOND_SHARE))
+        add_rows(1, 1)
+        new_out_codes(0, 256, "h_bf768")
         quantise_out(0, 256)
         store_words(nc.sync, 0)
-        add_rows(1, 1)
         round_out(2, on_scalar)
         add_rows(3, 0)
         round_out(3, on_scalar)
         add_rows(3, 1)
-        new_out_codes(256, 512, "res2_0")
+        new_out_codes(256, 512, "codes", 1024)
         quantise_out(512, 256)
         round_out(6, on_scalar)
         round_out(7, on_vector)

@@ -128,20 +128,16 @@ def tile_list_htabg_glu_resP_kernel(
             wgt_turned = bank_tile("wgt_turned", 0, [P, P])
             nc.tensor.transpose(wgt_turned[:], wgt_rows[:], ident[:])
             by_block = wgt_turned[:, : HEADS * blocks].rearrange("p (g b) -> p b g", b=blocks)
+            shape = [P, CHUNK // P, HEADS, LIST_ROWS]
             banks = []
-            for j0, width in WGT_PIECES:
-                shape = [P, width // P, HEADS, LIST_ROWS]
-                repeated = tile("repeated%d" % j0, shape, "f32")
-                nc.scalar.copy(repeated[:], by_block[:, j0 // P : (j0 + width) // P, :].unsqueeze(3).to_broadcast(shape))
-                bank = bank_tile("wgt_bank%d" % j0, 1 + len(banks), [P, width // P, P])
-                for b in range(width // P):
-                    nc.tensor.transpose(bank[:, b, :], repeated[:, b].rearrange("p g q -> p (g q)"), ident[:])
-                banks.append(bank)
-                if len(banks) > 1:
-                    k0, kw = WGT_PIECES[len(banks) - 2]
-                    nc.scalar.copy(wgt[:, k0 : k0 + kw], banks[-2][:].rearrange("p b j -> p (b j)"))
-            k0, kw = WGT_PIECES[-1]
-            nc.scalar.copy(wgt[:, k0 : k0 + kw], banks[-1][:].rearrange("p b j -> p (b j)"))
+            for c in range(CHUNKS):
+                repeated = tile("repeated%d" % c, shape, "f32")
+                nc.scalar.copy(repeated[:], by_block[:, 2 * c : 2 * c + 2, :].unsqueeze(3).to_broadcast(shape))
+                banks.append(bank_tile("wgt_bank%d" % c, 1 + c, [P, CHUNK // P, P]))
+                for b in range(CHUNK // P):
+                    nc.tensor.transpose(banks[c][:, b, :], repeated[:, b].rearrange("p g q -> p (g q)"), ident[:])
+            for c in range(CHUNKS):
+                nc.scalar.copy(wgt[:, c * CHUNK : (c + 1) * CHUNK], banks[c][:].rearrange("p b j -> p (b j)"))
 
         on_scalar, on_vector = nc.scalar.copy, nc.vector.tensor_copy
 

@@ -33,7 +33,7 @@ CHUNKS = J // CHUNK
 HALF = J // 2
 WGT_PIECES = ((0, 256), (256, 256), (512, 512))
 RES_TILES = (((0, 0), 2, "x_rows2", 0), ((0, 2), 2, "x_rows2", 2048), ((2, 0), 4, "x_rows3", 0), ((1, 0), 4, "x_rows3", 4096), ((3, 0), 4, "wa_bf", 0))
-FIRST_SHARE, SECOND_SHARE = 176, 128
+FIRST_SHARE, SECOND_SHARE = 208, 128
 WA_SCALAR, WB_SCALAR = 64, 48
 
 

@@ -33,7 +33,7 @@ CHUNKS = J // CHUNK
 HALF = J // 2
 WGT_PIECES = ((0, 256), (256, 256), (512, 512))
 RES_TILES = (((0, 0), 2, "x_rows2", 0), ((0, 2), 2, "x_rows2", 2048), ((2, 0), 4, "x_rows3", 0), ((1, 0), 4, "x_rows3", 4096), ((3, 0), 4, "wa_bf", 0))
-FIRST_SHARE, SECOND_SHARE = 208, 128
+FIRST_SHARE, SECOND_SHARE = 208, 160
 WA_SCALAR, WB_SCALAR = 64, 48
 
 
@@ -447,6 +447,7 @@ def tile_list_htabg_glu_resP_kernel(
         make_h(640)
         new_yb_copy(1024 - SECOND_SHARE, SECOND_SHARE)
         copy_yb(896, 128)
+        copy_yb(1024 - SECOND_SHARE, SECOND_SHARE - 128)
         add_rows(0, 0)
         add_rows(0, 1)
         round_out(0, on_scalar)

@@ -18,8 +18,7 @@ FP4X4 = mybir.dt.float4_e2m1fn_x4
 MULT = mybir.AluOpType.mult
 ADD = mybir.AluOpType.add
 SILU = mybir.ActivationFunctionType.Silu
-ITEM_BYTES = {"f32": 4, "bf16": 2, "u32": 4, "u8": 1}
-DTYPES = {"f32": F32, "bf16": BF16, "u32": U32, "u8": U8}
+KINDS = {"f32": (F32, 4), "bf16": (BF16, 2), "u32": (U32, 4), "u8": (U8, 1)}
 
 P = 128
 PACK = 4
@@ -28,13 +27,12 @@ SCALE_ROWS = 16
 LIST_ROWS = 16
 BANK = 512
 BLOCK = BANK // PACK
-CHUNK = 256
+CHUNK = 2 * BLOCK
 CHUNKS = J // CHUNK
 HALF = J // 2
-WGT_PIECES = ((0, 256), (256, 256), (512, 512))
-RES_TILES = (((0, 0), 2, "x_rows2", 0), ((0, 2), 2, "x_rows2", 2048), ((2, 0), 4, "x_rows3", 0), ((1, 0), 4, "x_rows3", 4096), ((3, 0), 4, "wa_bf", 0))
-FIRST_SHARE, SECOND_SHARE = 208, 160
-WA_SCALAR, WB_SCALAR = 64, 48
+LOW, HIGH = slice(0, 2), slice(2, 4)
+WA_SCALAR, WB_SCALAR = 28, 40
+FIRST_SHARE, SECOND_SHARE = 192, 208
 
 
 def tile_list_htabg_glu_resP_kernel(
@@ -48,54 +46,74 @@ def tile_list_htabg_glu_resP_kernel(
         spans = {"end": (0, 0)}
 
         def tile(name, shape, kind, over=None, at=0, room=0):
-            size = ITEM_BYTES[kind]
+            dtype, size = KINDS[kind]
             for extent in shape[1:]:
                 size = size * extent
-            size = max(size, room)
             if over is None:
                 start = spans["end"][0]
-                spans["end"] = (start + (size + 63) // 64 * 64, 0)
+                spans["end"] = (start + (max(size, room) + 63) // 64 * 64, 0)
             else:
                 start = spans[over][0] + at
                 assert at + size <= spans[over][1]
-            spans[name] = (start, size)
-            return sb.tile(shape, DTYPES[kind], name=name, align_bytes=64, offset=start)
+            spans[name] = (start, max(size, room))
+            return sb.tile(shape, dtype, name=name, align_bytes=64, offset=start)
 
-        def reserve(name, size):
+        def tile_room(name, lead, size):
             spans[name] = (spans["end"][0], size)
-            spans["end"] = (spans["end"][0] + size, 0)
+            spans["end"] = (spans["end"][0] + lead, 0)
 
-        def bank_tile(name, bank, shape=(P, PACK, BLOCK)):
+        def bank_tile(name, bank, shape):
             return ps.tile(list(shape), F32, name=name, offset=bank * BANK * 4)
 
         def scale_rows(scale_tile, q):
             return scale_tile[32 * q : 32 * q + 4, :].bitcast(I32)
 
-        def hbm_scale_rows(scales, q):
-            return scales[0, 4 * q : 4 * q + 4, :].bitcast(I32)
+        def places(c):
+            return slice(c * CHUNK, (c + 1) * CHUNK)
 
         tab_list = lists.tile([P, J // LIST_ROWS], U16, name="tab_list")
         head_lists = lists.tile([P, J // LIST_ROWS], U16, name="head_lists")
-        tab_scale_tile = tile("tab_scale_tile", [P, T], "u8")
+        staged = P - SCALE_ROWS
+        tab_staged = tile("tab_staged", [P, T], "u8")
         v_staged = tile("v_staged", [P, J], "u8")
         v_scales = tile("v_scales", [P, J], "u8")
         x_rows = [tile("x_rows%d" % i, [P, T], "f32") for i in range(PACK)]
         wgt = tile("wgt", [P, J], "f32")
-        tab_codes = tile("tab_codes", [P, T], "u32")
-        wa_raw = tile("wa_raw", [P, PACK, R], "f32", room=9216)
-        wb_raw = tile("wb_raw", [P, PACK, R], "f32")
-        wd_raw_scales = tile("wd_raw_scales", [P, N], "u8")
-        wd_raw_codes = tile("wd_raw_codes", [P, 2 * N], "u8", room=2048)
-        blocks = J // P
         wgt_rows = tile("wgt_rows", [P, P], "f32")
         ident = tile("ident", [P, P], "f32")
         warm = tile("warm", [P, 1], "f32")
-        staged = P - SCALE_ROWS
+        tab_codes = tile("tab_codes", [P, T], "u32")
+        wa_raw = tile("wa_raw", [P, PACK, R], "f32")
+        wb_raw = tile("wb_raw", [P, PACK, R], "f32", room=9216)
+        tile_room("wd_room", 768, 2048)
+        wd_raw_codes = tile("wd_raw_codes", [P, 2 * N], "u8", room=2048)
+        wd_raw_scales = tile("wd_raw_scales", [P, N], "u8")
+        wd_codes = tile("wd_codes", [P, 2 * N], "u8")
+        picked = tile("picked", [P, PACK, J], "f32")
+        wa_bf = tile("wa_bf", [P, PACK * R], "bf16")
+        wa_codes = tile("wa_codes", [P, R], "u32")
+        wa_scales = tile("wa_scales", [P, R], "u8")
+        wb_bf = tile("wb_bf", [P, PACK * R], "bf16")
+        wb_codes = tile("wb_codes", [P, R], "u32")
+        wb_scales = tile("wb_scales", [P, R], "u8")
+        h_scales = tile("h_scales", [P, J], "u8")
+        sums = [tile("sums%d" % c, [P, PACK, CHUNK], "f32") for c in range(CHUNKS)]
+        out_bf = tile("out_bf", [P, PACK * J], "bf16")
+        out_scales = tile("out_scales", [P, HALF], "u8")
+        x_bf, x_codes, x_scales, v_codes, gates, ya_banks, yb_banks = {}, {}, {}, {}, {}, {}, {}
+        wd_dealt = {}
+        yb_copies, h_bf, h_codes, y_banks, res_rows, out_codes = {}, {}, {}, {}, {}, {}
 
         x_hbm = xT.rearrange("(p i) t -> p i t", i=PACK)
         res_hbm = res.rearrange("(p t) j -> p t j", t=PACK)
         out_hbm = out_0.rearrange("(p t) j -> p t j", t=PACK)
         out_words_hbm = out_1[0].rearrange("p j i -> p (j i)").bitcast(I32)
+        on_scalar, on_vector = nc.scalar.copy, nc.vector.tensor_copy
+        blocks = J // P
+
+        def within(tiles, j0):
+            first = max(k for k in tiles if k <= j0)
+            return tiles[first], j0 - first
 
         def load_x(i):
             nc.sync.dma_start(x_rows[i][:], x_hbm[:, i, :])
@@ -103,31 +121,27 @@ def tile_list_htabg_glu_resP_kernel(
         def load_weight(raw, w):
             nc.sync.dma_start(raw[:], w.rearrange("(p i) r -> p i r", i=PACK))
 
-        def load_res(c, row):
-            rows = res_tiles[c, row].shape[1]
-            nc.sync.dma_start(res_tiles[c, row][:], res_hbm[:, row : row + rows, c * CHUNK : (c + 1) * CHUNK])
-
-        def load_tab():
-            nc.sync.dma_start(tab_codes[:].bitcast(I32), tab_words[0].rearrange("p t i -> p (t i)").bitcast(I32))
-
-        def load_wd_codes(queue):
-            queue.dma_start(wd_raw_codes[:].bitcast(I32), wd_words[0].bitcast(I32))
-
-        def load_wd_scales(queue):
+        def load_wd():
+            nc.sync.dma_start(wd_raw_codes[:].bitcast(I32), wd_words[0].bitcast(I32))
             for q in range(QUADRANTS):
-                queue.dma_start(scale_rows(wd_raw_scales, q), hbm_scale_rows(wd_scales, q))
-
-        def load_wgt(queue):
-            queue.dma_start(wgt_rows[: HEADS * blocks, :], wgt2.rearrange("(g q) (b j) -> q g b j", q=LIST_ROWS, j=P)[0])
+                nc.sync.dma_start(scale_rows(wd_raw_scales, q), wd_scales[0, 4 * q : 4 * q + 4, :].bitcast(I32))
 
         def carry_v_scales():
             for q in range(QUADRANTS):
                 nc.sync.dma_start(scale_rows(v_scales, q), v_staged[staged + 4 * q : staged + 4 * q + 4, :].bitcast(I32))
 
+        def load_res(c, row, rows, over, at):
+            res_rows[c, row] = tile("res%d_%d" % (c, row), [P, rows, CHUNK], "f32", over, at)
+            nc.sync.dma_start(res_rows[c, row][:], res_hbm[:, row : row + rows, places(c)])
+
+        def res_pair(c, u):
+            row = max(r for k, r in res_rows if k == c and r <= 2 * u)
+            return res_rows[c, row][:, 2 * u - row : 2 * u - row + 2, :]
+
         def spread_wgt():
-            wgt_turned = bank_tile("wgt_turned", 0, [P, P])
-            nc.tensor.transpose(wgt_turned[:], wgt_rows[:], ident[:])
-            by_block = wgt_turned[:, : HEADS * blocks].rearrange("p (g b) -> p b g", b=blocks)
+            turned = bank_tile("wgt_turned", 0, [P, P])
+            nc.tensor.transpose(turned[:], wgt_rows[:], ident[:])
+            by_block = turned[:, : HEADS * blocks].rearrange("p (g b) -> p b g", b=blocks)
             shape = [P, CHUNK // P, HEADS, LIST_ROWS]
             banks = []
             for c in range(CHUNKS):
@@ -137,43 +151,7 @@ def tile_list_htabg_glu_resP_kernel(
                 for b in range(CHUNK // P):
                     nc.tensor.transpose(banks[c][:, b, :], repeated[:, b].rearrange("p g q -> p (g q)"), ident[:])
             for c in range(CHUNKS):
-                nc.scalar.copy(wgt[:, c * CHUNK : (c + 1) * CHUNK], banks[c][:].rearrange("p b j -> p (b j)"))
-
-        on_scalar, on_vector = nc.scalar.copy, nc.vector.tensor_copy
-
-        def on_gpsimd(dst, src):
-            nc.gpsimd.tensor_scalar(dst, src, 1.0, 0.0, MULT, ADD)
-
-        wd_dealt = {}
-        picked = tile("picked", [P, PACK, J], "f32")
-        out_scales = tile("out_scales", [P, J], "u8")
-        x_scales = {}
-        h_scales = tile("h_scales", [P, J], "u8")
-        wa_bf = tile("wa_bf", [P, PACK * R], "bf16")
-        wa_codes = tile("wa_codes", [P, R], "u32")
-        wa_scales = tile("wa_scales", [P, R], "u8")
-        wb_bf = tile("wb_bf", [P, PACK * R], "bf16")
-        wb_codes = tile("wb_codes", [P, R], "u32")
-        wb_scales = tile("wb_scales", [P, R], "u8")
-        res_tiles = {key: tile("res%d_%d" % key, [P, rows, CHUNK], "f32", over, at) for key, rows, over, at in RES_TILES}
-        sums = [tile("sums%d" % c, [P, PACK, CHUNK], "f32") for c in range(CHUNKS)]
-        out_bf = tile("out_bf", [P, PACK * J], "bf16")
-        h_codes, ya_banks = {}, {}
-        x_bf, x_codes, v_codes, h_bf, gates, yb_copies, out_codes, yb_banks, y_banks = {}, {}, {}, {}, {}, {}, {}, {}, {}
-
-        def deal_wd_codes(copy, over=None, at=0):
-            wd_dealt["codes"] = tile("wd_codes", [P, 2 * N], "u8", over, at)
-            copy(
-                wd_dealt["codes"][:].bitcast(U16).rearrange("p (t m) -> p t m", t=PACK),
-                wd_raw_codes[:].bitcast(U16).rearrange("p (m t) -> p t m", t=PACK),
-            )
-
-        def deal_wd_scales(copy, over=None, at=0):
-            wd_dealt["scales"] = tile("wd_dealt_scales", [P, N], "u8", over, at)
-            copy(
-                wd_dealt["scales"][:].rearrange("p (t m) -> p t m", t=PACK),
-                wd_raw_scales[:].rearrange("p (m t) -> p t m", t=PACK),
-            )
+                nc.scalar.copy(wgt[:, places(c)], banks[c][:].rearrange("p b j -> p (b j)"))
 
         def gather_x(i, j0, width):
             nc.vector.tensor_tensor(
@@ -183,17 +161,29 @@ def tile_list_htabg_glu_resP_kernel(
                 MULT,
             )
 
-        def gather_v(first, chunks, over=None, at=0):
+        def gather_v(first, chunks, over, at):
             codes = tile("v_codes%d" % first, [P, chunks * CHUNK], "u32", over, at)
             entries = slice(first * CHUNK // LIST_ROWS, (first + chunks) * CHUNK // LIST_ROWS)
             nc.vector.tensor_copy(codes[:], tab_codes[:].indirect(tab_list[:, entries]))
-            for k in range(chunks):
-                v_codes[first + k] = codes[:, k * CHUNK : (k + 1) * CHUNK]
+            v_codes[first * CHUNK] = codes
 
         def round_weight(copy, bf, raw, m0, m1):
             src = raw[:].rearrange("p i (m t) -> p m i t", t=PACK)[:, m0:m1]
             dst = bf[:].rearrange("p (t m i) -> p m i t", t=PACK, i=PACK)[:, m0:m1]
             copy(dst, src)
+
+        def deal_wd_codes(copy):
+            copy(
+                wd_codes[:].bitcast(U16).rearrange("p (t m) -> p t m", t=PACK),
+                wd_raw_codes[:].bitcast(U16).rearrange("p (m t) -> p t m", t=PACK),
+            )
+
+        def deal_wd_scales(copy, over):
+            wd_dealt["scales"] = tile("wd_dealt_scales", [P, N], "u8", over)
+            copy(
+                wd_dealt["scales"][:].rearrange("p (t m) -> p t m", t=PACK),
+                wd_raw_scales[:].rearrange("p (m t) -> p t m", t=PACK),
+            )
 
         def quantise(codes, scales, src):
             nc.vector.quantize_mx(codes.bitcast(FP8X4), scales, src)
@@ -207,30 +197,18 @@ def tile_list_htabg_glu_resP_kernel(
         def new_x_bf(c, over=None, at=0):
             x_bf[c] = tile("x_bf%d" % c, [P, PACK * CHUNK], "bf16", over, at)
 
-        def round_x(c, copy, rows=slice(0, PACK), first=0, width=CHUNK):
-            j0 = c * CHUNK + first
-            round_into_words(copy, x_bf[c][:, PACK * first : PACK * (first + width)], picked[:, :, j0 : j0 + width], rows)
+        def round_x(c, rows=slice(0, PACK)):
+            round_into_words(on_scalar, x_bf[c][:], picked[:, :, places(c)], rows)
 
-        def round_x_gpsimd(c, first=0, width=CHUNK):
-            j0 = c * CHUNK + first
-            on_gpsimd(
-                x_bf[c][:, PACK * first : PACK * (first + width)].rearrange("p (j i) -> p j i", i=PACK),
-                picked[:, :, j0 : j0 + width].rearrange("p i j -> p j i"),
+        def round_x_gpsimd(c):
+            nc.gpsimd.tensor_scalar(
+                x_bf[c][:].rearrange("p (j i) -> p j i", i=PACK), picked[:, :, places(c)].rearrange("p i j -> p j i"), 1.0, 0.0, MULT, ADD
             )
 
         def quantise_x(c, over=None, at=0):
             x_codes[c] = tile("x_codes%d" % c, [P, CHUNK], "u32")
             x_scales[c] = tile("x_scales%d" % c, [P, CHUNK], "u8", over, at)
             quantise(x_codes[c][:], x_scales[c][:], x_bf[c][:])
-
-        def group_of(tiles, j0):
-            first = max(k for k in tiles if k <= j0)
-            return tiles[first], j0 - first
-
-        def quantise_h(first, over=None, at=0):
-            width = h_bf[first].shape[1] // PACK
-            h_codes[first] = tile("h_codes%d" % first, [P, width], "u32", over, at)
-            quantise(h_codes[first][:], h_scales[:, first : first + width], h_bf[first][:])
 
         def product(bank, codes, scales, fmt, moving_codes, moving_scales, rows=range(PACK)):
             width = codes.shape[1] // PACK
@@ -245,99 +223,64 @@ def tile_list_htabg_glu_resP_kernel(
                     stop=True,
                 )
 
-        def new_gates(first, width, over=None, at=0):
-            gates[first] = tile("gates%d" % first, [P, width, PACK], "f32", over, at)
-
-        def gate_places(j0, width):
-            group, at = group_of(gates, j0)
-            return group[:, at : at + width, :]
-
         def make_ya(b, bank):
             c, at = divmod(b * BLOCK, CHUNK)
-            ya_banks[b] = bank_tile("ya%d" % b, bank)
+            ya_banks[b] = bank_tile("ya%d" % b, bank, (P, PACK, BLOCK))
             product(ya_banks[b], wa_codes[:], wa_scales, FP8X4, x_codes[c][:, at : at + BLOCK], x_scales[c][:, at : at + BLOCK])
 
-        def apply_silu(b):
-            nc.scalar.activation(gate_places(b * BLOCK, BLOCK), ya_banks[b][:].rearrange("p t n -> p n t"), SILU)
-
-        def make_gate(b, bank):
-            make_ya(b, bank)
-            apply_silu(b)
-
         def make_yb(b, bank):
-            c, at = divmod(b * BLOCK, CHUNK)
-            yb = bank_tile("yb%d" % b, bank)
-            product(yb, wb_codes[:], wb_scales, FP8X4, v_codes[c][:, at : at + BLOCK], v_scales[:, b * BLOCK : (b + 1) * BLOCK])
+            codes, at = within(v_codes, b * BLOCK)
+            yb = bank_tile("yb%d" % b, bank, (P, PACK, BLOCK))
+            product(yb, wb_codes[:], wb_scales, FP8X4, codes[:, at : at + BLOCK], v_scales[:, b * BLOCK : (b + 1) * BLOCK])
             yb_banks[b] = yb[:].rearrange("p t n -> p n t")
 
-        def yb_places(j0, width):
+        def new_group(group, name, first, width, kind, over=None, at=0, room=0):
+            group[first] = tile("%s%d" % (name, first), [P, width, PACK], kind, over, at, room)
+
+        def part(group, j0, width):
+            whole, at = within(group, j0)
+            return whole[:, at : at + width, :]
+
+        def yb_part(j0, width):
             b, at = divmod(j0, BLOCK)
             return yb_banks[b][:, at : at + width, :]
 
-        def new_h_bf(first, width, over=None, at=0):
-            h_bf[first] = tile("h_bf%d" % first, [P, PACK * width], "bf16", over, at)
+        def apply_silu(b):
+            nc.scalar.activation(part(gates, b * BLOCK, BLOCK), ya_banks[b][:].rearrange("p t n -> p n t"), SILU)
 
-        def h_places(j0, width):
-            group, at = group_of(h_bf, j0)
-            return group[:, PACK * at : PACK * (at + width)].rearrange("p (n t) -> p n t", t=PACK)
+        def copy_yb(j0, width=BLOCK):
+            nc.scalar.copy(part(yb_copies, j0, width), yb_part(j0, width))
 
         def make_h(j0, width=BLOCK):
-            nc.vector.tensor_tensor(h_places(j0, width), gate_places(j0, width), yb_places(j0, width), MULT)
+            nc.vector.tensor_tensor(part(h_bf, j0, width), part(gates, j0, width), yb_part(j0, width), MULT)
 
-        def new_yb_copy(first, width, over=None, at=0):
-            yb_copies[first] = tile("yb_copy%d" % first, [P, width, PACK], "f32", over, at)
+        def make_h_gpsimd(j0, width):
+            nc.gpsimd.tensor_tensor(part(h_bf, j0, width), part(gates, j0, width), part(yb_copies, j0, width), MULT)
 
-        def copy_yb(j0, width):
-            group, at = group_of(yb_copies, j0)
-            nc.scalar.copy(group[:, at : at + width, :], yb_places(j0, width))
+        def quantise_h(c, over=None, at=0, room=0):
+            h_codes[c] = tile("h_codes%d" % c, [P, CHUNK], "u32", over, at, room)
+            quantise(h_codes[c][:], h_scales[:, places(c)], part(h_bf, c * CHUNK, CHUNK).rearrange("p n t -> p (n t)"))
 
-        def make_h_gpsimd(first):
-            width = yb_copies[first].shape[1]
-            nc.gpsimd.tensor_tensor(h_places(first, width), gate_places(first, width), yb_copies[first][:], MULT)
-
-        def make_y(b, bank):
-            places = slice(b * BLOCK, (b + 1) * BLOCK)
-            codes, at = group_of(h_codes, b * BLOCK)
-            y_banks[b] = bank_tile("y%d" % b, bank)
-            product(y_banks[b], wd_dealt["codes"][:], wd_dealt["scales"], FP4X4, codes[:, at : at + BLOCK], h_scales[:, places])
-
-        def make_y_rows(c, u, bank):
+        def make_y(c, u, bank):
             y_banks[c, u] = bank_tile("y%d_%d" % (c, u), bank, (P, 2, CHUNK))
-            scales = h_scales[:, c * CHUNK : (c + 1) * CHUNK]
-            product(y_banks[c, u], wd_dealt["codes"][:], wd_dealt["scales"], FP4X4, h_codes[c * CHUNK][:], scales, range(2 * u, 2 * u + 2))
+            product(y_banks[c, u], wd_codes[:], wd_dealt["scales"], FP4X4, h_codes[c][:], h_scales[:, places(c)], range(2 * u, 2 * u + 2))
 
-        def add_rows(c, u):
+        def add_res(c, u):
             rows = slice(2 * u, 2 * u + 2)
-            nc.vector.tensor_tensor(sums[c][:, rows, :], y_banks[c, u][:], res_rows(c, u), ADD)
-            nc.sync.dma_start(out_hbm[:, rows, c * CHUNK : (c + 1) * CHUNK], sums[c][:, rows, :])
+            nc.vector.tensor_tensor(sums[c][:, rows, :], y_banks[c, u][:], res_pair(c, u), ADD)
+            nc.sync.dma_start(out_hbm[:, rows, places(c)], sums[c][:, rows, :])
 
-        def res_rows(c, u):
-            row = max(r for k, r in res_tiles if k == c and r <= 2 * u)
-            return res_tiles[c, row][:, 2 * u - row : 2 * u - row + 2, :]
-
-        def sums_block(b):
+        def round_out(b, copy):
             c, at = divmod(b * BLOCK, CHUNK)
-            return sums[c][:, :, at : at + BLOCK]
-
-        def add_res(b):
-            nc.vector.tensor_tensor(sums_block(b), y_banks[b][:], res_tiles[b // 2, 0][:, :, b % 2 * BLOCK : (b % 2 + 1) * BLOCK], ADD)
-
-        def store_block(b):
-            nc.sync.dma_start(out_hbm[:, :, b * BLOCK : (b + 1) * BLOCK], sums_block(b))
-
-        def store_chunk(c):
-            nc.sync.dma_start(out_hbm[:, :, c * CHUNK : (c + 1) * CHUNK], sums[c][:])
-
-        def round_out(b, copy, first=0, width=BLOCK):
-            j0 = b * BLOCK + first
-            round_into_words(copy, out_bf[:, PACK * j0 : PACK * (j0 + width)], sums_block(b)[:, :, first : first + width])
+            round_into_words(copy, out_bf[:, PACK * b * BLOCK : PACK * (b + 1) * BLOCK], sums[c][:, :, at : at + BLOCK])
 
         def new_out_codes(j0, width, over=None, at=0):
             out_codes[j0] = tile("out_codes%d" % j0, [P, width], "u32", over, at)
 
         def quantise_out(j0, width):
-            codes, at = group_of(out_codes, j0)
-            quantise(codes[:, at : at + width], out_scales[:, j0 : j0 + width], out_bf[:, PACK * j0 : PACK * (j0 + width)])
+            codes, at = within(out_codes, j0)
+            half, column = divmod(j0, HALF)
+            quantise(codes[:, at : at + width], out_scales[4 * half :, column : column + width], out_bf[:, PACK * j0 : PACK * (j0 + width)])
 
         def store_words(queue, first):
             codes = out_codes[first]
@@ -346,145 +289,152 @@ def tile_list_htabg_glu_resP_kernel(
         def store_scales():
             for q in range(QUADRANTS):
                 queue = nc.sync if q < QUADRANTS // 2 else nc.scalar
-                queue.dma_start(hbm_scale_rows(out_2, q), scale_rows(out_scales, q))
-
+                rows = out_2[0, 4 * q : 4 * q + 4, :].bitcast(I32).rearrange("r (half w) -> half r w", half=2)
+                queue.dma_start(rows, out_scales[32 * q : 32 * q + 8, :].bitcast(I32))
 
         nc.sync.dma_start(tab_list[:], offs)
-        nc.sync.dma_start(tab_scale_tile[staged:, :].bitcast(I32), tab_scales[0].bitcast(I32))
-        load_wgt(nc.scalar)
+        nc.sync.dma_start(tab_staged[staged:, :].bitcast(I32), tab_scales[0].bitcast(I32))
+        nc.scalar.dma_start(wgt_rows[: HEADS * blocks, :], wgt2.rearrange("(g q) (b j) -> q g b j", q=LIST_ROWS, j=P)[0])
         load_x(0)
         nc.vector.memset(wd_raw_scales[:].bitcast(I32), 0)
         nc.vector.memset(wgt_rows[HEADS * blocks :, :], 0.0)
-        nc.vector.memset(tab_scale_tile[:staged, :].bitcast(I32), 0)
+        nc.vector.memset(tab_staged[:staged, :].bitcast(I32), 0)
         nc.vector.memset(v_scales[:].bitcast(I32), 0)
         make_identity(nc, ident[:])
         nc.scalar.activation(warm[:], ident[:, 0:1], SILU)
         nc.sync.dma_start(head_lists[:], offs2)
-        load_x(1)
-        load_x(2)
-        load_x(3)
-        nc.vector.tensor_copy(v_staged[:], tab_scale_tile[:].indirect(tab_list[:]))
-
+        for i in range(1, PACK):
+            load_x(i)
+        nc.vector.tensor_copy(v_staged[:], tab_staged[:].indirect(tab_list[:]))
         load_weight(wa_raw, wa)
-        load_tab()
+        nc.sync.dma_start(tab_codes[:].bitcast(I32), tab_words[0].rearrange("p t i -> p (t i)").bitcast(I32))
         load_weight(wb_raw, wb)
-        load_wd_codes(nc.sync)
-        load_wd_scales(nc.sync)
+        load_wd()
         carry_v_scales()
         spread_wgt()
-        for j0, width in WGT_PIECES:
-            gather_x(0, j0, width)
+
+        gather_x(0, 0, CHUNK)
+        gather_x(0, CHUNK, CHUNK)
+        gather_x(0, HALF, HALF)
         gather_x(1, 0, J)
         new_x_bf(0)
-        round_x(0, on_scalar, slice(0, 2))
+        round_x(0, LOW)
         gather_x(2, 0, J)
-        load_res(0, 0)
-        load_res(0, 2)
+        load_res(0, 0, 2, "x_rows2", 0)
+        load_res(0, 2, 2, "x_rows2", 2048)
+        load_res(1, 0, 4, "x_rows2", 4096)
         gather_x(3, 0, CHUNK)
-        gather_x(3, CHUNK, J - CHUNK)
-        load_res(2, 0)
-        load_res(1, 0)
-        round_x(0, on_scalar, slice(2, PACK))
+        round_x(0, HIGH)
+        gather_x(3, CHUNK, CHUNK)
+        new_x_bf(1)
+        round_x(1)
+        gather_x(3, HALF, HALF)
+        load_res(2, 0, 4, "x_rows3", 0)
+        load_res(3, 0, 4, "x_rows3", 4096)
         quantise_x(0)
         round_weight(on_scalar, wa_bf, wa_raw, 0, WA_SCALAR)
         round_weight(on_vector, wa_bf, wa_raw, WA_SCALAR, P)
-        quantise(wa_codes[:], wa_scales[:], wa_bf[:])
-        load_res(3, 0)
-        new_x_bf(3, "wa_raw", 4096)
-        round_x_gpsimd(3)
-        new_x_bf(1, "wa_raw")
-        round_x(1, on_scalar)
-        new_x_bf(2, "wa_raw", 2048)
-        round_x(2, on_scalar)
-        gather_v(0, 3, "wa_raw", 6144)
-        new_gates(0, 128)
-        make_gate(0, 0)
         quantise_x(1)
+        quantise(wa_codes[:], wa_scales[:], wa_bf[:])
+        new_x_bf(3, "wa_raw", 0)
+        round_x_gpsimd(3)
+        new_x_bf(2, "wa_raw", 2048)
+        round_x(2)
+        gather_v(0, 3, "wa_raw", 4096)
+        new_group(gates, "gates", 0, BLOCK, "f32")
+        tile_room("behind_h1", 1536, 5120)
+        new_group(gates, "gates", 128, BLOCK, "f32", room=3584)
+        for b in (0, 1):
+            make_ya(b, b)
+            apply_silu(b)
+        make_ya(2, 2)
+        make_ya(3, 3)
         quantise_x(2)
+        make_ya(5, 5)
+        make_ya(4, 4)
         round_weight(on_scalar, wb_bf, wb_raw, 0, WB_SCALAR)
         round_weight(on_vector, wb_bf, wb_raw, WB_SCALAR, P)
-        new_gates(128, 128, "wb_raw", 6144)
-        make_gate(1, 1)
-        new_gates(256, 256, "wb_raw")
-        make_gate(2, 2)
-        make_gate(3, 3)
-        new_gates(512, 128, "wb_raw", 4096)
-        make_gate(4, 7)
-        make_ya(5, 0)
         deal_wd_codes(on_vector)
         quantise(wb_codes[:], wb_scales[:], wb_bf[:])
-        quantise_x(3, "wd_raw_codes")
-        gather_v(3, 1, "wd_raw_codes", 256)
-        make_yb(0, 4)
-        make_yb(1, 6)
-        make_yb(3, 5)
-        make_yb(2, 1)
-        make_yb(4, 2)
-        new_h_bf(0, 256)
-        make_h(0)
-        new_yb_copy(512 - FIRST_SHARE, FIRST_SHARE)
-        copy_yb(384, 128)
-        copy_yb(512 - FIRST_SHARE, FIRST_SHARE - 128)
-        make_h(128)
-        make_yb(5, 3)
-        new_gates(640, 128, "gates128")
+        quantise_x(3, "wd_raw_codes", 768)
+        gather_v(3, 1, "wd_room", 0)
+        new_group(gates, "gates", 512, CHUNK, "f32", "wb_raw", 0)
+        new_group(gates, "gates", 256, BLOCK, "f32", "wb_raw", 4096)
+        new_group(yb_copies, "yb_copy", 768 - FIRST_SHARE, FIRST_SHARE, "f32")
+        apply_silu(2)
         apply_silu(5)
+        apply_silu(4)
+        make_yb(0, 6)
+        make_yb(5, 7)
+        make_yb(1, 0)
+        make_yb(4, 1)
+        make_yb(2, 5)
+        make_yb(3, 2)
+        copy_yb(640)
+        copy_yb(768 - FIRST_SHARE, FIRST_SHARE - BLOCK)
+        new_group(h_bf, "h_bf", 0, CHUNK, "bf16")
+        new_group(h_bf, "h_bf", 256, CHUNK, "bf16")
+        make_h(0)
+        make_yb(7, 4)
+        make_ya(7, 6)
+        make_h(128)
+        make_ya(6, 0)
+        new_group(gates, "gates", 384, BLOCK, "f32", "behind_h1")
+        apply_silu(3)
         deal_wd_scales(on_vector, "gates0")
-        reserve("codes", 3072)
+        tile_room("codes", 3072, 3072)
         quantise_h(0, "codes", 512)
-        new_gates(768, 256)
-        make_gate(7, 4)
-        make_gate(6, 6)
-        make_y_rows(0, 0, 7)
-        make_y_rows(0, 1, 5)
-        new_h_bf(256, 256)
-        make_h_gpsimd(512 - FIRST_SHARE)
-        new_h_bf(512, 256)
-        make_h(512)
-        make_h(256, 256 - FIRST_SHARE)
-        make_yb(7, 0)
-        make_yb(6, 2)
-        make_h(640)
-        new_yb_copy(1024 - SECOND_SHARE, SECOND_SHARE)
-        copy_yb(896, 128)
-        copy_yb(1024 - SECOND_SHARE, SECOND_SHARE - 128)
-        add_rows(0, 0)
-        add_rows(0, 1)
+        new_group(h_bf, "h_bf", 512, CHUNK, "bf16", "behind_h1", 3072)
+        make_h_gpsimd(768 - FIRST_SHARE, FIRST_SHARE)
+        new_group(gates, "gates", 768, CHUNK, "f32")
+        apply_silu(7)
+        apply_silu(6)
+        make_y(0, 0, 7)
+        make_yb(6, 3)
+        new_group(yb_copies, "yb_copy", J - SECOND_SHARE, SECOND_SHARE, "f32")
+        copy_yb(896)
+        copy_yb(J - SECOND_SHARE, SECOND_SHARE - BLOCK)
+        make_h(256)
+        make_y(0, 1, 5)
+        make_h(512, CHUNK - FIRST_SHARE)
+        make_h(384)
+        add_res(0, 0)
+        quantise_h(1, "codes")
+        quantise_h(2, "codes", 1024)
+        new_group(h_bf, "h_bf", 768, CHUNK, "bf16", "h_bf256")
+        make_h_gpsimd(J - SECOND_SHARE, SECOND_SHARE)
+        make_y(1, 0, 1)
+        make_y(1, 1, 6)
+        make_y(2, 0, 2)
+        make_y(2, 1, 0)
+        add_res(0, 1)
         round_out(0, on_scalar)
-        quantise_h(512, "codes")
-        quantise_h(256, "codes", 1024)
-        make_y_rows(2, 0, 1)
-        make_y_rows(2, 1, 6)
-        make_y_rows(1, 0, 3)
-        make_y_rows(1, 1, 4)
-        new_h_bf(768, 256, "h_bf512")
-        make_h_gpsimd(1024 - SECOND_SHARE)
-        make_h(768, 256 - SECOND_SHARE)
         round_out(1, on_scalar)
-        add_rows(2, 0)
-        add_rows(2, 1)
-        round_out(4, on_scalar)
-        add_rows(1, 0)
-        round_out(5, on_scalar)
-        quantise_h(768, "codes", 1024)
-        make_y_rows(3, 0, 7)
-        make_y_rows(3, 1, 5)
-        add_rows(1, 1)
-        new_out_codes(0, 256, "h_bf768")
-        quantise_out(0, 256)
-        store_words(nc.sync, 0)
+        make_h(768, CHUNK - SECOND_SHARE)
+        add_res(1, 0)
+        add_res(1, 1)
         round_out(2, on_scalar)
-        add_rows(3, 0)
         round_out(3, on_scalar)
-        add_rows(3, 1)
-        new_out_codes(256, 512, "codes", 1024)
-        quantise_out(512, 256)
+        add_res(2, 0)
+        quantise_h(3, "codes", 1024)
+        make_y(3, 0, 7)
+        make_y(3, 1, 4)
+        add_res(2, 1)
+        round_out(4, on_scalar)
+        round_out(5, on_scalar)
+        new_out_codes(0, CHUNK, "h_bf768")
+        quantise_out(0, CHUNK)
+        store_words(nc.sync, 0)
+        add_res(3, 0)
+        add_res(3, 1)
         round_out(6, on_scalar)
+        new_out_codes(256, HALF, "codes", 1024)
+        quantise_out(256, CHUNK)
         round_out(7, on_vector)
-        quantise_out(256, 256)
+        quantise_out(512, CHUNK)
         store_words(nc.sync, 256)
-        new_out_codes(768, 256)
-        quantise_out(896, 128)
-        quantise_out(768, 128)
+        new_out_codes(768, CHUNK)
+        quantise_out(896, BLOCK)
+        quantise_out(768, BLOCK)
         store_words(nc.scalar, 768)
         store_scales()

@@ -30,6 +30,7 @@ BLOCK = BANK // PACK
 CHUNK = 2 * BLOCK
 CHUNKS = J // CHUNK
 HALF = J // 2
+LAST_SCALAR = 96
 LOW, HIGH = slice(0, 2), slice(2, 4)
 WA_SCALAR, WB_SCALAR = 28, 40
 FIRST_SHARE, SECOND_SHARE = 192, 208
@@ -270,9 +271,10 @@ def tile_list_htabg_glu_resP_kernel(
             nc.vector.tensor_tensor(sums[c][:, rows, :], y_banks[c, u][:], res_pair(c, u), ADD)
             nc.sync.dma_start(out_hbm[:, rows, places(c)], sums[c][:, rows, :])
 
-        def round_out(b, copy):
-            c, at = divmod(b * BLOCK, CHUNK)
-            round_into_words(copy, out_bf[:, PACK * b * BLOCK : PACK * (b + 1) * BLOCK], sums[c][:, :, at : at + BLOCK])
+        def round_out(b, copy, first=0, width=BLOCK):
+            c, at = divmod(b * BLOCK + first, CHUNK)
+            j0 = b * BLOCK + first
+            round_into_words(copy, out_bf[:, PACK * j0 : PACK * (j0 + width)], sums[c][:, :, at : at + width])
 
         def new_out_codes(j0, width, over=None, at=0):
             out_codes[j0] = tile("out_codes%d" % j0, [P, width], "u32", over, at)
@@ -422,19 +424,17 @@ def tile_list_htabg_glu_resP_kernel(
         add_res(2, 1)
         round_out(4, on_scalar)
         round_out(5, on_scalar)
-        new_out_codes(0, CHUNK, "h_bf768")
+        new_out_codes(0, HALF, "h_bf768")
         quantise_out(0, CHUNK)
-        store_words(nc.sync, 0)
         add_res(3, 0)
         add_res(3, 1)
-        round_out(6, on_scalar)
-        new_out_codes(256, HALF, "codes", 1024)
+        round_out(6, on_scalar, 0, LAST_SCALAR)
         quantise_out(256, CHUNK)
-        round_out(7, on_vector)
+        store_words(nc.sync, 0)
+        new_out_codes(HALF, HALF, "codes", 1024)
+        round_out(6, on_vector, LAST_SCALAR, CHUNK - LAST_SCALAR)
         quantise_out(512, CHUNK)
-        store_words(nc.sync, 256)
-        new_out_codes(768, CHUNK)
         quantise_out(896, BLOCK)
         quantise_out(768, BLOCK)
-        store_words(nc.scalar, 768)
+        store_words(nc.scalar, HALF)
         store_scales()

@@ -32,7 +32,7 @@ CHUNKS = J // CHUNK
 HALF = J // 2
 LAST_SCALAR = 96
 LOW, HIGH = slice(0, 2), slice(2, 4)
-WA_SCALAR, WB_SCALAR = 28, 40
+WA_SCALAR, WB_SCALAR = 38, 40
 FIRST_SHARE, SECOND_SHARE = 192, 208
 
 
@@ -142,7 +142,7 @@ def tile_list_htabg_glu_resP_kernel(
         def spread_wgt():
             turned = bank_tile("wgt_turned", 0, [P, P])
             nc.tensor.transpose(turned[:], wgt_rows[:], ident[:])
-            by_block = turned[:, : HEADS * blocks].rearrange("p (g b) -> p b g", b=blocks)
+            by_block = turned[:, 32 : 32 + HEADS * blocks].rearrange("p (g b) -> p b g", b=blocks)
             shape = [P, CHUNK // P, HEADS, LIST_ROWS]
             banks = []
             for c in range(CHUNKS):
@@ -198,8 +198,9 @@ def tile_list_htabg_glu_resP_kernel(
         def new_x_bf(c, over=None, at=0):
             x_bf[c] = tile("x_bf%d" % c, [P, PACK * CHUNK], "bf16", over, at)
 
-        def round_x(c, rows=slice(0, PACK)):
-            round_into_words(on_scalar, x_bf[c][:], picked[:, :, places(c)], rows)
+        def round_x(c, first=0, width=CHUNK):
+            j0 = c * CHUNK + first
+            round_into_words(on_scalar, x_bf[c][:, PACK * first : PACK * (first + width)], picked[:, :, j0 : j0 + width])
 
         def round_x_gpsimd(c):
             nc.gpsimd.tensor_scalar(
@@ -296,10 +297,11 @@ def tile_list_htabg_glu_resP_kernel(
 
         nc.sync.dma_start(tab_list[:], offs)
         nc.sync.dma_start(tab_staged[staged:, :].bitcast(I32), tab_scales[0].bitcast(I32))
-        nc.scalar.dma_start(wgt_rows[: HEADS * blocks, :], wgt2.rearrange("(g q) (b j) -> q g b j", q=LIST_ROWS, j=P)[0])
+        nc.scalar.dma_start(wgt_rows[32 : 32 + HEADS * blocks, :], wgt2.rearrange("(g q) (b j) -> q g b j", q=LIST_ROWS, j=P)[0])
         load_x(0)
         nc.vector.memset(wd_raw_scales[:].bitcast(I32), 0)
-        nc.vector.memset(wgt_rows[HEADS * blocks :, :], 0.0)
+        nc.vector.memset(wgt_rows[:32, :], 0.0)
+        nc.vector.memset(wgt_rows[32 + HEADS * blocks :, :], 0.0)
         nc.vector.memset(tab_staged[:staged, :].bitcast(I32), 0)
         nc.vector.memset(v_scales[:].bitcast(I32), 0)
         make_identity(nc, ident[:])
@@ -319,14 +321,14 @@ def tile_list_htabg_glu_resP_kernel(
         gather_x(0, CHUNK, CHUNK)
         gather_x(0, HALF, HALF)
         gather_x(1, 0, J)
-        new_x_bf(0)
-        round_x(0, LOW)
         gather_x(2, 0, J)
         load_res(0, 0, 2, "x_rows2", 0)
         load_res(0, 2, 2, "x_rows2", 2048)
         load_res(1, 0, 4, "x_rows2", 4096)
-        gather_x(3, 0, CHUNK)
-        round_x(0, HIGH)
+        new_x_bf(0)
+        for first in (0, BLOCK):
+            gather_x(3, first, BLOCK)
+            round_x(0, first, BLOCK)
         gather_x(3, CHUNK, CHUNK)
         new_x_bf(1)
         round_x(1)

@@ -32,7 +32,7 @@ CHUNKS = J // CHUNK
 HALF = J // 2
 LAST_SCALAR = 96
 LOW, HIGH = slice(0, 2), slice(2, 4)
-WA_SCALAR, WB_SCALAR = 38, 40
+WA_SCALAR, WB_SCALAR = 88, 64
 FIRST_SHARE, SECOND_SHARE = 192, 208
 
 
@@ -86,15 +86,13 @@ def tile_list_htabg_glu_resP_kernel(
         tab_codes = tile("tab_codes", [P, T], "u32")
         wa_raw = tile("wa_raw", [P, PACK, R], "f32")
         wb_raw = tile("wb_raw", [P, PACK, R], "f32", room=9216)
-        tile_room("wd_room", 768, 2048)
-        wd_raw_codes = tile("wd_raw_codes", [P, 2 * N], "u8", room=2048)
+        wd_raw_codes = tile("wd_raw_codes", [P, 2 * N], "u8")
         wd_raw_scales = tile("wd_raw_scales", [P, N], "u8")
-        wd_codes = tile("wd_codes", [P, 2 * N], "u8")
         picked = tile("picked", [P, PACK, J], "f32")
-        wa_bf = tile("wa_bf", [P, PACK * R], "bf16")
+        wa_bf = [tile("wa_bf%d" % u, [P, 2 * R], "bf16") for u in range(2)]
         wa_codes = tile("wa_codes", [P, R], "u32")
         wa_scales = tile("wa_scales", [P, R], "u8")
-        wb_bf = tile("wb_bf", [P, PACK * R], "bf16")
+        wb_bf = [tile("wb_bf%d" % u, [P, 2 * R], "bf16") for u in range(2)]
         wb_codes = tile("wb_codes", [P, R], "u32")
         wb_scales = tile("wb_scales", [P, R], "u8")
         h_scales = tile("h_scales", [P, J], "u8")
@@ -122,8 +120,7 @@ def tile_list_htabg_glu_resP_kernel(
         def load_weight(raw, w):
             nc.sync.dma_start(raw[:], w.rearrange("(p i) r -> p i r", i=PACK))
 
-        def load_wd():
-            nc.sync.dma_start(wd_raw_codes[:].bitcast(I32), wd_words[0].bitcast(I32))
+        def load_wd_scales():
             for q in range(QUADRANTS):
                 nc.sync.dma_start(scale_rows(wd_raw_scales, q), wd_scales[0, 4 * q : 4 * q + 4, :].bitcast(I32))
 
@@ -168,14 +165,19 @@ def tile_list_htabg_glu_resP_kernel(
             nc.vector.tensor_copy(codes[:], tab_codes[:].indirect(tab_list[:, entries]))
             v_codes[first * CHUNK] = codes
 
-        def round_weight(copy, bf, raw, m0, m1):
-            src = raw[:].rearrange("p i (m t) -> p m i t", t=PACK)[:, m0:m1]
-            dst = bf[:].rearrange("p (t m i) -> p m i t", t=PACK, i=PACK)[:, m0:m1]
+        def round_weight(copy, bf, raw, u, m0, m1):
+            src = raw[:].rearrange("p i (m t) -> p m i t", t=PACK)[:, m0:m1, :, 2 * u : 2 * u + 2]
+            dst = bf[u][:].rearrange("p (t m i) -> p m i t", t=2, i=PACK)[:, m0:m1]
             copy(dst, src)
 
+        def quantise_weight(codes, scales, bf, u):
+            hands = slice(2 * u * P, (2 * u + 2) * P)
+            quantise(codes[:, hands], scales[:, hands], bf[u][:])
+
         def deal_wd_codes(copy):
+            wd_dealt["codes"] = tile("wd_codes", [P, 2 * N], "u8")
             copy(
-                wd_codes[:].bitcast(U16).rearrange("p (t m) -> p t m", t=PACK),
+                wd_dealt["codes"][:].bitcast(U16).rearrange("p (t m) -> p t m", t=PACK),
                 wd_raw_codes[:].bitcast(U16).rearrange("p (m t) -> p t m", t=PACK),
             )
 
@@ -214,9 +216,9 @@ def tile_list_htabg_glu_resP_kernel(
 
         def product(bank, codes, scales, fmt, moving_codes, moving_scales, rows=range(PACK)):
             width = codes.shape[1] // PACK
-            for k, t in enumerate(rows):
+            for t in rows:
                 nc.tensor.matmul_mx(
-                    bank[:, k, :],
+                    bank[:, t % bank.shape[1], :],
                     lhsT=codes[:, t * width : (t + 1) * width].bitcast(fmt),
                     lhsT_scale=scales[:, t * P : (t + 1) * P],
                     rhs=moving_codes.bitcast(FP8X4),
@@ -225,15 +227,18 @@ def tile_list_htabg_glu_resP_kernel(
                     stop=True,
                 )
 
+        def hand_order(b):
+            return (0, 1, 2, 3) if b == 0 else (2, 3, 0, 1)
+
         def make_ya(b, bank):
             c, at = divmod(b * BLOCK, CHUNK)
             ya_banks[b] = bank_tile("ya%d" % b, bank, (P, PACK, BLOCK))
-            product(ya_banks[b], wa_codes[:], wa_scales, FP8X4, x_codes[c][:, at : at + BLOCK], x_scales[c][:, at : at + BLOCK])
+            product(ya_banks[b], wa_codes[:], wa_scales, FP8X4, x_codes[c][:, at : at + BLOCK], x_scales[c][:, at : at + BLOCK], hand_order(b))
 
         def make_yb(b, bank):
             codes, at = within(v_codes, b * BLOCK)
             yb = bank_tile("yb%d" % b, bank, (P, PACK, BLOCK))
-            product(yb, wb_codes[:], wb_scales, FP8X4, codes[:, at : at + BLOCK], v_scales[:, b * BLOCK : (b + 1) * BLOCK])
+            product(yb, wb_codes[:], wb_scales, FP8X4, codes[:, at : at + BLOCK], v_scales[:, b * BLOCK : (b + 1) * BLOCK], hand_order(b))
             yb_banks[b] = yb[:].rearrange("p t n -> p n t")
 
         def new_group(group, name, first, width, kind, over=None, at=0, room=0):
@@ -265,7 +270,7 @@ def tile_list_htabg_glu_resP_kernel(
 
         def make_y(c, u, bank):
             y_banks[c, u] = bank_tile("y%d_%d" % (c, u), bank, (P, 2, CHUNK))
-            product(y_banks[c, u], wd_codes[:], wd_dealt["scales"], FP4X4, h_codes[c][:], h_scales[:, places(c)], range(2 * u, 2 * u + 2))
+            product(y_banks[c, u], wd_dealt["codes"][:], wd_dealt["scales"], FP4X4, h_codes[c][:], h_scales[:, places(c)], range(2 * u, 2 * u + 2))
 
         def add_res(c, u):
             rows = slice(2 * u, 2 * u + 2)
@@ -307,13 +312,15 @@ def tile_list_htabg_glu_resP_kernel(
         make_identity(nc, ident[:])
         nc.scalar.activation(warm[:], ident[:, 0:1], SILU)
         nc.sync.dma_start(head_lists[:], offs2)
-        for i in range(1, PACK):
-            load_x(i)
+        load_x(1)
+        load_x(2)
+        load_x(3)
         nc.vector.tensor_copy(v_staged[:], tab_staged[:].indirect(tab_list[:]))
         load_weight(wa_raw, wa)
         nc.sync.dma_start(tab_codes[:].bitcast(I32), tab_words[0].rearrange("p t i -> p (t i)").bitcast(I32))
         load_weight(wb_raw, wb)
-        load_wd()
+        nc.sync.dma_start(wd_raw_codes[:].bitcast(I32), wd_words[0].bitcast(I32))
+        load_wd_scales()
         carry_v_scales()
         spread_wgt()
 
@@ -336,10 +343,12 @@ def tile_list_htabg_glu_resP_kernel(
         load_res(2, 0, 4, "x_rows3", 0)
         load_res(3, 0, 4, "x_rows3", 4096)
         quantise_x(0)
-        round_weight(on_scalar, wa_bf, wa_raw, 0, WA_SCALAR)
-        round_weight(on_vector, wa_bf, wa_raw, WA_SCALAR, P)
+        round_weight(on_scalar, wa_bf, wa_raw, 1, 0, WA_SCALAR)
+        round_weight(on_vector, wa_bf, wa_raw, 0, 0, P)
+        round_weight(on_vector, wa_bf, wa_raw, 1, WA_SCALAR, P)
         quantise_x(1)
-        quantise(wa_codes[:], wa_scales[:], wa_bf[:])
+        quantise_weight(wa_codes, wa_scales, wa_bf, 0)
+        quantise_weight(wa_codes, wa_scales, wa_bf, 1)
         new_x_bf(3, "wa_raw", 0)
         round_x_gpsimd(3)
         new_x_bf(2, "wa_raw", 2048)
@@ -351,21 +360,23 @@ def tile_list_htabg_glu_resP_kernel(
         for b in (0, 1):
             make_ya(b, b)
             apply_silu(b)
+        new_group(gates, "gates", 256, BLOCK, "f32")
         make_ya(2, 2)
+        apply_silu(2)
         make_ya(3, 3)
         quantise_x(2)
         make_ya(5, 5)
         make_ya(4, 4)
-        round_weight(on_scalar, wb_bf, wb_raw, 0, WB_SCALAR)
-        round_weight(on_vector, wb_bf, wb_raw, WB_SCALAR, P)
-        deal_wd_codes(on_vector)
-        quantise(wb_codes[:], wb_scales[:], wb_bf[:])
-        quantise_x(3, "wd_raw_codes", 768)
-        gather_v(3, 1, "wd_room", 0)
+        round_weight(on_scalar, wb_bf, wb_raw, 1, 0, WB_SCALAR)
+        round_weight(on_vector, wb_bf, wb_raw, 0, 0, P)
+        round_weight(on_vector, wb_bf, wb_raw, 1, WB_SCALAR, P)
+        quantise_weight(wb_codes, wb_scales, wb_bf, 0)
+        quantise_weight(wb_codes, wb_scales, wb_bf, 1)
+        quantise_x(3, "wb_bf0", 1024)
+        gather_v(3, 1, "wb_bf0", 0)
         new_group(gates, "gates", 512, CHUNK, "f32", "wb_raw", 0)
-        new_group(gates, "gates", 256, BLOCK, "f32", "wb_raw", 4096)
         new_group(yb_copies, "yb_copy", 768 - FIRST_SHARE, FIRST_SHARE, "f32")
-        apply_silu(2)
+        deal_wd_codes(on_scalar)
         apply_silu(5)
         apply_silu(4)
         make_yb(0, 6)

@@ -32,7 +32,7 @@ CHUNKS = J // CHUNK
 HALF = J // 2
 LAST_SCALAR = 96
 LOW, HIGH = slice(0, 2), slice(2, 4)
-WA_SCALAR, WB_SCALAR = 88, 64
+WA_SCALAR, WB_SCALAR = 88, 88
 FIRST_SHARE, SECOND_SHARE = 192, 208
 
 
@@ -314,15 +314,16 @@ def tile_list_htabg_glu_resP_kernel(
         nc.sync.dma_start(head_lists[:], offs2)
         load_x(1)
         load_x(2)
+        nc.sync.dma_start(wd_raw_codes[:].bitcast(I32), wd_words[0].bitcast(I32))
         load_x(3)
         nc.vector.tensor_copy(v_staged[:], tab_staged[:].indirect(tab_list[:]))
         load_weight(wa_raw, wa)
         nc.sync.dma_start(tab_codes[:].bitcast(I32), tab_words[0].rearrange("p t i -> p (t i)").bitcast(I32))
         load_weight(wb_raw, wb)
-        nc.sync.dma_start(wd_raw_codes[:].bitcast(I32), wd_words[0].bitcast(I32))
         load_wd_scales()
         carry_v_scales()
         spread_wgt()
+        deal_wd_codes(on_scalar)
 
         gather_x(0, 0, CHUNK)
         gather_x(0, CHUNK, CHUNK)
@@ -360,9 +361,7 @@ def tile_list_htabg_glu_resP_kernel(
         for b in (0, 1):
             make_ya(b, b)
             apply_silu(b)
-        new_group(gates, "gates", 256, BLOCK, "f32")
         make_ya(2, 2)
-        apply_silu(2)
         make_ya(3, 3)
         quantise_x(2)
         make_ya(5, 5)
@@ -375,8 +374,9 @@ def tile_list_htabg_glu_resP_kernel(
         quantise_x(3, "wb_bf0", 1024)
         gather_v(3, 1, "wb_bf0", 0)
         new_group(gates, "gates", 512, CHUNK, "f32", "wb_raw", 0)
+        new_group(gates, "gates", 256, BLOCK, "f32", "wb_raw", 4096)
         new_group(yb_copies, "yb_copy", 768 - FIRST_SHARE, FIRST_SHARE, "f32")
-        deal_wd_codes(on_scalar)
+        apply_silu(2)
         apply_silu(5)
         apply_silu(4)
         make_yb(0, 6)

@@ -33,7 +33,7 @@ HALF = J // 2
 LAST_SCALAR = 96
 LOW, HIGH = slice(0, 2), slice(2, 4)
 WA_SCALAR, WB_SCALAR = 88, 88
-FIRST_SHARE, SECOND_SHARE = 192, 208
+FIRST_SHARE, SECOND_SHARE = 208, 208
 
 
 def tile_list_htabg_glu_resP_kernel(

from contextlib import ExitStack

import concourse.mybir as mybir
from concourse.masks import make_identity

K, L, R, N, T, J = 512, 512, 512, 512, 2048, 1024
HEADS = 8
FLOPS = 2 * J * (K * R + L * R + R * N)

F32 = mybir.dt.float32
BF16 = mybir.dt.bfloat16
I32 = mybir.dt.int32
U32 = mybir.dt.uint32
U16 = mybir.dt.uint16
U8 = mybir.dt.uint8
FP8X4 = mybir.dt.float8_e4m3fn_x4
FP4X4 = mybir.dt.float4_e2m1fn_x4
MULT = mybir.AluOpType.mult
ADD = mybir.AluOpType.add
SILU = mybir.ActivationFunctionType.Silu
KINDS = {"f32": (F32, 4), "bf16": (BF16, 2), "u32": (U32, 4), "u8": (U8, 1)}

P = 128
PACK = 4
QUADRANTS = 4
SCALE_ROWS = 16
LIST_ROWS = 16
BANK = 512
BLOCK = BANK // PACK
CHUNK = 2 * BLOCK
CHUNKS = J // CHUNK
HALF = J // 2
LAST_SCALAR = 96
LOW, HIGH = slice(0, 2), slice(2, 4)
WA_SCALAR, WB_SCALAR = 88, 88
FIRST_SHARE, SECOND_SHARE = 208, 208


def tile_list_htabg_glu_resP_kernel(
    tc, tab_words, tab_scales, xT, wgt2, wa, wb, wd_words, wd_scales, res, offs, offs2, out_0, out_1, out_2
):
    nc = tc.nc
    with ExitStack() as ctx:
        lists = ctx.enter_context(tc.tile_pool(name="lists", bufs=1))
        sb = ctx.enter_context(tc.tile_pool(name="sb", bufs=1))
        ps = ctx.enter_context(tc.psum_pool(name="ps", bufs=1))
        spans = {"end": (0, 0)}

        def tile(name, shape, kind, over=None, at=0, room=0):
            dtype, size = KINDS[kind]
            for extent in shape[1:]:
                size = size * extent
            if over is None:
                start = spans["end"][0]
                spans["end"] = (start + (max(size, room) + 63) // 64 * 64, 0)
            else:
                start = spans[over][0] + at
                assert at + size <= spans[over][1]
            spans[name] = (start, max(size, room))
            return sb.tile(shape, dtype, name=name, align_bytes=64, offset=start)

        def tile_room(name, lead, size):
            spans[name] = (spans["end"][0], size)
            spans["end"] = (spans["end"][0] + lead, 0)

        def bank_tile(name, bank, shape):
            return ps.tile(list(shape), F32, name=name, offset=bank * BANK * 4)

        def scale_rows(scale_tile, q):
            return scale_tile[32 * q : 32 * q + 4, :].bitcast(I32)

        def places(c):
            return slice(c * CHUNK, (c + 1) * CHUNK)

        tab_list = lists.tile([P, J // LIST_ROWS], U16, name="tab_list")
        head_lists = lists.tile([P, J // LIST_ROWS], U16, name="head_lists")
        staged = P - SCALE_ROWS
        tab_staged = tile("tab_staged", [P, T], "u8")
        v_staged = tile("v_staged", [P, J], "u8")
        v_scales = tile("v_scales", [P, J], "u8")
        x_rows = [tile("x_rows%d" % i, [P, T], "f32") for i in range(PACK)]
        wgt = tile("wgt", [P, J], "f32")
        wgt_rows = tile("wgt_rows", [P, P], "f32")
        ident = tile("ident", [P, P], "f32")
        warm = tile("warm", [P, 1], "f32")
        tab_codes = tile("tab_codes", [P, T], "u32")
        wa_raw = tile("wa_raw", [P, PACK, R], "f32")
        wb_raw = tile("wb_raw", [P, PACK, R], "f32", room=9216)
        wd_raw_codes = tile("wd_raw_codes", [P, 2 * N], "u8")
        wd_raw_scales = tile("wd_raw_scales", [P, N], "u8")
        picked = tile("picked", [P, PACK, J], "f32")
        wa_bf = [tile("wa_bf%d" % u, [P, 2 * R], "bf16") for u in range(2)]
        wa_codes = tile("wa_codes", [P, R], "u32")
        wa_scales = tile("wa_scales", [P, R], "u8")
        wb_bf = [tile("wb_bf%d" % u, [P, 2 * R], "bf16") for u in range(2)]
        wb_codes = tile("wb_codes", [P, R], "u32")
        wb_scales = tile("wb_scales", [P, R], "u8")
        h_scales = tile("h_scales", [P, J], "u8")
        sums = [tile("sums%d" % c, [P, PACK, CHUNK], "f32") for c in range(CHUNKS)]
        out_bf = tile("out_bf", [P, PACK * J], "bf16")
        out_scales = tile("out_scales", [P, HALF], "u8")
        x_bf, x_codes, x_scales, v_codes, gates, ya_banks, yb_banks = {}, {}, {}, {}, {}, {}, {}
        wd_dealt = {}
        yb_copies, h_bf, h_codes, y_banks, res_rows, out_codes = {}, {}, {}, {}, {}, {}

        x_hbm = xT.rearrange("(p i) t -> p i t", i=PACK)
        res_hbm = res.rearrange("(p t) j -> p t j", t=PACK)
        out_hbm = out_0.rearrange("(p t) j -> p t j", t=PACK)
        out_words_hbm = out_1[0].rearrange("p j i -> p (j i)").bitcast(I32)
        on_scalar, on_vector = nc.scalar.copy, nc.vector.tensor_copy
        blocks = J // P

        def within(tiles, j0):
            first = max(k for k in tiles if k <= j0)
            return tiles[first], j0 - first

        def load_x(i):
            nc.sync.dma_start(x_rows[i][:], x_hbm[:, i, :])

        def load_weight(raw, w):
            nc.sync.dma_start(raw[:], w.rearrange("(p i) r -> p i r", i=PACK))

        def load_wd_scales():
            for q in range(QUADRANTS):
                nc.sync.dma_start(scale_rows(wd_raw_scales, q), wd_scales[0, 4 * q : 4 * q + 4, :].bitcast(I32))

        def carry_v_scales():
            for q in range(QUADRANTS):
                nc.sync.dma_start(scale_rows(v_scales, q), v_staged[staged + 4 * q : staged + 4 * q + 4, :].bitcast(I32))

        def load_res(c, row, rows, over, at):
            res_rows[c, row] = tile("res%d_%d" % (c, row), [P, rows, CHUNK], "f32", over, at)
            nc.sync.dma_start(res_rows[c, row][:], res_hbm[:, row : row + rows, places(c)])

        def res_pair(c, u):
            row = max(r for k, r in res_rows if k == c and r <= 2 * u)
            return res_rows[c, row][:, 2 * u - row : 2 * u - row + 2, :]

        def spread_wgt():
            turned = bank_tile("wgt_turned", 0, [P, P])
            nc.tensor.transpose(turned[:], wgt_rows[:], ident[:])
            by_block = turned[:, 32 : 32 + HEADS * blocks].rearrange("p (g b) -> p b g", b=blocks)
            shape = [P, CHUNK // P, HEADS, LIST_ROWS]
            banks = []
            for c in range(CHUNKS):
                repeated = tile("repeated%d" % c, shape, "f32")
                nc.scalar.copy(repeated[:], by_block[:, 2 * c : 2 * c + 2, :].unsqueeze(3).to_broadcast(shape))
                banks.append(bank_tile("wgt_bank%d" % c, 1 + c, [P, CHUNK // P, P]))
                for b in range(CHUNK // P):
                    nc.tensor.transpose(banks[c][:, b, :], repeated[:, b].rearrange("p g q -> p (g q)"), ident[:])
            for c in range(CHUNKS):
                nc.scalar.copy(wgt[:, places(c)], banks[c][:].rearrange("p b j -> p (b j)"))

        def gather_x(i, j0, width):
            nc.vector.tensor_tensor(
                picked[:, i, j0 : j0 + width],
                x_rows[i][:].indirect(head_lists[:, j0 // LIST_ROWS : (j0 + width) // LIST_ROWS]),
                wgt[:, j0 : j0 + width],
                MULT,
            )

        def gather_v(first, chunks, over, at):
            codes = tile("v_codes%d" % first, [P, chunks * CHUNK], "u32", over, at)
            entries = slice(first * CHUNK // LIST_ROWS, (first + chunks) * CHUNK // LIST_ROWS)
            nc.vector.tensor_copy(codes[:], tab_codes[:].indirect(tab_list[:, entries]))
            v_codes[first * CHUNK] = codes

        def round_weight(copy, bf, raw, u, m0, m1):
            src = raw[:].rearrange("p i (m t) -> p m i t", t=PACK)[:, m0:m1, :, 2 * u : 2 * u + 2]
            dst = bf[u][:].rearrange("p (t m i) -> p m i t", t=2, i=PACK)[:, m0:m1]
            copy(dst, src)

        def quantise_weight(codes, scales, bf, u):
            hands = slice(2 * u * P, (2 * u + 2) * P)
            quantise(codes[:, hands], scales[:, hands], bf[u][:])

        def deal_wd_codes(copy):
            wd_dealt["codes"] = tile("wd_codes", [P, 2 * N], "u8")
            copy(
                wd_dealt["codes"][:].bitcast(U16).rearrange("p (t m) -> p t m", t=PACK),
                wd_raw_codes[:].bitcast(U16).rearrange("p (m t) -> p t m", t=PACK),
            )

        def deal_wd_scales(copy, over):
            wd_dealt["scales"] = tile("wd_dealt_scales", [P, N], "u8", over)
            copy(
                wd_dealt["scales"][:].rearrange("p (t m) -> p t m", t=PACK),
                wd_raw_scales[:].rearrange("p (m t) -> p t m", t=PACK),
            )

        def quantise(codes, scales, src):
            nc.vector.quantize_mx(codes.bitcast(FP8X4), scales, src)

        def round_into_words(copy, dst, src, rows=slice(0, PACK)):
            copy(
                dst.rearrange("p (c e i) -> p c i e", e=4, i=PACK)[:, :, rows, :],
                src.rearrange("p i (c e) -> p c i e", e=4)[:, :, rows, :],
            )

        def new_x_bf(c, over=None, at=0):
            x_bf[c] = tile("x_bf%d" % c, [P, PACK * CHUNK], "bf16", over, at)

        def round_x(c, first=0, width=CHUNK):
            j0 = c * CHUNK + first
            round_into_words(on_scalar, x_bf[c][:, PACK * first : PACK * (first + width)], picked[:, :, j0 : j0 + width])

        def round_x_gpsimd(c):
            nc.gpsimd.tensor_scalar(
                x_bf[c][:].rearrange("p (j i) -> p j i", i=PACK), picked[:, :, places(c)].rearrange("p i j -> p j i"), 1.0, 0.0, MULT, ADD
            )

        def quantise_x(c, over=None, at=0):
            x_codes[c] = tile("x_codes%d" % c, [P, CHUNK], "u32")
            x_scales[c] = tile("x_scales%d" % c, [P, CHUNK], "u8", over, at)
            quantise(x_codes[c][:], x_scales[c][:], x_bf[c][:])

        def product(bank, codes, scales, fmt, moving_codes, moving_scales, rows=range(PACK)):
            width = codes.shape[1] // PACK
            for t in rows:
                nc.tensor.matmul_mx(
                    bank[:, t % bank.shape[1], :],
                    lhsT=codes[:, t * width : (t + 1) * width].bitcast(fmt),
                    lhsT_scale=scales[:, t * P : (t + 1) * P],
                    rhs=moving_codes.bitcast(FP8X4),
                    rhs_scale=moving_scales,
                    start=True,
                    stop=True,
                )

        def hand_order(b):
            return (0, 1, 2, 3) if b == 0 else (2, 3, 0, 1)

        def make_ya(b, bank):
            c, at = divmod(b * BLOCK, CHUNK)
            ya_banks[b] = bank_tile("ya%d" % b, bank, (P, PACK, BLOCK))
            product(ya_banks[b], wa_codes[:], wa_scales, FP8X4, x_codes[c][:, at : at + BLOCK], x_scales[c][:, at : at + BLOCK], hand_order(b))

        def make_yb(b, bank):
            codes, at = within(v_codes, b * BLOCK)
            yb = bank_tile("yb%d" % b, bank, (P, PACK, BLOCK))
            product(yb, wb_codes[:], wb_scales, FP8X4, codes[:, at : at + BLOCK], v_scales[:, b * BLOCK : (b + 1) * BLOCK], hand_order(b))
            yb_banks[b] = yb[:].rearrange("p t n -> p n t")

        def new_group(group, name, first, width, kind, over=None, at=0, room=0):
            group[first] = tile("%s%d" % (name, first), [P, width, PACK], kind, over, at, room)

        def part(group, j0, width):
            whole, at = within(group, j0)
            return whole[:, at : at + width, :]

        def yb_part(j0, width):
            b, at = divmod(j0, BLOCK)
            return yb_banks[b][:, at : at + width, :]

        def apply_silu(b):
            nc.scalar.activation(part(gates, b * BLOCK, BLOCK), ya_banks[b][:].rearrange("p t n -> p n t"), SILU)

        def copy_yb(j0, width=BLOCK):
            nc.scalar.copy(part(yb_copies, j0, width), yb_part(j0, width))

        def make_h(j0, width=BLOCK):
            nc.vector.tensor_tensor(part(h_bf, j0, width), part(gates, j0, width), yb_part(j0, width), MULT)

        def make_h_gpsimd(j0, width):
            nc.gpsimd.tensor_tensor(part(h_bf, j0, width), part(gates, j0, width), part(yb_copies, j0, width), MULT)

        def quantise_h(c, over=None, at=0, room=0):
            h_codes[c] = tile("h_codes%d" % c, [P, CHUNK], "u32", over, at, room)
            quantise(h_codes[c][:], h_scales[:, places(c)], part(h_bf, c * CHUNK, CHUNK).rearrange("p n t -> p (n t)"))

        def make_y(c, u, bank):
            y_banks[c, u] = bank_tile("y%d_%d" % (c, u), bank, (P, 2, CHUNK))
            product(y_banks[c, u], wd_dealt["codes"][:], wd_dealt["scales"], FP4X4, h_codes[c][:], h_scales[:, places(c)], range(2 * u, 2 * u + 2))

        def add_res(c, u):
            rows = slice(2 * u, 2 * u + 2)
            nc.vector.tensor_tensor(sums[c][:, rows, :], y_banks[c, u][:], res_pair(c, u), ADD)
            nc.sync.dma_start(out_hbm[:, rows, places(c)], sums[c][:, rows, :])

        def round_out(b, copy, first=0, width=BLOCK):
            c, at = divmod(b * BLOCK + first, CHUNK)
            j0 = b * BLOCK + first
            round_into_words(copy, out_bf[:, PACK * j0 : PACK * (j0 + width)], sums[c][:, :, at : at + width])

        def new_out_codes(j0, width, over=None, at=0):
            out_codes[j0] = tile("out_codes%d" % j0, [P, width], "u32", over, at)

        def quantise_out(j0, width):
            codes, at = within(out_codes, j0)
            half, column = divmod(j0, HALF)
            quantise(codes[:, at : at + width], out_scales[4 * half :, column : column + width], out_bf[:, PACK * j0 : PACK * (j0 + width)])

        def store_words(queue, first):
            codes = out_codes[first]
            queue.dma_start(out_words_hbm[:, first : first + codes.shape[1]], codes[:].bitcast(I32))

        def store_scales():
            for q in range(QUADRANTS):
                queue = nc.sync if q < QUADRANTS // 2 else nc.scalar
                rows = out_2[0, 4 * q : 4 * q + 4, :].bitcast(I32).rearrange("r (half w) -> half r w", half=2)
                queue.dma_start(rows, out_scales[32 * q : 32 * q + 8, :].bitcast(I32))

        nc.sync.dma_start(tab_list[:], offs)
        nc.sync.dma_start(tab_staged[staged:, :].bitcast(I32), tab_scales[0].bitcast(I32))
        nc.scalar.dma_start(wgt_rows[32 : 32 + HEADS * blocks, :], wgt2.rearrange("(g q) (b j) -> q g b j", q=LIST_ROWS, j=P)[0])
        load_x(0)
        nc.vector.memset(wd_raw_scales[:].bitcast(I32), 0)
        nc.vector.memset(wgt_rows[:32, :], 0.0)
        nc.vector.memset(wgt_rows[32 + HEADS * blocks :, :], 0.0)
        nc.vector.memset(tab_staged[:staged, :].bitcast(I32), 0)
        nc.vector.memset(v_scales[:].bitcast(I32), 0)
        make_identity(nc, ident[:])
        nc.scalar.activation(warm[:], ident[:, 0:1], SILU)
        nc.sync.dma_start(head_lists[:], offs2)
        load_x(1)
        load_x(2)
        nc.sync.dma_start(wd_raw_codes[:].bitcast(I32), wd_words[0].bitcast(I32))
        load_x(3)
        nc.vector.tensor_copy(v_staged[:], tab_staged[:].indirect(tab_list[:]))
        load_weight(wa_raw, wa)
        nc.sync.dma_start(tab_codes[:].bitcast(I32), tab_words[0].rearrange("p t i -> p (t i)").bitcast(I32))
        load_weight(wb_raw, wb)
        load_wd_scales()
        carry_v_scales()
        spread_wgt()
        deal_wd_codes(on_scalar)

        gather_x(0, 0, CHUNK)
        gather_x(0, CHUNK, CHUNK)
        gather_x(0, HALF, HALF)
        gather_x(1, 0, J)
        gather_x(2, 0, J)
        load_res(0, 0, 2, "x_rows2", 0)
        load_res(0, 2, 2, "x_rows2", 2048)
        load_res(1, 0, 4, "x_rows2", 4096)
        new_x_bf(0)
        for first in (0, BLOCK):
            gather_x(3, first, BLOCK)
            round_x(0, first, BLOCK)
        gather_x(3, CHUNK, CHUNK)
        new_x_bf(1)
        round_x(1)
        gather_x(3, HALF, HALF)
        load_res(2, 0, 4, "x_rows3", 0)
        load_res(3, 0, 4, "x_rows3", 4096)
        quantise_x(0)
        round_weight(on_scalar, wa_bf, wa_raw, 1, 0, WA_SCALAR)
        round_weight(on_vector, wa_bf, wa_raw, 0, 0, P)
        round_weight(on_vector, wa_bf, wa_raw, 1, WA_SCALAR, P)
        quantise_x(1)
        quantise_weight(wa_codes, wa_scales, wa_bf, 0)
        quantise_weight(wa_codes, wa_scales, wa_bf, 1)
        new_x_bf(3, "wa_raw", 0)
        round_x_gpsimd(3)
        new_x_bf(2, "wa_raw", 2048)
        round_x(2)
        gather_v(0, 3, "wa_raw", 4096)
        new_group(gates, "gates", 0, BLOCK, "f32")
        tile_room("behind_h1", 1536, 5120)
        new_group(gates, "gates", 128, BLOCK, "f32", room=3584)
        for b in (0, 1):
            make_ya(b, b)
            apply_silu(b)
        make_ya(2, 2)
        make_ya(3, 3)
        quantise_x(2)
        make_ya(5, 5)
        make_ya(4, 4)
        round_weight(on_scalar, wb_bf, wb_raw, 1, 0, WB_SCALAR)
        round_weight(on_vector, wb_bf, wb_raw, 0, 0, P)
        round_weight(on_vector, wb_bf, wb_raw, 1, WB_SCALAR, P)
        quantise_weight(wb_codes, wb_scales, wb_bf, 0)
        quantise_weight(wb_codes, wb_scales, wb_bf, 1)
        quantise_x(3, "wb_bf0", 1024)
        gather_v(3, 1, "wb_bf0", 0)
        new_group(gates, "gates", 512, CHUNK, "f32", "wb_raw", 0)
        new_group(gates, "gates", 256, BLOCK, "f32", "wb_raw", 4096)
        new_group(yb_copies, "yb_copy", 768 - FIRST_SHARE, FIRST_SHARE, "f32")
        apply_silu(2)
        apply_silu(5)
        apply_silu(4)
        make_yb(0, 6)
        make_yb(5, 7)
        make_yb(1, 0)
        make_yb(4, 1)
        make_yb(2, 5)
        make_yb(3, 2)
        copy_yb(640)
        copy_yb(768 - FIRST_SHARE, FIRST_SHARE - BLOCK)
        new_group(h_bf, "h_bf", 0, CHUNK, "bf16")
        new_group(h_bf, "h_bf", 256, CHUNK, "bf16")
        make_h(0)
        make_yb(7, 4)
        make_ya(7, 6)
        make_h(128)
        make_ya(6, 0)
        new_group(gates, "gates", 384, BLOCK, "f32", "behind_h1")
        apply_silu(3)
        deal_wd_scales(on_vector, "gates0")
        tile_room("codes", 3072, 3072)
        quantise_h(0, "codes", 512)
        new_group(h_bf, "h_bf", 512, CHUNK, "bf16", "behind_h1", 3072)
        make_h_gpsimd(768 - FIRST_SHARE, FIRST_SHARE)
        new_group(gates, "gates", 768, CHUNK, "f32")
        apply_silu(7)
        apply_silu(6)
        make_y(0, 0, 7)
        make_yb(6, 3)
        new_group(yb_copies, "yb_copy", J - SECOND_SHARE, SECOND_SHARE, "f32")
        copy_yb(896)
        copy_yb(J - SECOND_SHARE, SECOND_SHARE - BLOCK)
        make_h(256)
        make_y(0, 1, 5)
        make_h(512, CHUNK - FIRST_SHARE)
        make_h(384)
        add_res(0, 0)
        quantise_h(1, "codes")
        quantise_h(2, "codes", 1024)
        new_group(h_bf, "h_bf", 768, CHUNK, "bf16", "h_bf256")
        make_h_gpsimd(J - SECOND_SHARE, SECOND_SHARE)
        make_y(1, 0, 1)
        make_y(1, 1, 6)
        make_y(2, 0, 2)
        make_y(2, 1, 0)
        add_res(0, 1)
        round_out(0, on_scalar)
        round_out(1, on_scalar)
        make_h(768, CHUNK - SECOND_SHARE)
        add_res(1, 0)
        add_res(1, 1)
        round_out(2, on_scalar)
        round_out(3, on_scalar)
        add_res(2, 0)
        quantise_h(3, "codes", 1024)
        make_y(3, 0, 7)
        make_y(3, 1, 4)
        add_res(2, 1)
        round_out(4, on_scalar)
        round_out(5, on_scalar)
        new_out_codes(0, HALF, "h_bf768")
        quantise_out(0, CHUNK)
        add_res(3, 0)
        add_res(3, 1)
        round_out(6, on_scalar, 0, LAST_SCALAR)
        quantise_out(256, CHUNK)
        store_words(nc.sync, 0)
        new_out_codes(HALF, HALF, "codes", 1024)
        round_out(6, on_vector, LAST_SCALAR, CHUNK - LAST_SCALAR)
        quantise_out(512, CHUNK)
        quantise_out(896, BLOCK)
        quantise_out(768, BLOCK)
        store_words(nc.scalar, HALF)
        store_scales()
